import numpy as np, ml_dtypes
CORES = [10,34,74,98]
N = 4
BF = ml_dtypes.bfloat16
def gentries(a):
    return np.ascontiguousarray(a.reshape(8, 16, -1).transpose(0, 2, 1)).reshape(8, -1)
def gtable(e):
    e = np.asarray(e); return np.ascontiguousarray(e.reshape(8, -1, 16).transpose(0, 2, 1)).reshape(128, -1).astype(np.int32)
W, WC, FR, X, H, V, FO = 4096, 4096, 4, 1024, 2, 7, 2
def loud(rng, lo, hi):
    v = 0.25 + 0.75 * rng.random((N, 8, 16, W), dtype=np.float32)
    return v * np.exp2(rng.integers(lo, hi + 1, (N, 8, 1, W)))
def perms(rng):
    return np.argsort(rng.random((N, 8, FR, W)), axis=-1)
def recs(rng):
    return 0.75 + 0.5 * rng.random((N, 8, 16, WC))
def turns(rng):
    return rng.integers(0, WC, (N, 8, W)), rng.integers(0, 4096, (N, 8, FR))
def put(a, m, v):
    i = int(np.argmax(a == v)); a[i] = a[m]; a[m] = v
def saw():
    n = np.arange(W)[None, :]; top = (16 - np.arange(16)[:, None]) % 16
    return 1.0 - np.where(n < top, top - n, (n - top) % 16) * 0.03125
def spikes(rng):
    v = 0.3125 + 0.5 * rng.random((N, 8, 16, W))
    n = rng.choice(np.array([0, 1, V - 1, V - 1, V, V, V + 1, 15, 16]), (N, 8, 1, W // 8))
    a = np.argsort(rng.random((N, 8, 16, W // 8)), axis=2) < n; k = rng.integers(0, 4, a.shape); miss = ~a & (k == 3)
    v[..., ::8] = np.where(a | miss, 1.0, 0.25)
    v[..., H::8] = np.where(miss, 1.0078125, np.where(a & (k == 1), 1.0, v[..., H::8]))
    v[..., H + 1::8] = np.where(a & (k == 2), 1.0078125, v[..., H + 1::8])
    return v
RATES = np.concatenate([np.arange(192, 256), np.arange(256, 321, 2)])
def near(k):
    s = np.concatenate([np.arange(128, 256), np.arange(256, 512, 2), np.arange(512, 1024, 4)]).astype(np.int64)
    a = np.tile(np.arange(RATES.size), s.size); s = np.repeat(s, RATES.size)
    x = s * RATES[a].astype(np.int64) ** k; b = x.astype(np.float32).view(np.int32)
    o = np.argsort(x, kind="stable"); i, j = o[:-1], o[1:]
    low = (b[i] != b[j]) & ((b[i] >> 2) == (b[j] >> 2)); tie = (x[i] != x[j]) & (b[i] == b[j])
    return s, a, [np.stack([i[w], j[w]], axis=1) for w in (low, tie) if np.any(w)]
def plant(rng, found, S, C, P, R, q, g):
    s, a, L = found; h = (W - (FR - 1) * X) // 8; n = 8 * np.arange(h)
    v = (1.0 + 0.5 * rng.random((16, 8 * h))) * 0.0625
    e = np.stack([L[int(w)][int(rng.integers(0, len(L[int(w)])))] for w in rng.integers(0, len(L), h)])
    e = np.where(rng.random((h, 1)) < 0.5, e, e[:, ::-1])
    on = np.argsort(rng.random((16, h)), axis=0) < rng.choice(np.array([V, V, 16]), h)
    for i in range(2):
        v[:, n + 3 + i] = np.where(on, s[e[:, i]] * 2.0 ** -8, v[:, n + 3 + i]); R[q, g, n + 3 + i] = a[e[:, i]]
    S[q, g, :, :8 * h] = v; C[q, g, :, :RATES.size] = RATES * 0.00390625; P[q, g, :FR - 1] = np.arange(W)
def pack(S, C, P, R, hp):
    return {"sp": np.ascontiguousarray(S.reshape(N, 128, W)).astype(BF), "rec": np.ascontiguousarray(C.reshape(N, 128, WC)).astype(BF), "itg": np.stack([gtable(a.reshape(8, FR * W)) for a in P]),
            "rot": np.ascontiguousarray(R).astype(np.int32), "hop": np.ascontiguousarray(hp).astype(np.int32)}
def setup_inputs(rng):
    S = loud(rng, -1, 1); C = recs(rng); P = perms(rng); R, hp = turns(rng)
    return pack(S, C, P, R, hp)
def setup_inputs_spread(rng):
    S = loud(rng, 0, 0) * rng.choice(np.array([0.5, 2.0]), (N, 8, 1, W)); C = recs(rng); P = perms(rng)
    R = np.exp2(np.log2(WC) * rng.random((N, 8, W))).astype(np.int64) - 1; R = np.where(rng.random(R.shape) < 0.5, R, WC - 1 - R)
    hp = np.exp2(12 * rng.random((N, 8, FR))).astype(np.int64) - 1
    found = near(FR - 1)
    for q in range(N):
        for g in range(8):
            if (q + g) % 4 == 1: plant(rng, found, S, C, P, R, q, g)
    return pack(S, C, P, np.clip(R, 0, WC - 1), np.clip(hp, 0, 4095))
def setup_inputs_ends(rng):
    share = rng.choice(np.array([0.0, 0.75, 1.0, 1.0]), (N, 8, 1, W)); share[..., 0] = 1.0; share[..., W - 1] = 1.0
    S = np.where(rng.random((N, 8, 16, W)) < share, 4.0, 0.0625)
    C = np.where(rng.random((N, 8, 16, WC)) < 0.5, 0.75, 1.25); C[..., 0] = 0.75; C[..., WC - 1] = 1.25
    P = perms(rng); R = rng.integers(0, 2, (N, 8, W)) * (WC - 1); hp = rng.integers(0, 2, (N, 8, FR)) * 4095
    hp[:, 1, 0] = 0; hp[:, 2, 0] = 4095
    for q in range(N):
        for g in range(8):
            k = (q + g) % 4
            if (q, g) in ((0, 0), (N - 1, 7)): k = 0; hp[q, g, 0] = 4095; R[q, g, 0] = WC - 1; R[q, g, W - 1] = 0
            if k == 0: P[q, g] = np.arange(W)[::-1]
            elif k == 2: P[q, g, ::2] = np.arange(W)
            else:
                for t in range(FR): put(P[q, g, t], 0, W - 1); put(P[q, g, t], W - 1, 0)
    return pack(S, C, P, R, hp)
def setup_inputs_corners(rng):
    S = loud(rng, -1, 1); C = recs(rng); P = perms(rng); R, hp = turns(rng); sk = spikes(rng); teeth = saw()
    for q in range(N):
        for g in range(8):
            k = (q + g) % 8
            if k == 0: S[q, g] = 0.75
            elif k == 1:
                S[q, g] = teeth; C[q, g] = 1.0
                for t in range(FR): put(P[q, g, t], (W - 1, 0, W // 2, W - 1)[q % 4], 0)
            elif k == 2: S[q, g] = sk[q, g]; P[q, g] = np.arange(W)
            elif k == 3: S[q, g] = sk[q, g]; P[q, g] = np.arange(W)[::-1]
            elif k == 4: S[q, g] = np.where(np.repeat(rng.random(W // 64) < 0.6, 64), S[q, g], 0.0625)
            elif k == 5: P[q, g] = (np.arange(W) + 1) % W
            elif k == 6:
                v = teeth.copy(); v[:, W - 1] = 1.5; S[q, g] = v
                for t in range(FR): put(P[q, g, t], 100, W - 1); put(P[q, g, t], 300, 0)
            else: R[q, g] = rng.integers(0, 2, W) * (WC - 1); hp[q, g] = rng.integers(0, 2, FR) * 4095
    for q, place in ((1, 0), (3, W - 1)):
        for a, g in ((q - 1, 5), (q - 1, 6), (q - 1, 7), (q, 7)):
            S[a, g] = teeth; P[a, g] = perms(rng)[a, g]; P[a, g, :FR - 1] = np.arange(W); R[a, g] = rng.integers(0, 4, W)
            C[a, g] = 0.75 + 0.5 * rng.random((16, WC)); C[a, g, :, :4] = 1.0
        put(P[q, 7, FR - 1], place, 0); hp[q, 7, FR - 1] = 4095
    return pack(S, C, P, R, hp)
def setup_inputs_crowd(rng):
    S = np.zeros((N, 8, 16, W)); C = recs(rng); P = perms(rng); R, hp = turns(rng); teeth = saw(); flat = (16, 15, V + 1, V, V - 1, V - 2, 1, 0)
    for q in range(N):
        for g in range(8):
            v = teeth.copy(); v[rng.permutation(16)[:flat[(q + g) % 8]]] = 0.75; S[q, g] = v * 0.125
    C[::2] = 0.75 + 0.0078125 * rng.integers(0, 65, C[::2].shape[:3] + (1,))
    return pack(S, C, P, R, hp)
def setup_inputs_calm(rng):
    S = spikes(rng) * 0.25; C = recs(rng); C[::2] = 1.0; R, hp = turns(rng); hp[:] = 0
    few = rng.choice(np.array([0, 1, 2, 3, 8, W - 1, W - 8]), (N, 8, FR, 1)); P = (np.arange(W) + few) % W
    R = np.where(np.arange(8)[None, :, None] % 2 == 0, rng.integers(0, 4, R.shape), rng.integers(WC - 2, WC, R.shape))
    C[1::2, :, :, [0, 1, 2, 3, WC - 2, WC - 1]] = np.array([0.75, 0.875, 1.0, 1.125, 1.25, 0.8125])
    return pack(S, C, P, R, hp)
def check_ranges(d):
    bad = []
    for k, lo, hi in (("itg", 0, W - 1), ("rot", 0, WC - 1), ("hop", 0, 4095)):
        if np.min(d[k]) < lo or np.max(d[k]) > hi: bad.append("range of " + k)
    p = np.sort(np.stack([gentries(a) for a in d["itg"]]).reshape(N, 8, FR, W), axis=-1)
    if not np.all(p == np.arange(W)): bad.append("itg: no permutation")
    s = np.asarray(d["sp"]).astype(np.float64); c = np.asarray(d["rec"]).astype(np.float64)
    if not np.all((s >= 0.0625) & (s <= 4)): bad.append("range of sp")
    if not np.all((c >= 0.75) & (c <= 1.25)): bad.append("range of rec")
    return bad
def reference(sp, rec, itg, rot, hop):
    S = sp.astype(np.float32).reshape(N, 8, 16, W); C = rec.astype(np.float32).reshape(N, 8, 16, WC); R = rot.astype(np.int64); hp = hop.astype(np.int64)
    P = np.stack([gentries(a) for a in itg]).astype(np.int64).reshape(N, 8, FR, W); m = np.arange(W)
    for t in range(FR):
        vote = np.ones(S.shape, bool)
        for d in range(1, H + 1):
            vote[..., d:] &= S[..., d:] >= S[..., :-d]; vote[..., :-d] &= S[..., :-d] >= S[..., d:]
        peak = np.add.reduce(vote, axis=2, dtype=np.int64) >= V; peak[..., 0] = True
        it = P[:, :, t]; moved = np.take_along_axis(peak, it, 2)
        left = np.maximum.accumulate(np.where(moved, m, -2 * W), axis=-1)
        right = np.minimum.accumulate(np.where(moved, m, 3 * W)[..., ::-1], axis=-1)[..., ::-1]
        q = np.where(m - left <= right - m, left, right); p = np.take_along_axis(it, q, 2)
        src = np.clip(p + m - q, 0, W - 1)
        T = np.take_along_axis(S, src[:, :, None, :], 3)
        Q = (np.take_along_axis(R, src, 2) + hp[:, :, t, None] * (q - p)) & (WC - 1)
        T = np.concatenate([np.roll(T[..., W - X:], (1, t), axis=(0, 1)), T[..., :W - X]], axis=-1)
        R = np.concatenate([np.roll(Q[..., W - X:], (1, t), axis=(0, 1)), Q[..., :W - X]], axis=-1)
        S = T * np.take_along_axis(C, R[:, :, None, :], 3)
    y = np.add.reduce(S.astype(np.float64).reshape(N, 128, FO, W // FO), axis=2)
    return {"y": y.astype(np.float32)}

def check_inputs(d):
    bad = list(check_ranges(d))
    if not bad:
        for name, y in reference(**d).items():
            for q in range(N):
                v = np.abs(np.asarray(y[q], np.float64)); s = np.sqrt(np.mean(v * v))
                if v.max() > 7 * s or s < 2.0 ** -3: bad.append('%s of rank %d is uneven or too small' % (name, q))
    return bad

@@ -1,0 +1,651 @@
+from concourse.bass import DstId, RemoteDMATransfer
+from concourse.mybir import AluOpType as A, ActivationFunctionType as F, AxisListType as AX
+
+W = 4096
+X = 1024
+FR = 4
+PF, PB = 8, 16
+XW = X + X // 16
+PARTS = [(512, X, 1), (0, 512, 0), (X, XW, 0)]
+BIG = float(2 ** 27)
+NONE = float(2 ** 26)
+
+CFG = {
+    "cuts0": [0, 512, 1408, 2304, 3200, W], "route0": "wGGww",
+    "route": "FFWVVV", "hfirst": 0,
+    "rq": "vaaaa", "tq": "avaaa", "dc": [256, 128, 0], "dcl": [256, 192, 0],
+    "rc": [3072, 2304, 1536, 768, 0], "yc": [W, 3328, 2560, 1792, X, 512, 0],
+    "lr": "vvav", "lt": "aaaa", "lc": [X, 512, 256, 0], "eps": 0.15, "short": 0.2,
+    "xs": [("v", 0, 4), ("a", 8, 12), ("v", 4, 6), ("a", 12, 14), ("v", 6, 7), ("a", 14, 15), ("v", 7, 8), ("a", 15, 16)],
+}
+
+SCRATCH = {
+    "s0": ("sbuf", [128, W + 2 * PB], "bfloat16"),
+    "sa": ("sbuf", [128, W + 2 * PF], "float32"),
+    "sb": ("sbuf", [128, W + 2 * PF], "float32"),
+    "bb": ("sbuf", [128, W], "float32"),
+    "bh": ("sbuf", [128, W], "bfloat16"),
+    "cw": ("sbuf", [128, (FR + 1) * W], "bfloat16"),
+    "tb": ("sbuf", [128, W - X], "float32"),
+    "xo": ("sbuf", [128, XW], "float32"),
+    "vt": ("sbuf", [128, W], "bfloat16"),
+    "gv": ("sbuf", [128, W], "bfloat16"),
+    "rw": ("sbuf", [128, W], "bfloat16"),
+    "rg": ("sbuf", [128, W], "bfloat16"),
+    "a0": ("sbuf", [128, 1024], "float32"),
+    "a1": ("sbuf", [128, 1024], "float32"),
+    "iti": ("sbuf", [128, 1024], "int32"),
+    "it16": ("sbuf", [128, 1024], "uint16"),
+    "el": ("sbuf", [128, 1024], "float32"),
+    "roti": ("sbuf", [128, 256], "int32"),
+    "hl": ("sbuf", [128, 512], "bfloat16"),
+    "hopi": ("sbuf", [128, 4], "int32"),
+    "hopf": ("sbuf", [128, 4], "float32"),
+    "kp": ("sbuf", [128, 288], "float32"),
+    "tw": ("sbuf", [128, 544], "float32"),
+    "kp2": ("sbuf", [128, 288], "float32"),
+    "tw2": ("sbuf", [128, 544], "float32"),
+    "kp3": ("sbuf", [128, 288], "float32"),
+    "tw3": ("sbuf", [128, 544], "float32"),
+    "dl": ("sbuf", [128, 256], "float32"),
+    "dr": ("sbuf", [128, 256], "float32"),
+    "fg": ("sbuf", [128, 512], "float32"),
+    "xe": ("sbuf", [128, 32], "float32"),
+    "yy": ("sbuf", [128, 64], "float32"),
+    "zz": ("sbuf", [128, 64], "float32"),
+    "st": ("sbuf", [128, 32], "float32"),
+    "kl": ("sbuf", [128, 256], "float32"),
+    "kr": ("sbuf", [128, 256], "float32"),
+    "ki": ("sbuf", [128, 256], "int32"),
+    "pay": ("sbuf", [128, 256], "int32"),
+    "dd": ("sbuf", [128, 256], "int32"),
+    "src": ("sbuf", [128, 256], "uint16"),
+    "mc": ("sbuf", [128, 256], "float32"),
+    "mci": ("sbuf", [128, 256], "int32"),
+    "hh": ("sbuf", [128, 256], "float32"),
+    "hw": ("sbuf", [128, 256], "float32"),
+    "qi": ("sbuf", [128, 256], "int32"),
+    "q16": ("sbuf", [128, 256], "uint16"),
+    "em": ("sbuf", [128, 144], "bfloat16"),
+    "idb": ("sbuf", [128, 128], "bfloat16"),
+    "idf": ("sbuf", [128, 128], "float32"),
+    "one": ("sbuf", [128, 128], "float32"),
+    "neg": ("sbuf", [128, 128], "float32"),
+    "ndb": ("sbuf", [128, 128], "bfloat16"),
+    "ndf": ("sbuf", [128, 128], "float32"),
+    "b0": ("sbuf", [128, 1024], "float32"),
+    "b1": ("sbuf", [128, 1024], "float32"),
+    "h0": ("sbuf", [128, 1024], "bfloat16"),
+    "h1": ("sbuf", [128, 1024], "bfloat16"),
+    "e8": ("sbuf", [128, 24], "float32"),
+    "col": ("sbuf", [128, 2], "float32"),
+    "c1": ("sbuf", [128, 48], "int32"),
+    "c2": ("sbuf", [128, 48], "int32"),
+    "c3": ("sbuf", [128, 48], "int32"),
+    "c4": ("sbuf", [128, 48], "int32"),
+    "lst": ("sbuf", [128, 48], "uint16"),
+    "p0": ("psum", [128, 1024], "float32"),
+    "p1": ("psum", [128, 1024], "float32"),
+    "p2": ("psum", [128, 1024], "float32"),
+    "pc": ("psum", [128, 512], "float32"),
+    "pr": ("psum", [128, 512], "float32"),
+}
+for _t in range(FR):
+    SCRATCH["lq%d" % _t] = ("sbuf", [128, X + 256], "float32")
+    for _k, (_a, _b, _w) in enumerate(PARTS):
+        SCRATCH["hx%d_%d" % (_t, _k)] = ("dram", [256, _b - _a], "float32")
+
+NP = 6
+SEMAPHORES = (["cv", "ca", "cp", "cg", "hs"] + ["sx%d" % k for k in range(len(PARTS))]
+              + ["%s%d_%d" % (s, t, k) for s in ("xa", "arr") for t in range(FR) for k in range(len(PARTS))]
+              + ["ld%d" % k for k in range(6)] + ["ldc%d" % k for k in range(FR + 1)] + ["ldi", "ldr", "ldh", "rwd"] + ["out%d" % k for k in range(6)]
+              + ["f%s%d" % (c, k) for c in "lab" for k in range(NP)])
+PSUM = ("p0", "p1", "p2", "pc", "pr")
+COUNTER = {"v": "cv", "a": "ca", "p": "cp", "g": "cg"}
+CY, GA, LAT = 0.00104, 1.56, 0.12
+
+
+def hazards(ops):
+    seen, chain, deps, soft = {}, {}, [], []
+    for i, o in enumerate(ops):
+        acc = []
+        for (name, lo, hi), wr in [(r, False) for r in o["r"]] + [(w, True) for w in o["w"]]:
+            if name in PSUM:
+                acc += [((name, b), max(lo, 512 * b), min(hi, 512 * b + 512), wr, True) for b in range(lo // 512, (hi - 1) // 512 + 1)]
+            else:
+                acc.append((name, lo, hi, wr, False))
+        d, s = set(o["after"]), set()
+        for name, lo, hi, wr, ps in acc:
+            for j, lo2, hi2, wr2 in seen.get(name, []):
+                if ps and ops[j]["q"] != o["q"]:
+                    d.add(j)
+                elif (wr or wr2) and lo < hi2 and lo2 < hi and not (ps and o["q"] == "p"):
+                    d.add(j)
+            if ps and o["q"] == "p":
+                if name in chain:
+                    s.add(chain[name])
+                chain[name] = i
+        for name, lo, hi, wr, ps in acc:
+            old = seen.get(name, [])
+            if wr:
+                old = [e for e in old if not (lo <= e[1] and e[2] <= hi)]
+            seen[name] = old + [(i, lo, hi, wr)]
+        d.discard(i)
+        s.discard(i)
+        deps.append(d)
+        soft.append(s)
+    return deps, soft
+
+
+def arrange(ops, deps, soft):
+    n = len(ops)
+    kids = [[] for _ in range(n)]
+    left = [0] * n
+    for i in range(n):
+        for j in deps[i] | soft[i]:
+            kids[j].append(i)
+            left[i] += 1
+    way = [0.0] * n
+    for i in range(n - 1, -1, -1):
+        way[i] = ops[i]["c"] + ops[i]["l"] + ops[i]["d"] + max([way[k] + LAT for k in kids[i]] + [0.0])
+    free, end, ready, order = {}, [0.0] * n, [i for i in range(n) if not left[i]], []
+    can = [0.0] * n
+    while ready:
+        first = min(ready, key=lambda i: (max(can[i], free.get(ops[i]["q"], 0.0)), -way[i]))
+        q = ops[first]["q"]
+        t = max(can[first], free.get(q, 0.0))
+        i = first if q is None else max([k for k in ready if ops[k]["q"] == q and can[k] <= t + CFG["eps"]], key=lambda k: way[k])
+        if can[i] > t + 0.02:
+            short = [k for k in ready if ops[k]["q"] == q and can[k] <= t + 0.02 and ops[k]["c"] <= CFG["short"]]
+            i = max(short, key=lambda k: way[k]) if short else i
+        ready.remove(i)
+        order.append(i)
+        o = ops[i]
+        t = max(can[i], free.get(q, 0.0)) + o["c"]
+        if q:
+            free[q] = t
+        t += o["l"]
+        if o["d"]:
+            t = max(t, free.get("e", 0.0)) + o["d"]
+            free["e"] = t
+        end[i] = t
+        for k in kids[i]:
+            can[k] = max(can[k], t + LAT if i in deps[k] else 0.0)
+            left[k] -= 1
+            if not left[k]:
+                ready.append(k)
+    return order
+
+
+def emit(g, T, ops, deps, order):
+    queue = {"v": g.vector, "a": g.scalar, "p": g.tensor, "g": g, "s": g.sync}
+    place = {j: k for k, j in enumerate(order)}
+    need, done, plan = set(), {}, {}
+    for i in order:
+        o = ops[i]
+        last = {}
+        for j in deps[i]:
+            key = ops[j]["sem"] or ops[j]["q"]
+            if key not in last or place[last[key]] < place[j]:
+                last[key] = j
+        plan[i] = []
+        for key, j in sorted(last.items()):
+            if o["q"] and done.get((o["q"], key), -1) < place[j]:
+                done[(o["q"], key)] = place[j]
+                plan[i].append(j)
+                need.add(j)
+    total, mark = {}, {}
+    for i in order:
+        o = ops[i]
+        q = queue.get(o["q"])
+        for j in plan[i]:
+            s = ops[j]["sem"]
+            q.wait_ge(T.sem[s or COUNTER[ops[j]["q"]]], total[s] if s else mark[j])
+        if o["sem"]:
+            if q is not None:
+                o["f"](q)
+            total[o["sem"]] = total.get(o["sem"], 0) + o["n"]
+        elif i in need:
+            s = COUNTER[o["q"]]
+            o["f"](q).then_inc(T.sem[s], 1)
+            total[s] = total.get(s, 0) + 1
+            mark[i] = total[s]
+        else:
+            o["f"](q)
+    for s in sorted(total):
+        g.wait_ge(T.sem[s], total[s])
+
+
+def helpers(core, nxt, T, topo):
+    others = [c for c in topo.cores_of(core) if T.rank_of(c) is None]
+    near = [c for c in others if topo.die(c) == topo.die(core)]
+    far = [c for c in others if topo.die(c) != topo.die(core)]
+    out = [[c for c in near if topo.may_write(c, nxt)][0], [c for c in far if topo.may_write(c, nxt)][0]]
+    return out, [c for c in near if c not in out][:2]
+
+
+def rank_program(g, core, T, topo):
+    n_ranks = len(T.cores)
+    for rank, rc in enumerate(T.cores):
+        nxt = T.cores[(rank + 1) % n_ranks]
+        ports, turns = helpers(rc, nxt, T, topo)
+        if core in ports:
+            hand_on(g, core, rc, nxt, ports.index(core), T, topo)
+        elif core == rc or core in turns:
+            ops = build(rc, T, topo)
+            deps, soft = hazards(ops)
+            order = arrange(ops, deps, soft)
+            if core == rc:
+                emit(g, T, ops, deps, order)
+            else:
+                hand_back(g, core, rc, [ops[i]["fold"] for i in order if ops[i]["fold"]], T, topo)
+
+
+def hand_on(g, core, rc, nxt, half, T, topo):
+    rid, pid, _ = topo.addr(nxt)
+    n_in = len(topo.engines(rc, core))
+    calls = 0
+    for t in range(FR):
+        r0 = (128 - 16 * t) % 128
+        for k, (a, b, who) in enumerate(PARTS):
+            if who == half:
+                g.wait_ge(T.sem["xa%d_%d" % (t, k)], n_in * (2 if t else 1))
+                g.remote_dma(T["lq%d" % t][:, a:b], T["hx%d_%d" % (t, k)][r0:r0 + 128, :], T.sem["arr%d_%d" % (t, k)], T.sem.hs,
+                             pid, rid, topo.mask(core, nxt))
+                calls += 1
+    g.wait_ge(T.sem.hs, calls * len(topo.engines(core, nxt)))
+
+
+def hand_back(g, core, rc, folds, T, topo):
+    rid, pid, _ = topo.addr(rc)
+    n = len(topo.engines(rc, core))
+    got, sent = {}, 0
+    for who, k, buf, v0, v1 in folds:
+        if who == core:
+            got[k] = got.get(k, 0) + n
+            g.wait_ge(T.sem["fa%d" % k], got[k])
+            g.remote_dma(T[buf][:, v0:v1], T[buf][:, v0:v1], T.sem["fb%d" % k], T.sem.hs, pid, rid, topo.mask(core, rc))
+            sent += len(topo.engines(core, rc))
+    if sent:
+        g.wait_ge(T.sem.hs, sent)
+
+
+def build(core, T, topo):
+    n_ranks = len(T.cores)
+    rank = T.rank_of(core)
+    nxt = T.cores[(rank + 1) % n_ranks]
+    prv = T.cores[(rank - 1) % n_ranks]
+    ports, turns = helpers(core, nxt, T, topo)
+    n_in = [len(topo.engines(c, core)) for c in helpers(prv, core, T, topo)[0]]
+    ops = []
+
+    def op(q, f, r, w, c, sem=None, n=0, l=0.0, d=0.0, after=(), fold=None):
+        ops.append({"q": q, "f": f, "r": r, "w": w, "c": c, "sem": sem, "n": n, "l": l, "d": d, "after": after, "fold": fold})
+        return len(ops) - 1
+
+    def ap(x):
+        return T[x[0]][:, x[1]:x[2]]
+
+    def rev(x):
+        return T[x[0]][:, slice(x[2] - 1, x[1] - 1 if x[1] else None, -1)]
+
+    def ind(win, off):
+        return ap(win).indirect(ap(off))
+
+    def cost(out, k=1.0):
+        return 0.05 + max(64, (out[2] - out[1]) * k) * CY
+
+    def dma(q, out, in_, r, w, sem, kb, add=False):
+        if add:
+            op(q, lambda e: e.dma_start(out, in_, accum_op=A.add).then_inc(T.sem[sem], 16), r, w, 1.0, sem, 16, 1.5, kb / 200)
+        else:
+            op(q, lambda e: e.dma_start(out, in_).then_inc(T.sem[sem], 16), r, w, 0.08, sem, 16, 1.8, kb / 400)
+
+    def tt(out, a, b, alu):
+        op("v", lambda e: e.tensor_tensor(ap(out), ap(a), ap(b), alu), [a, b], [out], cost(out, 1 if a[0] in PSUM or b[0] in PSUM else 2))
+
+    def ts(out, a, s1, o1, s2=None, o2=None, col=None):
+        if o2 is None:
+            op("v", lambda e: e.tensor_scalar(ap(out), ap(a), s1, None, o1), [a] + ([col] if col else []), [out], cost(out))
+        else:
+            op("v", lambda e: e.tensor_scalar(ap(out), ap(a), s1, s2, o1, o2), [a], [out], cost(out))
+
+    def cp(out, a):
+        op("v", lambda e: e.tensor_copy(ap(out), ap(a)), [a], [out], cost(out))
+
+    def acp(out, a, bias=None):
+        if bias is None:
+            op("a", lambda e: e.activation(ap(out), ap(a), F.Copy), [a], [out], cost(out))
+        else:
+            op("a", lambda e: e.activation(ap(out), ap(a), F.Identity, bias=bias), [a], [out], cost(out))
+
+    def fill(out, c):
+        op("v", lambda e: e.memset(ap(out), c), [], [out], cost(out))
+
+    def tr(out, a):
+        op("v", lambda e: e.transpose(ap(out), ap(a)), [a], [out], cost(out))
+
+    def gat(q, out, win, off, scale=None, bias=None, also=()):
+        r, c = [win, off] + list(also), cost(out, GA)
+        if q == "a" and scale is None:
+            op(q, lambda e: e.activation(ap(out), ind(win, off), F.Copy), r, [out], c)
+        elif q == "a":
+            op(q, lambda e: e.activation(ap(out), ind(win, off), F.Identity, bias=bias, scale=scale), r, [out], c)
+        elif scale is None:
+            op(q, lambda e: e.tensor_copy(ap(out), ind(win, off)), r, [out], c)
+        else:
+            op(q, lambda e: e.tensor_scalar(ap(out), ind(win, off), scale, bias, A.mult, A.add), r, [out], c)
+
+    def gtt(out, win, off, x, alu):
+        op("v", lambda e: e.tensor_tensor(ap(out), ind(win, off), ap(x), alu), [win, off, x], [out], cost(out, GA))
+
+    def scan(out, d0, d1, init, back=False):
+        o = rev(out) if back else ap(out)
+        x = rev(d1) if back else ap(d1)
+        col = [] if init == NONE else [init]
+        s0 = ap(init) if col else init
+        op("v", lambda e: e.tensor_tensor_scan(o, ap(d0), x, s0, A.add, A.min), [d0, d1] + col, [out], cost(out))
+
+    def iota(out, pattern, base, cm, small=False, also=()):
+        if small:
+            op("g", lambda e: e.iota(ap(out), pattern, base, cm, allow_small_or_imprecise_dtypes=True), [], [out] + list(also), 0.15 + cost(out, 2))
+        else:
+            op("g", lambda e: e.iota(ap(out), pattern, base, cm), [], [out], 0.15 + cost(out, 2))
+
+    def pick(out, a, pattern, alu, base, cm, o=None):
+        o = ap(out) if o is None else o
+        op("g", lambda e: e.affine_select(o, ap(a), pattern, alu, 0.0, base, cm), [a], [out], 0.2 + cost(a, 2))
+
+    def mm(out, lhs, x, rhs, start, stop, k=1):
+        n = out[2] - out[1]
+        op("p", lambda e: e.matmul(ap(out), ap(lhs), rhs, start, stop), [x, lhs], [out], 0.01 + max(64, n) * k * CY / 2)
+
+    LA, LB, LP = ("lst", 0, 16), ("lst", 16, 32), ("lst", 32, 48)
+
+    def turn(kp, tw):
+        tr((tw, 0, 256), (kp, 16, 272))
+        tr((tw, 256, 544), (kp, 0, 288))
+
+    cuts0 = CFG["cuts0"]
+    n0 = len(cuts0) - 1
+    for k in range(n0):
+        a, b = cuts0[k], cuts0[k + 1]
+        dma("s", T.s0[:, PB + a:PB + b], T.sp[:, a:b], [], [("s0", PB + a, PB + b)], "ld%d" % k, (b - a) / 4)
+    dma("a", T.iti[:], T.itg[:], [], [("iti", 0, 1024)], "ldi", 512)
+    dma("a", T.roti[:], T.rot[:], [], [("roti", 0, 256)], "ldr", 128)
+    for c in range(16):
+        dma("s", T.hopi[c::16, :], T.hop[:], [], [("hopi%d" % c, 0, 4)], "ldh", 1)
+
+    fill(("one", 0, 128), 1.0)
+    fill(("s0", 0, PB), 0.0)
+    fill(("s0", PB + W, 2 * PB + W), 0.0)
+    fill(("em", 0, 144), 0.0)
+    pick(("idb", 0, 128), ("one", 0, 128), [[-1, 128]], A.is_equal, 0, 1)
+    pick(("idf", 0, 128), ("one", 0, 128), [[-1, 128]], A.is_equal, 0, 1)
+    fill(("neg", 0, 128), -1.0)
+    pick(("ndb", 0, 128), ("neg", 0, 128), [[-1, 128]], A.is_equal, 0, 1)
+    pick(("ndf", 0, 128), ("neg", 0, 128), [[-1, 128]], A.is_equal, 0, 1)
+    iota(("c1", 0, 48), [[0, 48]], 0, 1)
+    iota(("c2", 0, 16), [[0, 16]], 0, 1)
+    iota(("c2", 16, 32), [[1, 16]], 0, 0)
+    iota(("c3", 0, 16), [[1, 16]], 0, 0)
+    iota(("c3", 16, 32), [[16, 16]], 0, 0)
+    pick(("e8", 16, 24), ("one", 0, 8), [[-16, 8]], A.is_ge, 0, 1)
+    pick(("em", 0, 144), ("e8", 16, 24), [[16, 8]], A.is_ge, 15, -1, T.em[:, 15:143:16])
+    pick(("e8", 0, 8), ("one", 0, 8), [[-16, 8]], A.is_equal, 0, 1)
+    pick(("e8", 8, 16), ("one", 0, 8), [[-16, 8]], A.is_equal, -15, 1)
+    iota(("mci", 0, 256), [[16, 256]], -6143, 0)
+    iota(("kl", 1, 256), [[0, 255]], 8192, 0, True)
+    iota(("kr", 1, 256), [[0, 255]], 8192, 0, True)
+    for k in range(4):
+        op("v", lambda e, k=k: e.memset(T.rw[:, X * k:X * k + X], 0.0), [], [("rw", X * k, X * k + X), ("rwl", X * k, X * k + X)], 0.6)
+    ts(("c4", 0, 32), ("c1", 0, 32), 4, A.arith_shift_right)
+    ts(("c1", 0, 32), ("c1", 0, 32), 15, A.bitwise_and)
+    fill(("vt", 0, 1), 1.0)
+    tt(("c2", 0, 32), ("c2", 0, 32), ("c4", 0, 32), A.add)
+    tt(("c3", 16, 32), ("c3", 16, 32), ("c1", 16, 32), A.add)
+    ts(("c4", 32, 48), ("c1", 0, 16), 16.0, A.mult)
+    ts(("c2", 0, 32), ("c2", 0, 32), 1, A.bitwise_and)
+    tt(("c3", 0, 16), ("c3", 0, 16), ("c4", 32, 48), A.add)
+    ts(("c2", 0, 32), ("c2", 0, 32), 272.0, A.mult)
+    cp(LP, ("c3", 0, 16))
+    cp(("col", 0, 1), ("c1", 0, 1))
+    tt(("c2", 0, 32), ("c2", 0, 32), ("c3", 0, 32), A.add)
+    cp(("lst", 0, 32), ("c2", 0, 32))
+    for kp in ("kp", "kp2", "kp3"):
+        fill((kp, 0, 16), 0.0)
+        fill((kp, 272, 288), 0.0)
+    ts(("mc", 0, 256), ("mci", 0, 256), T.col[:, 0:1], A.add, col=("col", 0, 1))
+    op("v", lambda e: e.tensor_reduce(T.kl[:, 0:1], T.e8[:, 0:8], AX.X, A.add), [("e8", 0, 8)], [("kl", 0, 1)], 0.12)
+    op("v", lambda e: e.tensor_reduce(T.kr[:, 0:1], T.e8[:, 8:16], AX.X, A.add), [("e8", 8, 16)], [("kr", 0, 1)], 0.12)
+    fill(("st", 0, 32), float(2 ** 21))
+    fill(("yy", 0, 64), NONE)
+    ts(("kl", 0, 1), ("kl", 0, 1), BIG, A.mult, 8192.0, A.add)
+    ts(("kr", 0, 1), ("kr", 0, 1), BIG, A.mult, 8192.0, A.add)
+    fill(("st", 16, 17), BIG)
+    for s in ("sa", "sb"):
+        fill((s, 0, PF), 0.0)
+        fill((s, PF + W, 2 * PF + W), 0.0)
+    op("v", lambda e: e.tensor_copy(T.hopf[:], T.hopi[:]), [("hopi%d" % c, 0, 4) for c in range(16)], [("hopf", 0, 4)], 0.12)
+    for t in range(FR):
+        cp(("it16", 256 * t, 256 * t + 256), ("iti", 256 * t, 256 * t + 256))
+
+    def targets(t):
+        gat("v", ("kp2", 16, 272), ("iti", 256 * t, 256 * t + 256), LP)
+        turn("kp2", "tw2")
+        gat("a", ("el", 256 * t, 256 * t + 256), ("tw2", 0, 544), LB, -1.0, float(4095 - 2 ** 24))
+
+    def rows():
+        dma("s", T.rw[0::16, :], T.hl[:, 0:256], [("hl", 0, 256)], [("rw", 0, W)], "rwd", 100)
+        dma("s", T.rw[4::16, :], T.hl[:, 256:512], [("hl", 256, 512)], [("rwl", 0, W)], "rwd", 100)
+
+    def to_psum(out, x, by):
+        if by.isupper():
+            acp(out, x)
+            return
+        for a in range(out[1], out[2], 512):
+            b = min(out[2], a + 512)
+            y = (x[0], x[1] + a - out[1], x[1] + b - out[1])
+            mm((out[0], a, b), ("idb" if x[0] == "s0" else "idf", 0, 128), y, ap(y), True, True, 1 if x[0] == "s0" else 4)
+
+    turnno = [0, 0, 0]
+
+    def piece_v(s, pad, v0, v1, by):
+        k = turnno[0] % 2
+        turnno[0] += 1
+        p, a, n = "p%d" % k, "a%d" % k, v1 - v0
+        z = 1 if v0 == 0 else 0
+        to_psum((p, 0, n + 3), (s, pad + v0 - 2, pad + v1 + 1), by)
+        tt((p, 0, n + 3), (p, 0, n + 3), (s, pad + v0 - 1, pad + v1 + 2), A.max)
+        acp((a, 0, n + 3), (p, 0, n + 3))
+        if by in "Vv":
+            tt((p, 0, n), (p, 0, n), (a, 3, n + 3), A.max)
+            tt(("vt", v0 + z, v1), (s, pad + v0 + z, pad + v1), (p, z, n), A.is_ge)
+        else:
+            buf = ("h%d" if s == "s0" else "b%d") % k
+            tt((buf, 0, n), (p, 0, n), (a, 3, n + 3), A.max)
+            compare(s, pad, v0, v1, buf, v0, "G")
+
+    def fold_out(s, pad, v0, v1, k):
+        buf = "bh" if s == "s0" else "bb"
+        who = turns[k % len(turns)]
+        rid, pid, _ = topo.addr(who)
+        kb = (v1 - v0) / (4 if s == "s0" else 2)
+        x = RemoteDMATransfer(dst_ids=[DstId(rid=rid, pnc=pid)], dma_engine_mask=topo.mask(core, who), remote_sem=T.sem["fa%d" % k],
+                              srcs=[T[s][:, pad + v0 + h:pad + v1 + h] for h in (-2, -1, 1, 2)], dsts=[T[buf][:, v0:v1]], alu_op=2)
+        i = op("g", lambda e: e.remote_dma_fused([x], local_sem=T.sem["fl%d" % k]), [(s, pad + v0 - 2, pad + v1 + 2), (buf + "w", v0, v1)], [],
+               1.0, "fl%d" % k, len(topo.engines(core, who)), 1.5, 4 * kb / 300, fold=(who, k, buf, v0, v1))
+        op(None, None, [], [(buf, v0, v1)], 0.0, "fb%d" % k, len(topo.engines(who, core)), 3.5 + kb / 300, after=(i,))
+
+    def compare(s, pad, v0, v1, buf, at, by):
+        parts = (v1 - v0 + 511) // 512
+        for h in range(parts):
+            a, b = v0 + (v1 - v0) * h // parts, v0 + (v1 - v0) * (h + 1) // parts
+            a = max(a, 1)
+            o = 512 * (turnno[1] % 2)
+            turnno[1] += 1
+            p, x, y = ("p2", o, o + b - a), (s, pad + a, pad + b), (buf, a - at, b - at)
+            if by == "G":
+                kind, k = ("b", 1) if s == "s0" else ("f", 4)
+                mm(p, ("id" + kind, 0, 128), x, ap(x), True, False, k)
+                mm(p, ("nd" + kind, 0, 128), y, ap(y), False, True, k)
+                ops[-1]["w"].append((buf + "w", a, b))
+                op("a", lambda e, p=p, a=a, b=b: e.activation(T.vt[:, a:b], ap(p), F.Sigmoid, bias=512.0, scale=float(2 ** 40)),
+                   [p], [("vt", a, b)], cost(p))
+            else:
+                to_psum(p, x, by)
+                tt(("vt", a, b), p, y, A.is_ge)
+                ops[-1]["w"].append((buf + "w", a, b))
+
+    def all_votes(s, pad, pcs, route, make):
+        for k, (v0, v1) in enumerate(pcs):
+            make(k)
+            if route[k] in "FfG":
+                fold_out(s, pad, v0, v1, k)
+            else:
+                piece_v(s, pad, v0, v1, route[k])
+        for k, (v0, v1) in enumerate(pcs):
+            if route[k] in "FfG":
+                compare(s, pad, v0, v1, "bh" if s == "s0" else "bb", 0, route[k])
+
+    vc = [0] + [c - 2 for c in cuts0[1:n0]] + [W]
+    targets(0)
+    cp(("hl", 0, 256), ("roti", 0, 256))
+    tt(("hl", 256, 512), ("roti", 0, 256), ("hl", 0, 256), A.subtract)
+    rows()
+    all_votes("s0", PB, [(vc[k], vc[k + 1]) for k in range(n0)], CFG["route0"], lambda k: None)
+
+    def records(k):
+        dma("s", T.cw[:, k * W:k * W + W], T.rec[:], [("vt", 0, W)], [("cw", k * W, k * W + W)], "ldc%d" % k, 1024)
+
+    records(0)
+
+    def frame(t):
+        last = t == FR - 1
+        old, opad = ("s0", PB) if t == 0 else (("sa", "sb")[(t - 1) % 2], PF)
+        new = ("sa", "sb")[t % 2]
+        lq = "lq%d" % t
+        win = (old, opad, opad + W)
+
+        def votes(q, b0, b1):
+            gat(q, ("gv", 256 * b0, 256 * b1), ("vt", 0, W), ("it16", 256 * t + 16 * b0, 256 * t + 16 * b1), -BIG, BIG * 13 / 32)
+
+        records(t + 1)
+        if t:
+            gat("a", ("kp3", 16, 272), ("lq%d" % (t - 1), X, X + 256), LP)
+            turn("kp3", "tw3")
+            gat("a", ("hl", 0, 256), ("tw3", 0, 544), LB)
+            gtt(("hl", 256, 512), ("tw3", 0, 544), LB, ("hl", 0, 256), A.subtract)
+            rows()
+        for q, b0, b1 in CFG["xs"]:
+            votes(q, b0, b1)
+            for b in range(b0, b1):
+                x = ("gv", 256 * b, 256 * b + 256)
+                mm(("pc", 0, 256), ("em", 15 - b, 143 - b), x, ap(x), b == 0, b == 15)
+
+        tt(("dl", 0, 256), ("pc", 0, 256), ("el", 256 * t, 256 * t + 256), A.max)
+        acp(("dr", 0, 256), ("dl", 0, 256), 4096.0)
+        scan(("fg", 0, 256), ("kl", 0, 256), ("dl", 0, 256), NONE)
+        scan(("fg", 256, 512), ("kr", 0, 256), ("dr", 0, 256), NONE, True)
+        tr(("xe", 0, 32), ("fg", 240, 272))
+        scan(("yy", 1, 32), ("st", 0, 31), ("xe", 0, 31), NONE)
+        scan(("yy", 32, 63), ("st", 0, 31), ("xe", 1, 32), NONE, True)
+        tr(("zz", 0, 64), ("yy", 0, 64))
+        scan(("fg", 0, 256), ("kl", 0, 256), ("dl", 0, 256), ("zz", 15, 16))
+        scan(("pc", 256, 512), ("kr", 0, 256), ("dr", 0, 256), ("zz", 48, 49), True)
+        tt(("kp", 16, 272), ("fg", 0, 256), ("pc", 256, 512), A.min)
+        turn("kp", "tw")
+        dc = CFG["dcl" if last else "dc"]
+        for a, b in zip(dc[1:], dc):
+            z = ("p2", a, b)
+            gat("v", ("ki", a, b), ("tw", 0, 544), ("lst", a // 16, b // 16))
+            ts(("pay", a, b), ("ki", a, b), 8191, A.bitwise_and)
+            ts(("dd", a, b), ("ki", a, b), 12, A.arith_shift_right, -2, A.bitwise_and)
+            ts(z, ("pay", a, b), 4096.0, A.is_lt, 0.5, A.subtract)
+            tt(z, z, ("dd", a, b), A.mult)
+            tt(z, z, ("pay", a, b), A.subtract)
+            ts(("src", a, b), z, 6143.0, A.add, 4095.0, A.min)
+            tt(("hw", a, b), ("mc", a, b), z, A.subtract)
+            ts(("qi", a, b), ("hw", a, b), T.hopf[:, t:t + 1], A.mult, col=("hopf", 0, 4))
+            ts(("qi", a, b), ("qi", a, b), W - 1, A.bitwise_and)
+            cp(("hh", a, b), ("qi", a, b))
+
+        def rot_of(q, ps, m0, m1):
+            a, b = m0 // 16, m1 // 16
+            gat(q, ("rg", m0, m1), ("rw", 0, W), ("src", a, b), also=[("rwl", 0, W)] + ([("hh", a, b)] if q == "v" and CFG["hfirst"] else []))
+            for r in range(16):
+                mm((ps, 0, b - a), ("em", 15 - r, 143 - r), ("rg", m0, m1), T.rg[:, m0 + r:m1:16], r == 0, False)
+            mm((ps, 0, b - a), ("idf", 0, 128), ("hh", a, b), T.hh[:, a:b], False, True, 4)
+            if m0 >= W - X:
+                cp(("xo", X, XW), (ps, 0, b - a))
+            else:
+                cp(("q16", 64 + a, 64 + b), (ps, 0, b - a))
+                if not last:
+                    acp((lq, XW + a, XW + b), (ps, 0, b - a))
+
+        def t_gather(q, m0, m1):
+            out = ("xo", m0 - (W - X), m1 - (W - X)) if m0 >= W - X else ("tb", m0, m1)
+            gat(q, out, win, ("src", m0 // 16, m1 // 16))
+
+        def product(n0, n1):
+            gtt((new, PF + n0, PF + n1), ("cw", 0, (t + 2) * W), ("q16", n0 // 16, n1 // 16), (lq, n0, n1) if n0 < X else ("tb", n0 - X, n1 - X), A.mult)
+
+        def send():
+            twice = 2 if t else 1
+            for k, (a, b, w) in enumerate(PARTS):
+                who = ports[w]
+                rid, pid, _ = topo.addr(who)
+                x = RemoteDMATransfer(dst_ids=[DstId(rid=rid, pnc=pid)] * twice, dma_engine_mask=topo.mask(core, who),
+                                      remote_sem=T.sem["xa%d_%d" % (t, k)], srcs=[T.xo[:, a:b]],
+                                      dsts=[T["hx%d_%d" % (t, k)][128 * j:128 * j + 128, :] for j in range(twice)])
+                i = op("g", lambda e, x=x, k=k: e.remote_dma_fused([x], local_sem=T.sem["sx%d" % k]), [("xo", a, b)], [],
+                       1.0, "sx%d" % k, len(topo.engines(core, who)), 1.5, twice * (b - a) / 600)
+                op(None, None, [], [(lq, a, b)], 0.0, "arr%d_%d" % (t, k), n_in[w], 8.0, after=(i,))
+            cp(("q16", 0, 64), (lq, X, XW))
+
+        def t_top(q):
+            t_gather(q, W - 512, W)
+            t_gather(q, W - X, W - 512)
+
+        top = (W - X, W)
+        if not last:
+            rq, tq = CFG["rq"], CFG["tq"]
+            rot_of(rq[0], "pr", *top)
+            t_top(tq[0])
+            send()
+            rc, yc = CFG["rc"], CFG["yc"]
+            for k in range(len(rc) - 1):
+                rot_of(rq[k + 1], ("pc", "pr")[k % 2], rc[k + 1], rc[k])
+            targets(t + 1)
+
+            def make(k):
+                if yc[k + 1] >= X:
+                    t_gather(tq[k + 1], yc[k + 1] - X, yc[k] - X)
+                product(yc[k + 1], yc[k])
+
+            vc = [W] + [c + 2 for c in yc[1:-1]] + [0]
+            all_votes(new, PF, [(vc[k + 1], vc[k]) for k in range(len(yc) - 1)], CFG["route"], make)
+        else:
+            def store(n0, n1, ps, k):
+                y0, y1 = n0 % 2048, n0 % 2048 + n1 - n0
+                product(n0, n1)
+                tt(("bb", y0, y1), (new, PF + n0, PF + n1), (ps, y0 % X, y0 % X + n1 - n0), A.add)
+                dma("sa"[k % 2], T.y[:, y0:y1], T.bb[:, y0:y1], [("bb", y0, y1)], [("y", y0, y1)], "out%d" % k, (n1 - n0) / 2)
+
+            rot_of(CFG["lr"][0], "pr", *top)
+            t_top(CFG["lt"][0])
+            send()
+            for k in range(3):
+                rot_of(CFG["lr"][k + 1], ("pc", "pr")[k % 2], k * X, k * X + X)
+                t_gather(CFG["lt"][k + 1], k * X, k * X + X)
+                if k < 2:
+                    product(k * X + X, k * X + 2 * X)
+                    acp((("p1", "p0")[k], 0, X), (new, PF + k * X + X, PF + k * X + 2 * X))
+            store(3 * X, W, "p1", 0)
+            lc = CFG["lc"]
+            for k in range(len(lc) - 1):
+                store(lc[k + 1], lc[k], "p0", k + 1)
+
+    for t in range(FR):
+        frame(t)
+    return ops

@@ -5,35 +5,44 @@ W = 4096
 X = 1024
 FR = 4
 PF, PB = 8, 16
-XW = X + X // 16
-PARTS = [(512, X, 1), (0, 512, 0), (X, XW, 0)]
+HX, QX = X // 2, X // 16
+XW = X + QX
+PARTS = [(0, HX), (HX, XW)]
 BIG = float(2 ** 27)
 NONE = float(2 ** 26)
+RND = 1.5 * 2 ** 23
+BB = W // 2
 
 CFG = {
-    "cuts0": [0, 512, 1408, 2304, 3200, W], "route0": "wGGww",
-    "route": "FFWVVV", "hfirst": 0,
-    "rq": "vaaaa", "tq": "avaaa", "dc": [256, 128, 0], "dcl": [256, 192, 0],
-    "rc": [3072, 2304, 1536, 768, 0], "yc": [W, 3328, 2560, 1792, X, 512, 0],
-    "lr": "vvav", "lt": "aaaa", "lc": [X, 512, 256, 0], "eps": 0.15, "short": 0.2,
-    "xs": [("v", 0, 4), ("a", 8, 12), ("v", 4, 6), ("a", 12, 14), ("v", 6, 7), ("a", 14, 15), ("v", 7, 8), ("a", 15, 16)],
+    "cuts0": [0, 896, 1536, 2304, 3200, W], "route0": "XwXWW",
+    "yc": [W, 3200, 2432, 1792, X, 512, 0], "vc": [3200, 2432, 1792, X, 512], "route": ["zzzwwv"] * 3, "by": "vvvvvv",
+    "now": False, "cut": 2048, "kq": "va", "lo": "a", "add": 3.0, "jc": 512, "jl": 0, "hold": 0, "ya": "a",
+    "top": "xxxx", "rq": "xxxax", "tq": "axxxx",
+    "steps": "g0 t s p0 h v0 g1 g2 n p1 v1 p2 g3 p3 v3 j0 q v2 c p4 p5 j1 v4 j2 v5 j3 j4 j5",
+    "ls": [0, 2 * X, X, -1], "ld": [X, 512, 256, 0], "lc": [X, 512, 256, 0], "eps": [0.05, 0.2, 0.35], "short": 0.05, "loose": 0,
+    "xs": [0, 2, 5, 8, 11, 13, 14, 15, 16],
+    "ways": [(0.25, 0.8, 1.0), (0.15, 1.3, 1.0), (0.25, 1.0, 1.5), (0.3, 1.3, 1.1)], "safe": 1.5, "dr": "v", "tn": "c", "dc": 128,
+    "cy": 0.00088, "lat": 0.25, "arr": 6.0, "far": 2.0, "back": 3.5, "once": 3.0, "turns": 3, "ga": 1.45,
 }
 
 SCRATCH = {
     "s0": ("sbuf", [128, W + 2 * PB], "bfloat16"),
     "sa": ("sbuf", [128, W + 2 * PF], "float32"),
     "sb": ("sbuf", [128, W + 2 * PF], "float32"),
-    "bb": ("sbuf", [128, W], "float32"),
-    "bh": ("sbuf", [128, W], "bfloat16"),
+    "bb": ("sbuf", [128, W // 2], "float32"),
     "cw": ("sbuf", [128, (FR + 1) * W], "bfloat16"),
+    "cr": ("sbuf", [128, W], "bfloat16"),
     "tb": ("sbuf", [128, W - X], "float32"),
     "xo": ("sbuf", [128, XW], "float32"),
-    "vt": ("sbuf", [128, W], "bfloat16"),
+    "vt": ("sbuf", [128, W], "float32"),
     "gv": ("sbuf", [128, W], "bfloat16"),
-    "rw": ("sbuf", [128, W], "bfloat16"),
     "rg": ("sbuf", [128, W], "bfloat16"),
-    "a0": ("sbuf", [128, 1024], "float32"),
-    "a1": ("sbuf", [128, 1024], "float32"),
+    "a0": ("sbuf", [128, 512], "float32"),
+    "a1": ("sbuf", [128, 512], "float32"),
+    "b0": ("sbuf", [128, 1024], "float32"),
+    "b1": ("sbuf", [128, 1024], "float32"),
+    "h0": ("sbuf", [128, 1024], "bfloat16"),
+    "h1": ("sbuf", [128, 1024], "bfloat16"),
     "iti": ("sbuf", [128, 1024], "int32"),
     "it16": ("sbuf", [128, 1024], "uint16"),
     "el": ("sbuf", [128, 1024], "float32"),
@@ -49,6 +58,7 @@ SCRATCH = {
     "tw3": ("sbuf", [128, 544], "float32"),
     "dl": ("sbuf", [128, 256], "float32"),
     "dr": ("sbuf", [128, 256], "float32"),
+    "elr": ("sbuf", [128, 256], "float32"),
     "fg": ("sbuf", [128, 512], "float32"),
     "xe": ("sbuf", [128, 32], "float32"),
     "yy": ("sbuf", [128, 64], "float32"),
@@ -61,126 +71,173 @@ SCRATCH = {
     "dd": ("sbuf", [128, 256], "int32"),
     "src": ("sbuf", [128, 256], "uint16"),
     "mc": ("sbuf", [128, 256], "float32"),
-    "mci": ("sbuf", [128, 256], "int32"),
-    "hh": ("sbuf", [128, 256], "float32"),
     "hw": ("sbuf", [128, 256], "float32"),
-    "qi": ("sbuf", [128, 256], "int32"),
+    "qb": ("sbuf", [128, 256], "float32"),
+    "hd": ("sbuf", [128, 128], "float32"),
+    "kk": ("sbuf", [128, 256], "float32"),
+    "qf": ("sbuf", [128, 256], "float32"),
+    "qi": ("sbuf", [128, 64], "int32"),
     "q16": ("sbuf", [128, 256], "uint16"),
-    "em": ("sbuf", [128, 144], "bfloat16"),
+    "cb": ("sbuf", [128, 256], "bfloat16"),
+    "cm": ("sbuf", [128, QX], "bfloat16"),
+    "ea": ("sbuf", [128, 144], "bfloat16"),
+    "ev": ("sbuf", [128, 144], "bfloat16"),
+    "b2": ("sbuf", [128, 1024], "float32"),
+    "b3": ("sbuf", [128, 1024], "float32"),
+    "er": ("sbuf", [128, 144], "bfloat16"),
+    "one": ("sbuf", [128, 16], "float32"),
+    "nil": ("sbuf", [128, 128], "float32"),
+    "idf": ("sbuf", [128, 256], "float32"),
+    "upf": ("sbuf", [128, 128], "float32"),
+    "dnf": ("sbuf", [128, 128], "float32"),
+    "hff": ("sbuf", [128, 128], "float32"),
     "idb": ("sbuf", [128, 128], "bfloat16"),
-    "idf": ("sbuf", [128, 128], "float32"),
-    "one": ("sbuf", [128, 128], "float32"),
-    "neg": ("sbuf", [128, 128], "float32"),
-    "ndb": ("sbuf", [128, 128], "bfloat16"),
-    "ndf": ("sbuf", [128, 128], "float32"),
-    "b0": ("sbuf", [128, 1024], "float32"),
-    "b1": ("sbuf", [128, 1024], "float32"),
-    "h0": ("sbuf", [128, 1024], "bfloat16"),
-    "h1": ("sbuf", [128, 1024], "bfloat16"),
-    "e8": ("sbuf", [128, 24], "float32"),
+    "upb": ("sbuf", [128, 128], "bfloat16"),
+    "dnb": ("sbuf", [128, 128], "bfloat16"),
+    "hfb": ("sbuf", [128, 128], "bfloat16"),
+    "e8": ("sbuf", [128, 32], "float32"),
     "col": ("sbuf", [128, 2], "float32"),
     "c1": ("sbuf", [128, 48], "int32"),
     "c2": ("sbuf", [128, 48], "int32"),
     "c3": ("sbuf", [128, 48], "int32"),
     "c4": ("sbuf", [128, 48], "int32"),
     "lst": ("sbuf", [128, 48], "uint16"),
-    "p0": ("psum", [128, 1024], "float32"),
-    "p1": ("psum", [128, 1024], "float32"),
-    "p2": ("psum", [128, 1024], "float32"),
+    "pe0": ("psum", [128, 512], "float32"),
+    "pe1": ("psum", [128, 512], "float32"),
+    "pm": ("psum", [128, 1024], "float32"),
+    "pd": ("psum", [128, 1024], "float32"),
     "pc": ("psum", [128, 512], "float32"),
     "pr": ("psum", [128, 512], "float32"),
 }
 for _t in range(FR):
-    SCRATCH["lq%d" % _t] = ("sbuf", [128, X + 256], "float32")
-    for _k, (_a, _b, _w) in enumerate(PARTS):
+    SCRATCH["lq%d" % _t] = ("sbuf", [128, XW], "float32")
+    if 0 < _t < FR - 1:
+        SCRATCH["lu%d" % _t] = ("sbuf", [128, XW - HX], "float32")
+    for _k, (_a, _b) in enumerate(PARTS):
         SCRATCH["hx%d_%d" % (_t, _k)] = ("dram", [256, _b - _a], "float32")
 
-NP = 6
+NP = 8
 SEMAPHORES = (["cv", "ca", "cp", "cg", "hs"] + ["sx%d" % k for k in range(len(PARTS))]
               + ["%s%d_%d" % (s, t, k) for s in ("xa", "arr") for t in range(FR) for k in range(len(PARTS))]
-              + ["ld%d" % k for k in range(6)] + ["ldc%d" % k for k in range(FR + 1)] + ["ldi", "ldr", "ldh", "rwd"] + ["out%d" % k for k in range(6)]
-              + ["f%s%d" % (c, k) for c in "lab" for k in range(NP)])
-PSUM = ("p0", "p1", "p2", "pc", "pr")
+              + ["ld%d" % k for k in range(6)] + ["ldc%d" % k for k in range(FR + 1)] + ["ldi0", "ldi1", "ldr", "ldh", "ldq", "rwd", "trn", "zd0", "zd1", "zd2", "zd3", "ya"]
+              + ["out%d" % k for k in range(8)] + ["f%s%d" % (c, k) for c in "lab" for k in range(NP)])
+PSUM = ("pe0", "pe1", "pm", "pd", "pc", "pr")
 COUNTER = {"v": "cv", "a": "ca", "p": "cp", "g": "cg"}
-CY, GA, LAT = 0.00104, 1.56, 0.12
 
 
 def hazards(ops):
     seen, chain, deps, soft = {}, {}, [], []
     for i, o in enumerate(ops):
         acc = []
-        for (name, lo, hi), wr in [(r, False) for r in o["r"]] + [(w, True) for w in o["w"]]:
+        for x, wr in [(r, False) for r in o["r"]] + [(w, True) for w in o["w"]]:
+            name, lo, hi = x[:3]
+            lane = lo % 2 if len(x) > 3 else None
             if name in PSUM:
-                acc += [((name, b), max(lo, 512 * b), min(hi, 512 * b + 512), wr, True) for b in range(lo // 512, (hi - 1) // 512 + 1)]
+                acc += [((name, b), max(lo, 512 * b), min(hi, 512 * b + 512), wr, True, lane) for b in range(lo // 512, (hi - 1) // 512 + 1)]
             else:
-                acc.append((name, lo, hi, wr, False))
+                acc.append((name, lo, hi, wr, False, lane))
         d, s = set(o["after"]), set()
-        for name, lo, hi, wr, ps in acc:
-            for j, lo2, hi2, wr2 in seen.get(name, []):
+        for name, lo, hi, wr, ps, lane in acc:
+            for j, lo2, hi2, wr2, lane2 in seen.get(name, []):
                 if ps and ops[j]["q"] != o["q"]:
                     d.add(j)
-                elif (wr or wr2) and lo < hi2 and lo2 < hi and not (ps and o["q"] == "p"):
-                    d.add(j)
+                elif (wr or wr2) and lo < hi2 and lo2 < hi and not (ps and o["q"] == "p") and (lane is None or lane2 is None or lane == lane2):
+                    if CFG["loose"] and wr and not wr2 and o["q"] in ("v", "a") and ops[j]["q"] == o["q"] and not o["sem"] and not ops[j]["sem"]:
+                        s.add(j)
+                    else:
+                        d.add(j)
             if ps and o["q"] == "p":
                 if name in chain:
                     s.add(chain[name])
                 chain[name] = i
-        for name, lo, hi, wr, ps in acc:
+        for name, lo, hi, wr, ps, lane in acc:
             old = seen.get(name, [])
             if wr:
-                old = [e for e in old if not (lo <= e[1] and e[2] <= hi)]
-            seen[name] = old + [(i, lo, hi, wr)]
+                old = [e for e in old if not (lo <= e[1] and e[2] <= hi and lane in (None, e[4]) and (not ps or e[0] in d or ops[e[0]]["q"] == o["q"]))]
+            seen[name] = old + [(i, lo, hi, wr, lane)]
         d.discard(i)
         s.discard(i)
         deps.append(d)
-        soft.append(s)
+        soft.append(s - d)
     return deps, soft
 
 
 def arrange(ops, deps, soft):
-    n = len(ops)
-    kids = [[] for _ in range(n)]
-    left = [0] * n
+    n, lat = len(ops), CFG["lat"]
+    kids, parents = [[] for _ in range(n)], [sorted(deps[i] | soft[i]) for i in range(n)]
     for i in range(n):
-        for j in deps[i] | soft[i]:
+        for j in parents[i]:
             kids[j].append(i)
-            left[i] += 1
-    way = [0.0] * n
-    for i in range(n - 1, -1, -1):
-        way[i] = ops[i]["c"] + ops[i]["l"] + ops[i]["d"] + max([way[k] + LAT for k in kids[i]] + [0.0])
-    free, end, ready, order = {}, [0.0] * n, [i for i in range(n) if not left[i]], []
-    can = [0.0] * n
-    while ready:
-        first = min(ready, key=lambda i: (max(can[i], free.get(ops[i]["q"], 0.0)), -way[i]))
-        q = ops[first]["q"]
-        t = max(can[first], free.get(q, 0.0))
-        i = first if q is None else max([k for k in ready if ops[k]["q"] == q and can[k] <= t + CFG["eps"]], key=lambda k: way[k])
-        if can[i] > t + 0.02:
-            short = [k for k in ready if ops[k]["q"] == q and can[k] <= t + 0.02 and ops[k]["c"] <= CFG["short"]]
-            i = max(short, key=lambda k: way[k]) if short else i
-        ready.remove(i)
-        order.append(i)
-        o = ops[i]
-        t = max(can[i], free.get(q, 0.0)) + o["c"]
-        if q:
+
+    def lay(rank, queue, back, eps):
+        before, after = (kids, parents) if back else (parents, kids)
+        left = [len(x) for x in before]
+        free, order, can, end, took = {}, [], [0.0] * n, [0.0] * n, list(queue)
+        ready = {q: [] for q in set(queue) | set("av")}
+        for i in range(n):
+            if not left[i]:
+                ready[queue[i]].append(i)
+        while len(order) < n:
+            t, q = min((max(min(can[i] for i in r), free.get(x, 0.0)), x) for y, r in ready.items() if r for x in ("av" if y == "x" else [y]))
+            mine = ready[q] + (ready.get("x", []) if q in ("a", "v") else [])
+
+            def place(k):
+                return (q == "v" and queue[k] == "x" and not ops[k]["now"], rank[k], k)
+
+            i = min([k for k in mine if can[k] <= t + eps], key=place)
+            if can[i] > t + 0.02:
+                short = [k for k in mine if max(t, can[k]) + ops[k]["c"] <= can[i] + CFG["short"]]
+                i = min(short, key=place) if short else i
+            ready[queue[i]].remove(i)
+            order.append(i)
+            o = ops[i]
+            t = max(can[i], free.get(q, 0.0)) + o["c"]
+            took[i] = q
+            if q:
+                free[q] = t
+            if not back:
+                t += o["l"]
+                if o["d"]:
+                    t = max(t, free.get("e", 0.0)) + o["d"]
+                    free["e"] = t
+            end[i] = t
+            for k in after[i]:
+                if (k in deps[i]) if back else (i in deps[k]):
+                    can[k] = max(can[k], t + lat + (ops[k]["l"] * CFG["safe"] + ops[k]["d"] if back else 0.0))
+                left[k] -= 1
+                if not left[k]:
+                    ready[queue[k]].append(k)
+        return max(end), order, took, end
+
+    def replay(order, took, wake, dma, pe):
+        free, end = {}, [0.0] * n
+        for i in order:
+            o, q = ops[i], took[i]
+            t = max([free.get(q, 0.0) if q else 0.0] + [end[j] + wake for j in deps[i]]) + o["c"] * (pe if q == "p" else 1.0)
             free[q] = t
-        t += o["l"]
-        if o["d"]:
-            t = max(t, free.get("e", 0.0)) + o["d"]
-            free["e"] = t
-        end[i] = t
-        for k in kids[i]:
-            can[k] = max(can[k], t + LAT if i in deps[k] else 0.0)
-            left[k] -= 1
-            if not left[k]:
-                ready.append(k)
-    return order
+            t += o["l"] * dma
+            if o["d"]:
+                t = free["e"] = max(t, free.get("e", 0.0)) + o["d"] * dma
+            end[i] = t
+        return max(end)
+
+    queue = [o["q"] or "" for o in ops]
+    best = None
+    for eps in CFG["eps"]:
+        now = lay([o["p"] for o in ops], queue, False, eps)
+        for _ in range(CFG["turns"]):
+            now = lay([-e for e in lay([-e for e in now[3]], now[2], True, eps)[3]], queue, False, eps)
+            now = (sum(replay(now[1], now[2], *w) for w in CFG["ways"]),) + now[1:]
+            best = min(best or now, now)
+    for o, q in zip(ops, best[2]):
+        o["q"] = q or None
+    return best[1]
 
 
 def emit(g, T, ops, deps, order):
     queue = {"v": g.vector, "a": g.scalar, "p": g.tensor, "g": g, "s": g.sync}
     place = {j: k for k, j in enumerate(order)}
-    need, done, plan = set(), {}, {}
+    need, done, knew, plan = set(), {}, {}, {}
     for i in order:
         o = ops[i]
         last = {}
@@ -189,11 +246,14 @@ def emit(g, T, ops, deps, order):
             if key not in last or place[last[key]] < place[j]:
                 last[key] = j
         plan[i] = []
-        for key, j in sorted(last.items()):
-            if o["q"] and done.get((o["q"], key), -1) < place[j]:
-                done[(o["q"], key)] = place[j]
+        mine = done.setdefault(o["q"], {})
+        for key, j in sorted(last.items(), key=lambda x: -place[x[1]]):
+            if o["q"] and mine.get(key, -1) < place[j]:
+                for k, v in list(knew[j].items()) + [(key, place[j])]:
+                    mine[k] = max(mine.get(k, -1), v)
                 plan[i].append(j)
                 need.add(j)
+        knew[i] = dict(mine) if o["q"] else {}
     total, mark = {}, {}
     for i in order:
         o = ops[i]
@@ -220,8 +280,17 @@ def helpers(core, nxt, T, topo):
     others = [c for c in topo.cores_of(core) if T.rank_of(c) is None]
     near = [c for c in others if topo.die(c) == topo.die(core)]
     far = [c for c in others if topo.die(c) != topo.die(core)]
-    out = [[c for c in near if topo.may_write(c, nxt)][0], [c for c in far if topo.may_write(c, nxt)][0]]
+    out = [[c for c in far if topo.may_write(c, nxt)][0], [c for c in near if topo.may_write(c, nxt)][0]]
     return out, [c for c in near if c not in out][:2]
+
+
+def turned(t):
+    return t if t < FR - 1 else 0
+
+
+def senders(t, core, nxt, T, topo):
+    ports = helpers(core, nxt, T, topo)[0]
+    return [ports[0], core if topo.may_write(core, nxt) else ports[1]]
 
 
 def rank_program(g, core, T, topo):
@@ -230,7 +299,7 @@ def rank_program(g, core, T, topo):
         nxt = T.cores[(rank + 1) % n_ranks]
         ports, turns = helpers(rc, nxt, T, topo)
         if core in ports:
-            hand_on(g, core, rc, nxt, ports.index(core), T, topo)
+            hand_on(g, core, rc, nxt, T, topo)
         elif core == rc or core in turns:
             ops = build(rc, T, topo)
             deps, soft = hazards(ops)
@@ -241,30 +310,31 @@ def rank_program(g, core, T, topo):
                 hand_back(g, core, rc, [ops[i]["fold"] for i in order if ops[i]["fold"]], T, topo)
 
 
-def hand_on(g, core, rc, nxt, half, T, topo):
+def hand_on(g, core, rc, nxt, T, topo):
     rid, pid, _ = topo.addr(nxt)
     n_in = len(topo.engines(rc, core))
     calls = 0
     for t in range(FR):
-        r0 = (128 - 16 * t) % 128
-        for k, (a, b, who) in enumerate(PARTS):
-            if who == half:
-                g.wait_ge(T.sem["xa%d_%d" % (t, k)], n_in * (2 if t else 1))
+        r0 = (128 - 16 * turned(t)) % 128
+        for k, (a, b) in enumerate(PARTS):
+            if senders(t, rc, nxt, T, topo)[k] == core:
+                g.wait_ge(T.sem["xa%d_%d" % (t, k)], n_in * (2 if turned(t) else 1))
                 g.remote_dma(T["lq%d" % t][:, a:b], T["hx%d_%d" % (t, k)][r0:r0 + 128, :], T.sem["arr%d_%d" % (t, k)], T.sem.hs,
                              pid, rid, topo.mask(core, nxt))
                 calls += 1
-    g.wait_ge(T.sem.hs, calls * len(topo.engines(core, nxt)))
+    if calls:
+        g.wait_ge(T.sem.hs, calls * len(topo.engines(core, nxt)))
 
 
 def hand_back(g, core, rc, folds, T, topo):
     rid, pid, _ = topo.addr(rc)
     n = len(topo.engines(rc, core))
     got, sent = {}, 0
-    for who, k, buf, v0, v1 in folds:
+    for who, k, v0, v1 in folds:
         if who == core:
             got[k] = got.get(k, 0) + n
             g.wait_ge(T.sem["fa%d" % k], got[k])
-            g.remote_dma(T[buf][:, v0:v1], T[buf][:, v0:v1], T.sem["fb%d" % k], T.sem.hs, pid, rid, topo.mask(core, rc))
+            g.remote_dma(T.bb[:, v0 - BB:v1 - BB], T.bb[:, v0 - BB:v1 - BB], T.sem["fb%d" % k], T.sem.hs, pid, rid, topo.mask(core, rc))
             sent += len(topo.engines(core, rc))
     if sent:
         g.wait_ge(T.sem.hs, sent)
@@ -275,16 +345,25 @@ def build(core, T, topo):
     rank = T.rank_of(core)
     nxt = T.cores[(rank + 1) % n_ranks]
     prv = T.cores[(rank - 1) % n_ranks]
-    ports, turns = helpers(core, nxt, T, topo)
-    n_in = [len(topo.engines(c, core)) for c in helpers(prv, core, T, topo)[0]]
-    ops = []
+    turns = helpers(core, nxt, T, topo)[1]
+    cy, GA = CFG["cy"], CFG["ga"]
+    ops, lag, firsts = [], [0], set()
 
-    def op(q, f, r, w, c, sem=None, n=0, l=0.0, d=0.0, after=(), fold=None):
-        ops.append({"q": q, "f": f, "r": r, "w": w, "c": c, "sem": sem, "n": n, "l": l, "d": d, "after": after, "fold": fold})
+    def op(q, f, r, w, c, sem=None, n=0, l=0.0, d=0.0, after=(), fold=None, now=False):
+        ops.append({"q": q, "f": f, "r": r, "w": w, "c": c, "sem": sem, "n": n, "l": l, "d": d, "after": after, "fold": fold,
+                    "now": now, "p": len(ops) + lag[0]})
         return len(ops) - 1
 
+    def once(who):
+        new = who not in firsts
+        firsts.add(who)
+        return CFG["once"] if new else 0.0
+
     def ap(x):
-        return T[x[0]][:, x[1]:x[2]]
+        return T[x[0]][:, x[1]:x[2]:x[3]] if len(x) > 3 else T[x[0]][:, x[1]:x[2]]
+
+    def size(x):
+        return len(range(*x[1:]))
 
     def rev(x):
         return T[x[0]][:, slice(x[2] - 1, x[1] - 1 if x[1] else None, -1)]
@@ -293,13 +372,10 @@ def build(core, T, topo):
         return ap(win).indirect(ap(off))
 
     def cost(out, k=1.0):
-        return 0.05 + max(64, (out[2] - out[1]) * k) * CY
+        return (0.05 if k == GA else 0.02) + max(64, size(out) * k) * cy
 
-    def dma(q, out, in_, r, w, sem, kb, add=False):
-        if add:
-            op(q, lambda e: e.dma_start(out, in_, accum_op=A.add).then_inc(T.sem[sem], 16), r, w, 1.0, sem, 16, 1.5, kb / 200)
-        else:
-            op(q, lambda e: e.dma_start(out, in_).then_inc(T.sem[sem], 16), r, w, 0.08, sem, 16, 1.8, kb / 400)
+    def dma(q, out, in_, r, w, sem, kb):
+        op(q, lambda e: e.dma_start(out, in_).then_inc(T.sem[sem], 16), r, w, 0.08, sem, 16, 1.5, kb / 600)
 
     def tt(out, a, b, alu):
         op("v", lambda e: e.tensor_tensor(ap(out), ap(a), ap(b), alu), [a, b], [out], cost(out, 1 if a[0] in PSUM or b[0] in PSUM else 2))
@@ -308,16 +384,13 @@ def build(core, T, topo):
         if o2 is None:
             op("v", lambda e: e.tensor_scalar(ap(out), ap(a), s1, None, o1), [a] + ([col] if col else []), [out], cost(out))
         else:
-            op("v", lambda e: e.tensor_scalar(ap(out), ap(a), s1, s2, o1, o2), [a], [out], cost(out))
+            op("v", lambda e: e.tensor_scalar(ap(out), ap(a), s1, s2, o1, o2), [a] + ([col] if col else []), [out], cost(out))
 
     def cp(out, a):
         op("v", lambda e: e.tensor_copy(ap(out), ap(a)), [a], [out], cost(out))
 
-    def acp(out, a, bias=None):
-        if bias is None:
-            op("a", lambda e: e.activation(ap(out), ap(a), F.Copy), [a], [out], cost(out))
-        else:
-            op("a", lambda e: e.activation(ap(out), ap(a), F.Identity, bias=bias), [a], [out], cost(out))
+    def act(out, a, func=F.Copy, col=None, **k):
+        op("a", lambda e: e.activation(ap(out), ap(a), func, **k), [a] + ([col] if col else []), [out], cost(out) + 0.03)
 
     def fill(out, c):
         op("v", lambda e: e.memset(ap(out), c), [], [out], cost(out))
@@ -325,16 +398,23 @@ def build(core, T, topo):
     def tr(out, a):
         op("v", lambda e: e.transpose(ap(out), ap(a)), [a], [out], cost(out))
 
-    def gat(q, out, win, off, scale=None, bias=None, also=()):
-        r, c = [win, off] + list(also), cost(out, GA)
-        if q == "a" and scale is None:
-            op(q, lambda e: e.activation(ap(out), ind(win, off), F.Copy), r, [out], c)
-        elif q == "a":
-            op(q, lambda e: e.activation(ap(out), ind(win, off), F.Identity, bias=bias, scale=scale), r, [out], c)
-        elif scale is None:
-            op(q, lambda e: e.tensor_copy(ap(out), ind(win, off)), r, [out], c)
+    def gat(q, out, win, off, func=F.Copy, now=False, **k):
+        i = len(ops)
+
+        def call(e):
+            if ops[i]["q"] == "a":
+                return e.activation(ap(out), ind(win, off), func, **k)
+            if func == F.Sign:
+                return e.tensor_scalar(ap(out), ind(win, off), 0.0, 0.5, A.is_le, A.subtract)
+            return e.tensor_copy(ap(out), ind(win, off))
+
+        op(q, call, [win, off], [out], cost(out, GA), now=now)
+
+    def gts(out, win, off, s1, o1, s2=None, o2=None):
+        if o2 is None:
+            op("v", lambda e: e.tensor_scalar(ap(out), ind(win, off), s1, None, o1), [win, off], [out], cost(out, GA))
         else:
-            op(q, lambda e: e.tensor_scalar(ap(out), ind(win, off), scale, bias, A.mult, A.add), r, [out], c)
+            op("v", lambda e: e.tensor_scalar(ap(out), ind(win, off), s1, s2, o1, o2), [win, off], [out], cost(out, GA))
 
     def gtt(out, win, off, x, alu):
         op("v", lambda e: e.tensor_tensor(ap(out), ind(win, off), ap(x), alu), [win, off, x], [out], cost(out, GA))
@@ -346,19 +426,20 @@ def build(core, T, topo):
         s0 = ap(init) if col else init
         op("v", lambda e: e.tensor_tensor_scan(o, ap(d0), x, s0, A.add, A.min), [d0, d1] + col, [out], cost(out))
 
-    def iota(out, pattern, base, cm, small=False, also=()):
+    def iota(out, pattern, base, cm, small=False):
         if small:
-            op("g", lambda e: e.iota(ap(out), pattern, base, cm, allow_small_or_imprecise_dtypes=True), [], [out] + list(also), 0.15 + cost(out, 2))
+            op("g", lambda e: e.iota(ap(out), pattern, base, cm, allow_small_or_imprecise_dtypes=True), [], [out], 0.15 + cost(out, 2))
         else:
             op("g", lambda e: e.iota(ap(out), pattern, base, cm), [], [out], 0.15 + cost(out, 2))
 
-    def pick(out, a, pattern, alu, base, cm, o=None):
-        o = ap(out) if o is None else o
-        op("g", lambda e: e.affine_select(o, ap(a), pattern, alu, 0.0, base, cm), [a], [out], 0.2 + cost(a, 2))
+    def pick(out, a, pattern, alu, base, cm, c=0.0):
+        op("g", lambda e: e.affine_select(ap(out), ap(a), pattern, alu, c, base, cm), [a], [out], 0.17 + size(a) * 2 * cy)
 
-    def mm(out, lhs, x, rhs, start, stop, k=1):
-        n = out[2] - out[1]
-        op("p", lambda e: e.matmul(ap(out), ap(lhs), rhs, start, stop), [x, lhs], [out], 0.01 + max(64, n) * k * CY / 2)
+    def mm(out, lhs, x, start, stop, k=1):
+        op("p", lambda e: e.matmul(ap(out), ap(lhs), ap(x), start, stop), [x[:3], lhs], [out], 0.015 + max(64, size(out)) * k * cy * 0.53)
+
+    def mat(name, s):
+        return ((name + "b", 0, 128), 1) if s == "s0" else ((name + "f", 0, 128), 4)
 
     LA, LB, LP = ("lst", 0, 16), ("lst", 16, 32), ("lst", 32, 48)
 
@@ -370,38 +451,67 @@ def build(core, T, topo):
     n0 = len(cuts0) - 1
     for k in range(n0):
         a, b = cuts0[k], cuts0[k + 1]
-        dma("s", T.s0[:, PB + a:PB + b], T.sp[:, a:b], [], [("s0", PB + a, PB + b)], "ld%d" % k, (b - a) / 4)
-    dma("a", T.iti[:], T.itg[:], [], [("iti", 0, 1024)], "ldi", 512)
-    dma("a", T.roti[:], T.rot[:], [], [("roti", 0, 256)], "ldr", 128)
+        dma("sa"[k % 2], T.s0[:, PB + a:PB + b], T.sp[:, a:b], [], [("s0", PB + a, PB + b)], "ld%d" % k, (b - a) / 4)
+    dma("s", T.iti[:, 0:256], T.itg[:, 0:256], [], [("iti", 0, 256)], "ldi0", 128)
+    dma("s", T.roti[:], T.rot[:], [], [("roti", 0, 256)], "ldr", 128)
+    dma("s", T.iti[:, 256:1024], T.itg[:, 256:1024], [("s0", PB, PB + W)], [("iti", 256, 1024)], "ldi1", 384)
     for c in range(16):
-        dma("s", T.hopi[c::16, :], T.hop[:], [], [("hopi%d" % c, 0, 4)], "ldh", 1)
+        dma("s", T.hopi[c::16, :], T.hop[:], [("iti", 0, 256)], [("hopi%d" % c, 0, 4)], "ldh", 1)
 
-    fill(("one", 0, 128), 1.0)
+    fill(("nil", 0, 128), 0.0)
     fill(("s0", 0, PB), 0.0)
     fill(("s0", PB + W, 2 * PB + W), 0.0)
-    fill(("em", 0, 144), 0.0)
-    pick(("idb", 0, 128), ("one", 0, 128), [[-1, 128]], A.is_equal, 0, 1)
-    pick(("idf", 0, 128), ("one", 0, 128), [[-1, 128]], A.is_equal, 0, 1)
-    fill(("neg", 0, 128), -1.0)
-    pick(("ndb", 0, 128), ("neg", 0, 128), [[-1, 128]], A.is_equal, 0, 1)
-    pick(("ndf", 0, 128), ("neg", 0, 128), [[-1, 128]], A.is_equal, 0, 1)
+
+    def diag(out, c):
+        pick(out, ("nil", 0, 128), [[-1, 128]], A.not_equal, 0, 1, c)
+
+    def const(out, c):
+        pick(out, ("nil", 0, size(out)), [[0, size(out)]], A.not_equal, 0, 0, c)
+
+    diag(("idb", 0, 128), 1.0)
+    act(("dnb", 0, 128), ("idb", 0, 128), scale=-4096.0)
+    act(("hfb", 0, 128), ("idb", 0, 128), scale=2048.0)
+    if "W" in CFG["route0"].upper():
+        act(("upb", 0, 128), ("idb", 0, 128), scale=4096.0)
+    lag[0] = 400
+    fill(("one", 0, 8), 1.0)
+    fill(("one", 8, 16), -BIG)
+    fill(("ea", 0, 144), 0.0)
+    fill(("er", 0, 144), 0.0)
+    fill(("cb", 0, 256), -3 * BIG)
     iota(("c1", 0, 48), [[0, 48]], 0, 1)
     iota(("c2", 0, 16), [[0, 16]], 0, 1)
     iota(("c2", 16, 32), [[1, 16]], 0, 0)
     iota(("c3", 0, 16), [[1, 16]], 0, 0)
     iota(("c3", 16, 32), [[16, 16]], 0, 0)
-    pick(("e8", 16, 24), ("one", 0, 8), [[-16, 8]], A.is_ge, 0, 1)
-    pick(("em", 0, 144), ("e8", 16, 24), [[16, 8]], A.is_ge, 15, -1, T.em[:, 15:143:16])
+    for kp in ("kp2", "kp", "kp3"):
+        const((kp, 0, 16), 0.0)
+        const((kp, 272, 288), 0.0)
+        lag[0] = 600
+    lag[0] = 450
+    pick(("e8", 16, 24), ("one", 8, 16), [[-16, 8]], A.is_ge, 0, 1)
+    pick(("ea", 15, 143, 16), ("e8", 16, 24), [[16, 8]], A.is_ge, 15, -1)
+    const(("vt", 0, 1), -1.0)
     pick(("e8", 0, 8), ("one", 0, 8), [[-16, 8]], A.is_equal, 0, 1)
     pick(("e8", 8, 16), ("one", 0, 8), [[-16, 8]], A.is_equal, -15, 1)
-    iota(("mci", 0, 256), [[16, 256]], -6143, 0)
     iota(("kl", 1, 256), [[0, 255]], 8192, 0, True)
     iota(("kr", 1, 256), [[0, 255]], 8192, 0, True)
-    for k in range(4):
-        op("v", lambda e, k=k: e.memset(T.rw[:, X * k:X * k + X], 0.0), [], [("rw", X * k, X * k + X), ("rwl", X * k, X * k + X)], 0.6)
+    const(("st", 0, 32), float(2 ** 21))
+    const(("yy", 0, 64), NONE)
+    const(("st", 16, 17), BIG)
+    act(("ev", 0, 144), ("ea", 0, 144), scale=2.0)
+    lag[0] = 600
+    iota(("mc", 0, 256), [[16, 256]], -6143, 0, True)
+    const(("cm", 0, QX), W * RND)
+    for name, c in (("dnf", -4096.0), ("upf", 4096.0), ("idf", 1.0), ("hff", 2048.0)):
+        diag((name, 0, 128), c)
+    diag(("idf", 128, 256), 1.0)
+    for s in ("sa", "sb"):
+        const((s, 0, PF), 0.0)
+        const((s, PF + W, 2 * PF + W), 0.0)
+    lag[0] = 400
     ts(("c4", 0, 32), ("c1", 0, 32), 4, A.arith_shift_right)
     ts(("c1", 0, 32), ("c1", 0, 32), 15, A.bitwise_and)
-    fill(("vt", 0, 1), 1.0)
     tt(("c2", 0, 32), ("c2", 0, 32), ("c4", 0, 32), A.add)
     tt(("c3", 16, 32), ("c3", 16, 32), ("c1", 16, 32), A.add)
     ts(("c4", 32, 48), ("c1", 0, 16), 16.0, A.mult)
@@ -412,113 +522,125 @@ def build(core, T, topo):
     cp(("col", 0, 1), ("c1", 0, 1))
     tt(("c2", 0, 32), ("c2", 0, 32), ("c3", 0, 32), A.add)
     cp(("lst", 0, 32), ("c2", 0, 32))
-    for kp in ("kp", "kp2", "kp3"):
-        fill((kp, 0, 16), 0.0)
-        fill((kp, 272, 288), 0.0)
-    ts(("mc", 0, 256), ("mci", 0, 256), T.col[:, 0:1], A.add, col=("col", 0, 1))
-    op("v", lambda e: e.tensor_reduce(T.kl[:, 0:1], T.e8[:, 0:8], AX.X, A.add), [("e8", 0, 8)], [("kl", 0, 1)], 0.12)
-    op("v", lambda e: e.tensor_reduce(T.kr[:, 0:1], T.e8[:, 8:16], AX.X, A.add), [("e8", 8, 16)], [("kr", 0, 1)], 0.12)
-    fill(("st", 0, 32), float(2 ** 21))
-    fill(("yy", 0, 64), NONE)
-    ts(("kl", 0, 1), ("kl", 0, 1), BIG, A.mult, 8192.0, A.add)
-    ts(("kr", 0, 1), ("kr", 0, 1), BIG, A.mult, 8192.0, A.add)
-    fill(("st", 16, 17), BIG)
-    for s in ("sa", "sb"):
-        fill((s, 0, PF), 0.0)
-        fill((s, PF + W, 2 * PF + W), 0.0)
-    op("v", lambda e: e.tensor_copy(T.hopf[:], T.hopi[:]), [("hopi%d" % c, 0, 4) for c in range(16)], [("hopf", 0, 4)], 0.12)
-    for t in range(FR):
+    lag[0] = 600
+    act(("mc", 0, 256), ("mc", 0, 256), F.Identity, ("col", 0, 1), bias=T.col[:, 0:1])
+    tt(("er", 15, 143, 16), ("e8", 0, 8), ("e8", 8, 16), A.add)
+    for k, a in (("kl", 0), ("kr", 8)):
+        act(("e8", 24, 32), ("e8", a, a + 8), F.Identity, scale=BIG, bias=1024.0, accum_out=T[k][:, 0:1])
+        ops[-1]["w"].append((k, 0, 1))
+    op("v", lambda e: e.tensor_scalar(T.hopf[:], T.hopi[:], -1.0 / W, None, A.mult), [("hopi%d" % c, 0, 4) for c in range(16)], [("hopf", 0, 4)], 0.12)
+
+    def targets(t, *after):
         cp(("it16", 256 * t, 256 * t + 256), ("iti", 256 * t, 256 * t + 256))
-
-    def targets(t):
+        ops[-1]["after"] = after
         gat("v", ("kp2", 16, 272), ("iti", 256 * t, 256 * t + 256), LP)
+        ops[-1]["after"] = after
         turn("kp2", "tw2")
-        gat("a", ("el", 256 * t, 256 * t + 256), ("tw2", 0, 544), LB, -1.0, float(4095 - 2 ** 24))
+        gat("a", ("el", 256 * t, 256 * t + 256), ("tw2", 0, 544), LB, F.Identity, scale=-1.0, bias=float(4095 - 2 ** 24))
 
-    def rows():
-        dma("s", T.rw[0::16, :], T.hl[:, 0:256], [("hl", 0, 256)], [("rw", 0, W)], "rwd", 100)
-        dma("s", T.rw[4::16, :], T.hl[:, 256:512], [("hl", 256, 512)], [("rwl", 0, W)], "rwd", 100)
-
-    def to_psum(out, x, by):
-        if by.isupper():
-            acp(out, x)
-            return
-        for a in range(out[1], out[2], 512):
-            b = min(out[2], a + 512)
-            y = (x[0], x[1] + a - out[1], x[1] + b - out[1])
-            mm((out[0], a, b), ("idb" if x[0] == "s0" else "idf", 0, 128), y, ap(y), True, True, 1 if x[0] == "s0" else 4)
+    def rows(rw):
+        buf, a, b = rw
+        dma("s", T[buf][0::16, a:b], T.hl[:, 0:256], [("hl", 0, 256)], [(buf, a, b, 2)], "rwd", 100)
+        dma("s", T[buf][15::16, a:b], T.hl[:, 256:512], [("hl", 256, 512)], [(buf, a + 1, b, 2)], "rwd", 100)
 
     turnno = [0, 0, 0]
 
-    def piece_v(s, pad, v0, v1, by):
-        k = turnno[0] % 2
-        turnno[0] += 1
-        p, a, n = "p%d" % k, "a%d" % k, v1 - v0
-        z = 1 if v0 == 0 else 0
-        to_psum((p, 0, n + 3), (s, pad + v0 - 2, pad + v1 + 1), by)
-        tt((p, 0, n + 3), (p, 0, n + 3), (s, pad + v0 - 1, pad + v1 + 2), A.max)
-        acp((a, 0, n + 3), (p, 0, n + 3))
-        if by in "Vv":
-            tt((p, 0, n), (p, 0, n), (a, 3, n + 3), A.max)
-            tt(("vt", v0 + z, v1), (s, pad + v0 + z, pad + v1), (p, z, n), A.is_ge)
-        else:
-            buf = ("h%d" if s == "s0" else "b%d") % k
-            tt((buf, 0, n), (p, 0, n), (a, 3, n + 3), A.max)
-            compare(s, pad, v0, v1, buf, v0, "G")
+    def bank(n):
+        o = 512 * (turnno[1] % 2)
+        turnno[1] += 1
+        return ("pd", o, o + n)
 
-    def fold_out(s, pad, v0, v1, k):
-        buf = "bh" if s == "s0" else "bb"
-        who = turns[k % len(turns)]
-        rid, pid, _ = topo.addr(who)
-        kb = (v1 - v0) / (4 if s == "s0" else 2)
-        x = RemoteDMATransfer(dst_ids=[DstId(rid=rid, pnc=pid)], dma_engine_mask=topo.mask(core, who), remote_sem=T.sem["fa%d" % k],
-                              srcs=[T[s][:, pad + v0 + h:pad + v1 + h] for h in (-2, -1, 1, 2)], dsts=[T[buf][:, v0:v1]], alu_op=2)
-        i = op("g", lambda e: e.remote_dma_fused([x], local_sem=T.sem["fl%d" % k]), [(s, pad + v0 - 2, pad + v1 + 2), (buf + "w", v0, v1)], [],
-               1.0, "fl%d" % k, len(topo.engines(core, who)), 1.5, 4 * kb / 300, fold=(who, k, buf, v0, v1))
-        op(None, None, [], [(buf, v0, v1)], 0.0, "fb%d" % k, len(topo.engines(who, core)), 3.5 + kb / 300, after=(i,))
-
-    def compare(s, pad, v0, v1, buf, at, by):
+    def judge(s, pad, v0, v1, terms, by="G"):
         parts = (v1 - v0 + 511) // 512
         for h in range(parts):
-            a, b = v0 + (v1 - v0) * h // parts, v0 + (v1 - v0) * (h + 1) // parts
-            a = max(a, 1)
-            o = 512 * (turnno[1] % 2)
-            turnno[1] += 1
-            p, x, y = ("p2", o, o + b - a), (s, pad + a, pad + b), (buf, a - at, b - at)
-            if by == "G":
-                kind, k = ("b", 1) if s == "s0" else ("f", 4)
-                mm(p, ("id" + kind, 0, 128), x, ap(x), True, False, k)
-                mm(p, ("nd" + kind, 0, 128), y, ap(y), False, True, k)
-                ops[-1]["w"].append((buf + "w", a, b))
-                op("a", lambda e, p=p, a=a, b=b: e.activation(T.vt[:, a:b], ap(p), F.Sigmoid, bias=512.0, scale=float(2 ** 40)),
-                   [p], [("vt", a, b)], cost(p))
-            else:
-                to_psum(p, x, by)
-                tt(("vt", a, b), p, y, A.is_ge)
-                ops[-1]["w"].append((buf + "w", a, b))
+            a, b = max(1, v0 + (v1 - v0) * h // parts), v0 + (v1 - v0) * (h + 1) // parts
+            p = bank(b - a)
+            if by == "F":
+                act(p, ("bb", a - BB, b - BB))
+                ops[-1]["w"].append(("bbw", a, b))
+                tt(("vt", a, b), p, (s, pad + a, pad + b), A.subtract)
+                continue
+            step = b - a if s == "s0" else CFG["jc"]
+            lag[0] += CFG["jl"]
+            for c in range(a, b, step):
+                for j, (name, buf, at) in enumerate([("dn", s, -pad)] + terms):
+                    lhs, k = mat(name, s)
+                    mm((p[0], p[1] + c - a, p[1] + min(b, c + step) - a), lhs, (buf, c - at, min(b, c + step) - at), j == 0, j == len(terms), k)
+            lag[0] -= CFG["jl"]
+            if terms[0][1] == "bb":
+                ops[-1]["w"].append(("bbw", a, b))
+            act(("vt", a, b), p)
 
-    def all_votes(s, pad, pcs, route, make):
-        for k, (v0, v1) in enumerate(pcs):
-            make(k)
-            if route[k] in "FfG":
-                fold_out(s, pad, v0, v1, k)
-            else:
-                piece_v(s, pad, v0, v1, route[k])
-        for k, (v0, v1) in enumerate(pcs):
-            if route[k] in "FfG":
-                compare(s, pad, v0, v1, "bh" if s == "s0" else "bb", 0, route[k])
+    def piece(s, pad, v0, v1, by):
+        k = turnno[0] % 2
+        turnno[0] += 1
+        p, h, n = "pe%d" % k, (v1 - v0) // 2, v1 - v0
+        j = (turnno[0] - 1) % 4
+        u = "h%d" % k if s == "s0" and by not in "YZyz" else "b%d" % j
+        lhs, c = mat("id", s)
+        lo, hi = pad + v0, pad + v1
+        if by.islower():
+            act((p, 0, h + 2), (s, lo - 2, hi + 2, 2))
+        else:
+            mm((p, 0, h + 2), lhs, (s, lo - 2, hi + 2, 2), True, True, c)
+        by = by.upper()
 
-    vc = [0] + [c - 2 for c in cuts0[1:n0]] + [W]
+        def add(at):
+            op("g", lambda e: e.dma_start(T.vt[:, v0:v1], T[u][:, at:at + n], accum_op=A.add).then_inc(T.sem["zd%d" % j], 16),
+               [(u, at, at + n)], [("vt", v0, v1)], 1.0 + once("g") / 3, "zd%d" % j, 16, CFG["add"], n / 600)
+
+        if by in "YZ":
+            act(("vt", v0, v1), (s, lo, hi), scale=-2.0 if by == "Y" else -1.0)
+        if by in "XY":
+            tt((p, 0, h + 2), (p, 0, h + 2), (s, lo - 1, hi + 2, 2), A.max)
+            tt((u, 0, n + 2, 2), (p, 0, h + 1), (s, lo, hi + 1, 2), A.max)
+            tt((u, 1, n + 2, 2), (p, 1, h + 2), (s, lo - 1, hi, 2), A.max)
+            if by == "X":
+                judge(s, pad, v0, v1, [("hf", u, v0), ("hf", u, v0 - 2)])
+            else:
+                add(0)
+                add(2)
+            return
+        b, m = "a%d" % k, "pm" if by == "V" else u
+        a = ("pm", 512 * k, 512 * k + h) if by != "V" else ("pm", 1024 - h, 1024) if n + h <= 1024 else (p, 2, h + 2)
+        tt((b, 0, h + 1), (p, 0, h + 1), (s, lo + 1, hi + 2, 2), A.max)
+        tt(a, (p, 2, h + 2), (s, lo - 1, hi - 1, 2), A.max)
+        tt((m, 0, n, 2), a, (b, 0, h), A.max)
+        tt((m, 1, n, 2), a, (b, 1, h + 1), A.max)
+        if by == "V":
+            z = 1 if v0 == 0 else 0
+            tt(("vt", v0 + z, v1), (m, z, n), (s, lo + z, hi), A.subtract)
+        elif by == "Z":
+            add(0)
+        else:
+            judge(s, pad, v0, v1, [("up", u, v0)])
+
+    def fold_out(s, pad, v0, v1, k):
+        who = turns[k % len(turns)]
+        rid, pid, _ = topo.addr(who)
+        kb = (v1 - v0) / 2
+        x = RemoteDMATransfer(dst_ids=[DstId(rid=rid, pnc=pid)], dma_engine_mask=topo.mask(core, who), remote_sem=T.sem["fa%d" % k],
+                              srcs=[T[s][:, pad + v0 + h:pad + v1 + h] for h in (-2, -1, 1, 2)], dsts=[T.bb[:, v0 - BB:v1 - BB]], alu_op=2)
+        i = op("g", lambda e: e.remote_dma_fused([x], local_sem=T.sem["fl%d" % k]), [(s, pad + v0 - 2, pad + v1 + 2), ("bbw", v0, v1)], [],
+               1.0, "fl%d" % k, len(topo.engines(core, who)), 1.0, 4 * kb / 500, fold=(who, k, v0, v1))
+        op(None, None, [], [("bb", v0 - BB, v1 - BB)], 0.0, "fb%d" % k, len(topo.engines(who, core)), CFG["back"] + kb / 500 + once(who), after=(i,))
+
+    vc = [0] + [c - 4 for c in cuts0[1:n0]] + [W]
+    lag[0] = 0
+    for k in range(n0):
+        piece("s0", PB, vc[k], vc[k + 1], CFG["route0"][k])
+    lag[0] = 400
     targets(0)
-    cp(("hl", 0, 256), ("roti", 0, 256))
-    tt(("hl", 256, 512), ("roti", 0, 256), ("hl", 0, 256), A.subtract)
-    rows()
-    all_votes("s0", PB, [(vc[k], vc[k + 1]) for k in range(n0)], CFG["route0"], lambda k: None)
+    lag[0] = 1000
+    cp(("pr", 0, 256), ("roti", 0, 256))
+    act(("hl", 0, 256), ("pr", 0, 256))
+    tt(("hl", 256, 512), ("pr", 0, 256), ("hl", 0, 256), A.subtract)
 
-    def records(k):
-        dma("s", T.cw[:, k * W:k * W + W], T.rec[:], [("vt", 0, W)], [("cw", k * W, k * W + W)], "ldc%d" % k, 1024)
+    def records(k, after):
+        dma("s", T.cw[:, k * W:k * W + W], T.rec[:], [after], [("cw", k * W, k * W + W)], "ldc%d" % k, 1024)
 
-    records(0)
+    for k in range(3):
+        records(k, ("iti", 256, 1024))
 
     def frame(t):
         last = t == FR - 1
@@ -526,25 +648,53 @@ def build(core, T, topo):
         new = ("sa", "sb")[t % 2]
         lq = "lq%d" % t
         win = (old, opad, opad + W)
+        rw = ("s0", PB, PB + W) if t else ("gv", 0, W)
+        up = float(W * (t // 2 + 1))
+        kept = []
 
-        def votes(q, b0, b1):
-            gat(q, ("gv", 256 * b0, 256 * b1), ("vt", 0, W), ("it16", 256 * t + 16 * b0, 256 * t + 16 * b1), -BIG, BIG * 13 / 32)
-
-        records(t + 1)
+        if t in (1, 2):
+            records(t + 2, ("vt", 0, W))
+        act(("hd", 0, 128), ("upf", 0, 128), F.Identity, ("hopf", 0, 4), scale=T.hopf[:, t:t + 1])
+        if last:
+            r0 = 16 * t
+            dma("s", T.cr[0:128 - r0, :], T.rec[r0:128, :], [("vt", 0, W)], [("cr", 0, W, 2)], "ldq", 600)
+            dma("s", T.cr[128 - r0:128, :], T.rec[0:r0, :], [("vt", 0, W)], [("cr", 1, W, 2)], "ldq", 400)
         if t:
-            gat("a", ("kp3", 16, 272), ("lq%d" % (t - 1), X, X + 256), LP)
+            gat("a", ("kp3", 16, 272), ("qf", 0, 256), LP)
             turn("kp3", "tw3")
-            gat("a", ("hl", 0, 256), ("tw3", 0, 544), LB)
-            gtt(("hl", 256, 512), ("tw3", 0, 544), LB, ("hl", 0, 256), A.subtract)
-            rows()
-        for q, b0, b1 in CFG["xs"]:
-            votes(q, b0, b1)
+            if CFG["hold"]:
+                for o in ops[-2:]:
+                    o["r"].append(("vt", 0, X))
+            if CFG["lo"] == "v":
+                gat("a", ("hl", 0, 256), ("tw3", 0, 544), LB)
+                gtt(("hl", 256, 512), ("tw3", 0, 544), LB, ("hl", 0, 256), A.subtract)
+            else:
+                gat("a", ("qb", 0, 256), ("tw3", 0, 544), LB)
+                act(("hl", 0, 256), ("qb", 0, 256))
+                mm(("pr", 0, 256), ("upf", 0, 128), ("qb", 0, 256), True, False, 4)
+                mm(("pr", 0, 256), ("dnb", 0, 128), ("hl", 0, 256), False, True)
+                act(("hl", 256, 512), ("pr", 0, 256), scale=1.0 / W)
+            rows(rw)
+        if CFG["dr"] == "v":
+            act(("elr", 0, 256), ("el", 256 * t, 256 * t + 256), F.Identity, bias=4096.0)
+        mm(("pc", 0, 256), ("idb", 0, 128), ("cb", 0, 256), True, False)
+        for b0, b1 in zip(CFG["xs"], CFG["xs"][1:]):
+            i = len(ops)
+            gat("x", ("gv", 256 * b0, 256 * b1), ("vt", 0, W), ("it16", 256 * t + 16 * b0, 256 * t + 16 * b1), F.Sign, scale=-1.0, bias=2.0 ** -32)
             for b in range(b0, b1):
-                x = ("gv", 256 * b, 256 * b + 256)
-                mm(("pc", 0, 256), ("em", 15 - b, 143 - b), x, ap(x), b == 0, b == 15)
+                op("p", lambda e, i=i, b=b: e.matmul(T.pc[:, 0:256], T["e" + ops[i]["q"]][:, 15 - b:143 - b], T.gv[:, 256 * b:256 * b + 256], False, b == 15),
+                   [("gv", 256 * b, 256 * b + 256), ("ea", 0, 144), ("ev", 0, 144)], [("pc", 0, 256)], 0.015 + 136 * cy)
+        if not t:
+            rows(rw)
 
         tt(("dl", 0, 256), ("pc", 0, 256), ("el", 256 * t, 256 * t + 256), A.max)
-        acp(("dr", 0, 256), ("dl", 0, 256), 4096.0)
+        counted = len(ops) - 1
+        if CFG["dr"] == "a":
+            act(("dr", 0, 256), ("dl", 0, 256), F.Identity, bias=4096.0)
+        else:
+            tt(("dr", 0, 256), ("pc", 0, 256), ("elr", 0, 256), A.max)
+        if not last and CFG["tn"] == "c":
+            targets(t + 1, counted)
         scan(("fg", 0, 256), ("kl", 0, 256), ("dl", 0, 256), NONE)
         scan(("fg", 256, 512), ("kr", 0, 256), ("dr", 0, 256), NONE, True)
         tr(("xe", 0, 32), ("fg", 240, 272))
@@ -553,98 +703,191 @@ def build(core, T, topo):
         tr(("zz", 0, 64), ("yy", 0, 64))
         scan(("fg", 0, 256), ("kl", 0, 256), ("dl", 0, 256), ("zz", 15, 16))
         scan(("pc", 256, 512), ("kr", 0, 256), ("dr", 0, 256), ("zz", 48, 49), True)
-        tt(("kp", 16, 272), ("fg", 0, 256), ("pc", 256, 512), A.min)
-        turn("kp", "tw")
-        dc = CFG["dcl" if last else "dc"]
-        for a, b in zip(dc[1:], dc):
-            z = ("p2", a, b)
-            gat("v", ("ki", a, b), ("tw", 0, 544), ("lst", a // 16, b // 16))
+        for a in range(0, 256, CFG["dc"]):
+            b = a + CFG["dc"]
+            z = ("pc", a, b)
+            tt(("ki", a, b), ("fg", a, b), ("pc", 256 + a, 256 + b), A.min)
             ts(("pay", a, b), ("ki", a, b), 8191, A.bitwise_and)
             ts(("dd", a, b), ("ki", a, b), 12, A.arith_shift_right, -2, A.bitwise_and)
             ts(z, ("pay", a, b), 4096.0, A.is_lt, 0.5, A.subtract)
             tt(z, z, ("dd", a, b), A.mult)
-            tt(z, z, ("pay", a, b), A.subtract)
-            ts(("src", a, b), z, 6143.0, A.add, 4095.0, A.min)
-            tt(("hw", a, b), ("mc", a, b), z, A.subtract)
-            ts(("qi", a, b), ("hw", a, b), T.hopf[:, t:t + 1], A.mult, col=("hopf", 0, 4))
-            ts(("qi", a, b), ("qi", a, b), W - 1, A.bitwise_and)
-            cp(("hh", a, b), ("qi", a, b))
+            tt(("kp", 16 + a, 16 + b), z, ("pay", a, b), A.subtract)
+            tr(("tw", a, b), ("kp", 16 + a, 16 + b))
+            e = b if b < 256 else 288
+            tr(("tw", 256 + a, 256 + e), ("kp", a, e))
 
-        def rot_of(q, ps, m0, m1):
-            a, b = m0 // 16, m1 // 16
-            gat(q, ("rg", m0, m1), ("rw", 0, W), ("src", a, b), also=[("rwl", 0, W)] + ([("hh", a, b)] if q == "v" and CFG["hfirst"] else []))
-            for r in range(16):
-                mm((ps, 0, b - a), ("em", 15 - r, 143 - r), ("rg", m0, m1), T.rg[:, m0 + r:m1:16], r == 0, False)
-            mm((ps, 0, b - a), ("idf", 0, 128), ("hh", a, b), T.hh[:, a:b], False, True, 4)
-            if m0 >= W - X:
-                cp(("xo", X, XW), (ps, 0, b - a))
+        def source(a, b):
+            gts(("src", a, b), ("tw", 0, 544), ("lst", a // 16, b // 16), 6143.0, A.add, 4095.0, A.min)
+
+        def phase(a, b):
+            gtt(("hw", a, b), ("tw", 0, 544), ("lst", a // 16, b // 16), ("mc", a, b), A.subtract)
+            if CFG["kq"][a == 0] == "a":
+                act(("kk", a, b), ("hw", a, b), F.Identity, ("hopf", 0, 4), scale=T.hopf[:, t:t + 1], bias=RND)
             else:
-                cp(("q16", 64 + a, 64 + b), (ps, 0, b - a))
-                if not last:
-                    acp((lq, XW + a, XW + b), (ps, 0, b - a))
+                ts(("kk", a, b), ("hw", a, b), T.hopf[:, t:t + 1], A.mult, RND, A.add, ("hopf", 0, 4))
 
-        def t_gather(q, m0, m1):
-            out = ("xo", m0 - (W - X), m1 - (W - X)) if m0 >= W - X else ("tb", m0, m1)
-            gat(q, out, win, ("src", m0 // 16, m1 // 16))
+        def r_gather(m0, m1, now=False, q="x"):
+            gat(q, ("rg", m0, m1), rw, ("src", m0 // 16, m1 // 16), now=now)
 
-        def product(n0, n1):
-            gtt((new, PF + n0, PF + n1), ("cw", 0, (t + 2) * W), ("q16", n0 // 16, n1 // 16), (lq, n0, n1) if n0 < X else ("tb", n0 - X, n1 - X), A.mult)
+        def rot_of(ps, m0, m1):
+            a, b = m0 // 16, m1 // 16
+            p = (ps, 256 + a, 256 + b)
+            mm(p, ("dnf", 0, 128), ("kk", a, b), True, False, 4)
+            mm(p, ("idb", 0, 128), ("cm", 0, b - a), False, False)
+            mm(p, ("hd", 0, 128), ("hw", a, b), False, False, 4)
+            for r in range(16):
+                mm(p, ("er", 15 - r, 143 - r), ("rg", m0 + r, m1, 16), False, r == 15)
+                ops[-1]["r"][0] = ("rg", m0, m1)
+            if m0 >= W - X and last:
+                ts(("qi", 0, QX), p, up, A.add)
+                ts(("qi", 0, QX), ("qi", 0, QX), W - 1, A.bitwise_and)
+                cp(("xo", HX, HX + QX), ("qi", 0, QX))
+            elif m0 >= W - X:
+                cp(("xo", HX, HX + QX), p)
+            else:
+                ts(("q16", QX + a, QX + b), p, up, A.add)
+                kept.append((("qf", QX + a, QX + b), p))
 
-        def send():
-            twice = 2 if t else 1
-            for k, (a, b, w) in enumerate(PARTS):
-                who = ports[w]
-                rid, pid, _ = topo.addr(who)
-                x = RemoteDMATransfer(dst_ids=[DstId(rid=rid, pnc=pid)] * twice, dma_engine_mask=topo.mask(core, who),
-                                      remote_sem=T.sem["xa%d_%d" % (t, k)], srcs=[T.xo[:, a:b]],
-                                      dsts=[T["hx%d_%d" % (t, k)][128 * j:128 * j + 128, :] for j in range(twice)])
-                i = op("g", lambda e, x=x, k=k: e.remote_dma_fused([x], local_sem=T.sem["sx%d" % k]), [("xo", a, b)], [],
-                       1.0, "sx%d" % k, len(topo.engines(core, who)), 1.5, twice * (b - a) / 600)
-                op(None, None, [], [(lq, a, b)], 0.0, "arr%d_%d" % (t, k), n_in[w], 8.0, after=(i,))
-            cp(("q16", 0, 64), (lq, X, XW))
+        def t_gather(m0, m1, now=False, q="x"):
+            at = 0 if m0 < W - X else W - X if m0 < W - HX else W - XW
+            gat(q, ("xo" if at else "tb", m0 - at, m1 - at), win, ("src", m0 // 16, m1 // 16), now=now)
 
-        def t_top(q):
-            t_gather(q, W - 512, W)
-            t_gather(q, W - X, W - 512)
+        def product(n0, n1, by="v"):
+            x = ("tb", n0 - X, n1 - X) if n0 >= X else (lq, n0, n1) if n0 < HX else (lq, n0 + QX, n1 + QX)
+            c = ("cr", 0, W) if last and n0 < X else ("cw", 0, (t // 2 * 2 + 3) * W)
+            off, out, n = ("q16", n0 // 16, n1 // 16), (new, PF + n0, PF + n1), n1 - n0
+            if by == "v":
+                gtt(out, c, off, x, A.mult)
+                return
+            h = "h%d" % (turnno[2] % 2)
+            turnno[2] += 1
+            gat("a", (h, 0, n), c, off)
+            parts = (n + 511) // 512
+            for j in range(parts):
+                a, b = n * j // parts, n * (j + 1) // parts
+                p = bank(b - a)
+                mm(p, ("idb", 0, 128), (h, a, b), True, True)
+                tt((new, out[1] + a, out[1] + b), (x[0], x[1] + a, x[1] + b), p, A.mult)
 
-        top = (W - X, W)
+        def send(k):
+            a, b = PARTS[k]
+            who = senders(t, core, nxt, T, topo)[k]
+            to = nxt if who == core else who
+            rid, pid, _ = topo.addr(to)
+            r0 = 16 * turned(t) if who == core else 0
+            land = ("lu%d" % t, 0, b - a) if r0 else (lq, a, b)
+            if who == core:
+                dsts, sem = [ap(land)], "arr%d_%d" % (t, k)
+            else:
+                dsts, sem = [T["hx%d_%d" % (t, k)][128 * j:128 * j + 128, :] for j in range(2 if turned(t) else 1)], "xa%d_%d" % (t, k)
+            x = RemoteDMATransfer(dst_ids=[DstId(rid=rid, pnc=pid)] * len(dsts), dma_engine_mask=topo.mask(core, to),
+                                  remote_sem=T.sem[sem], srcs=[T.xo[:, a:b]], dsts=dsts)
+            i = op("g", lambda e: e.remote_dma_fused([x], local_sem=T.sem["sx%d" % k]), [("xo", a, b)], [],
+                   1.0 + once(core), "sx%d" % k, len(topo.engines(core, to)), 1.0, len(dsts) * (b - a) / (300 if who == core else 1000))
+            op(None, None, [], [land], 0.0, "arr%d_%d" % (t, k), len(topo.engines(senders(t, prv, core, T, topo)[k], core)),
+               CFG["far"] if who == core else CFG["arr"] + once(who), after=(i,))
+            if r0:
+                dma("s", T[lq][r0:128, a:b], T[land[0]][0:128 - r0, :], [land], [(lq, a, b, 2)], "trn", 250)
+                dma("s", T[lq][0:r0, a:b], T[land[0]][128 - r0:128, :], [land], [(lq, a + 1, b, 2)], "trn", 50)
+
+        def top_bins(now):
+            q = "xxxx" if now else CFG["top"]
+            t_gather(W - X, W - HX, now, q[0])
+            send(0)
+            r_gather(W - X, W - HX, now, q[1])
+            r_gather(W - HX, W, now, q[2])
+            t_gather(W - HX, W, now, q[3])
+            rot_of("pr", W - X, W)
+            send(1)
+
+        yc = CFG["yc"]
+        cut = (W - X if last else CFG["cut"]) // 16
+        source(cut, 256)
+        phase(cut, 256)
+        begun = len(ops) - 1
+        if last:
+            source(0, cut)
+            phase(0, cut)
+        got = (lq, HX, HX + QX)
         if not last:
-            rq, tq = CFG["rq"], CFG["tq"]
-            rot_of(rq[0], "pr", *top)
-            t_top(tq[0])
-            send()
-            rc, yc = CFG["rc"], CFG["yc"]
-            for k in range(len(rc) - 1):
-                rot_of(rq[k + 1], ("pc", "pr")[k % 2], rc[k + 1], rc[k])
-            targets(t + 1)
-
-            def make(k):
-                if yc[k + 1] >= X:
-                    t_gather(tq[k + 1], yc[k + 1] - X, yc[k] - X)
-                product(yc[k + 1], yc[k])
-
-            vc = [W] + [c + 2 for c in yc[1:-1]] + [0]
-            all_votes(new, PF, [(vc[k + 1], vc[k]) for k in range(len(yc) - 1)], CFG["route"], make)
+            vc = [W] + [c + 4 for c in CFG["vc"]] + [0]
+            route = CFG["route"][t]
+            for step in CFG["steps"].split():
+                k = int(step[1:] or 0)
+                if step == "t":
+                    top_bins(CFG["now"])
+                elif step == "s":
+                    source(0, cut)
+                elif step == "h":
+                    phase(0, cut)
+                elif step == "n":
+                    if CFG["tn"] != "c":
+                        targets(t + 1, begun)
+                elif step == "q":
+                    ts(("q16", 0, QX), got, up, A.add)
+                    act(("qf", 0, QX), got)
+                elif step == "c":
+                    for out, p in kept:
+                        act(out, p)
+                elif step[0] == "g":
+                    r_gather(yc[k + 1] - X, yc[k] - X, q=CFG["rq"][k])
+                    t_gather(yc[k + 1] - X, yc[k] - X, q=CFG["tq"][k])
+                    rot_of(("pc", "pr")[k % 2], yc[k + 1] - X, yc[k] - X)
+                elif step[0] == "p":
+                    product(yc[k + 1], yc[k], CFG["by"][k])
+                elif step[0] == "v" and route[k] in "FG":
+                    fold_out(new, PF, vc[k + 1], vc[k], k)
+                elif step[0] == "v":
+                    piece(new, PF, vc[k + 1], vc[k], route[k])
+                elif route[k] in "FG":
+                    judge(new, PF, vc[k + 1], vc[k], [("up", "bb", BB)], route[k])
         else:
+            r0 = 16 * t
+
+            def early(n0, ps, at):
+                mm((ps, n0 % X, n0 % X + HX), ("idf", at, at + 128), (new, PF + n0, PF + n0 + HX), True, True, 4)
+
             def store(n0, n1, ps, k):
                 y0, y1 = n0 % 2048, n0 % 2048 + n1 - n0
                 product(n0, n1)
-                tt(("bb", y0, y1), (new, PF + n0, PF + n1), (ps, y0 % X, y0 % X + n1 - n0), A.add)
-                dma("sa"[k % 2], T.y[:, y0:y1], T.bb[:, y0:y1], [("bb", y0, y1)], [("y", y0, y1)], "out%d" % k, (n1 - n0) / 2)
+                out = ("vt", y0, y1)
+                tt(out, (new, PF + n0, PF + n1), (ps, y0 % X, y0 % X + n1 - n0), A.add)
+                if n0 >= X:
+                    dma("s", T.y[:, y0:y1], T.vt[:, y0:y1], [out], [("y", y0, y1)], "out%d" % k, (n1 - n0) / 2)
+                else:
+                    dma("s", T.y[r0:128, y0:y1], T.vt[0:128 - r0, y0:y1], [out], [("y", y0, y1, 2)], "out%d" % k, (n1 - n0) / 4)
+                    dma("a", T.y[0:r0, y0:y1], T.vt[128 - r0:128, y0:y1], [out], [("y", y0 + 1, y1, 2)], "out%d" % k, (n1 - n0) / 4)
 
-            rot_of(CFG["lr"][0], "pr", *top)
-            t_top(CFG["lt"][0])
-            send()
-            for k in range(3):
-                rot_of(CFG["lr"][k + 1], ("pc", "pr")[k % 2], k * X, k * X + X)
-                t_gather(CFG["lt"][k + 1], k * X, k * X + X)
-                if k < 2:
-                    product(k * X + X, k * X + 2 * X)
-                    acp((("p1", "p0")[k], 0, X), (new, PF + k * X + X, PF + k * X + 2 * X))
-            store(3 * X, W, "p1", 0)
-            lc = CFG["lc"]
-            for k in range(len(lc) - 1):
-                store(lc[k + 1], lc[k], "p0", k + 1)
+            top_bins(True)
+            for j, a in enumerate(CFG["ls"]):
+                if a < 0:
+                    cp(("q16", 0, QX), got)
+                    for k, (n1, n0) in enumerate(zip(CFG["lc"], CFG["lc"][1:])):
+                        store(n0, n1, "pd", k)
+                    continue
+                for h in (a, a + HX):
+                    r_gather(h, h + HX)
+                for h in (a, a + HX):
+                    t_gather(h, h + HX)
+                rot_of(("pc", "pr")[j % 2], a, a + X)
+                x = (new, PF + a + X, PF + a + 2 * X)
+                if a == 2 * X and CFG["ya"] != "d":
+                    for k, (n1, n0) in enumerate(zip(CFG["ld"], CFG["ld"][1:])):
+                        store(3 * X + n0, 3 * X + n1, "pm", 4 + k)
+                    continue
+                for h in (a + X, a + X + HX):
+                    product(h, h + HX)
+                    if a == X:
+                        early(h, "pd", r0)
+                    elif CFG["ya"] == "v":
+                        early(h, "pm", 0)
+                    elif CFG["ya"] == "a":
+                        act(("pm", h % X, h % X + HX), (new, PF + h, PF + h + HX))
+                if CFG["ya"] == "d" and a == 0:
+                    dma("s", T.y[:, X:2 * X], ap(x), [x], [("y", X, 2 * X)], "out4", 512)
+                elif CFG["ya"] == "d" and a == 2 * X:
+                    op("g", lambda e, x=x: e.dma_start(T.y[:, X:2 * X], ap(x), accum_op=A.add).then_inc(T.sem.ya, 16),
+                       [x], [("y", X, 2 * X)], 1.0, "ya", 16, CFG["add"], 1.7)
 
     for t in range(FR):
         frame(t)

@@ -5,9 +5,9 @@ W = 4096
 X = 1024
 FR = 4
 PF, PB = 8, 16
-HX, QX = X // 2, X // 16
+HX, QX = 512, X // 16
 XW = X + QX
-PARTS = [(0, HX), (HX, XW)]
+PARTS = [(0, HX), (HX + QX, XW), (HX, HX + QX)]
 BIG = float(2 ** 27)
 NONE = float(2 ** 26)
 RND = 1.5 * 2 ** 23
@@ -15,25 +15,50 @@ BB = W // 2
 
 CFG = {
     "cuts0": [0, 896, 1536, 2304, 3200, W], "route0": "XwXWW",
-    "yc": [W, 3200, 2432, 1792, X, 512, 0], "vc": [3200, 2432, 1792, X, 512], "route": ["zzzwwv"] * 3, "by": "vvvvvv",
-    "now": False, "cut": 2048, "kq": "va", "lo": "a", "add": 3.0, "jc": 512, "jl": 0, "hold": 0, "ya": "a",
-    "top": "xxxx", "rq": "xxxax", "tq": "axxxx",
-    "steps": "g0 t s p0 h v0 g1 g2 n p1 v1 p2 g3 p3 v3 j0 q v2 c p4 p5 j1 v4 j2 v5 j3 j4 j5",
-    "ls": [0, 2 * X, X, -1], "ld": [X, 512, 256, 0], "lc": [X, 512, 256, 0], "eps": [0.05, 0.2, 0.35], "short": 0.05, "loose": 0,
-    "xs": [0, 2, 5, 8, 11, 13, 14, 15, 16],
-    "ways": [(0.25, 0.8, 1.0), (0.15, 1.3, 1.0), (0.25, 1.0, 1.5), (0.3, 1.3, 1.1)], "safe": 1.5, "dr": "v", "tn": "c", "dc": 128,
-    "cy": 0.00088, "lat": 0.25, "arr": 6.0, "far": 2.0, "back": 3.5, "once": 3.0, "turns": 3, "ga": 1.45,
+    "yc": [W, 3584, 3072, 2432, 1728, X, 512, 0], "route": ["ZZZZZwv"] * 3, "strict": 1,
+    "front": "r1 z a:g0 v:g1 C a:g2 v:g3 a:g4 v:g5 a:g6 r2 r3 d e r4 r5 c L t1 R t2 x y t3 w t4 F B t5 h D",
+    "cut": 2048, "ya": "p", "lo": "a", "add": 3.0, "jc": 512, "jl": 0,
+    "steps": "a:Rw S H v:Tb Xb a:r0 v:Ta K Qw Xa v:t0 q0 a:r1 a:t1 p0 e0 q1 a:r2 p1 a:t2 e1 m0 q2 a:r3 m1 a:t3 p2 e2 q3 p3 n0 f0 n1 f1 e3 m2 n2 f2 I m3 f3 p4 e4 c p5 e5 m4 f4 m5 f5",
+    "lp": [(2048, 2560), (2560, 3072), (3072, W), (X, 1536), (1536, 2048), (512, X), (256, 512), (0, 256)],
+    "last": "a:Rw S H v:Tb Xb a:r0 v:Ta K Qw Xa v:t0 q0 a:r1 a:t1 p0 q1 a:r2 p1 v:t2 y0 y1 q2 a:r3 a:t3 p2 y2 q3 a:r4 a:t4 p3 q4 y3 p4 y4 I p5 y5 p6 y6 p7 y7",
+    "eps": [0.05, 0.2, 0.35], "short": 0.05, "loose": 0, "tries": 2000, "heat": 0.3, "seed": 1,
+    "xs": [0, 2, 5, 8, 11, 13, 14, 15, 16], "xq": "xxxxxxxx", "kl": 0, "tl": 0, "ai": 0, "fw": "p",
+    "ways": [(0.15, 1.0, 1.0, 1.0, 1.0), (0.12, 1.4, 1.0, 0.95, 0.8), (0.25, 1.2, 1.3, 1.25, 1.2)], "safe": 1.5, "dr": "v", "dc": 128,
+    "cy": 0.00088, "lat": 0.25, "arr": 5.0, "far": 2.0, "back": 3.5, "once": 3.0, "turns": 3, "ga": 1.45, "fv": 0.045,
 }
+CFG.update(
+    xs=[0, 2, 4, 7, 10, 12, 14, 15, 16], lp=[(3584, W), (3072, 3584), (2048, 3072), (1536, 2048), (X, 1536), (512, X), (0, 512)],
+    yc=[W, 3584, 2688, 1696, X, 512, 0], route=["ZZZWwv"] * 3, far=1.2,
+    front="z A:g0 V:g1 C A:g2 V:g3 A:g4 V:g5 A:g6 V:g7 t2 r2 r3 t1 d e r4 r5 c L R t3 x y t4 w F B h t5 D",
+    steps="a:r0 v:k V:Tb Xb q0 A:t0 S H K o0 A:r1 q1 p0 e0 V:Ta A:t1 m0 o1 M0 A:Ra V:Rb p1 e1 Qw A:r2 q2 A:t2 v:C Xa m1 o2 M1 A:r3 q3 p2 e2 A:t3 o3 c p3 e3 n0 f0 n1 f1 n2 m2 M2 I f2 n3 g4 u4 g5 u5 m3 M3 f3 P4 e4 P5 e5 J Z m4 m5 M4 f4 M5 f5",
+    last="a:Rw v:k v:Tb Xb Qw v:Ta S v:C Xa H A:r0 K q0 V:t0 A:r1 q1 o0 A:r2 q2 p0 y0 V:t1 o1 A:t2 p1 y1 A:r3 q3 o2 V:t3 p2 y2 A:r4 q4 o3 V:t4 p3 y3 I g5 u5 o4 g6 u6 p4 y4 P5 P6 y5 y6",
+    ub=0, rf=0, rp=0, td=9, tw=9, seed=2, yk="ddaddvv", own=[0], route0="xXXXv", cuts0=[0, 576, 1584, 2592, 3600, W],
+    start="e0 e1 m0 m1 M0 f0 e2 M1 f1 e3 t2 m2 m3 M2 f2 e4 M3 f3 m4 t1 M4 f4 t3 t4 t5",
+    tries=[[5000, 9000, 9000, 9000, 8000]], heat=0.3, dr="a", ai=1, strict="va", cy=0.00083, ga=1.56, fv=0.05, arr=5.0, add=2.9, once=1.8,
+    ways=[(0.11, 1.0, 1.0, 1.0, 1.0), (0.11, 1.0, 1.6, 1.05, 0.85), (0.1, 1.3, 1.1, 1.0, 0.75), (0.15, 1.1, 1.45, 1.4, 1.0)])
+CFG.update(
+    tw=1, route0="xxxwv", route=["ZZZwwv"] * 3, yc=[W, 3456, 2464, 1472, X, 512, 0], tries=[[6000, 3000, 16000, 3000, 9000], [0, 2000, 0, 0, 0]],
+    link=130.0, far=0.3, arr=2.6, own=[], fv=0.04,
+    steps="a:r0 v:k U v:Tb Xb q0 a:t0 S H K o0 A:r1 q1 p0 e0 v:Ta Xa A:t1 m0 o1 M0 A:Ra V:Rb p1 e1 Qw A:r2 q2 A:t2 v:C Xq m1 o2 M1 A:r3 q3 p2 e2 A:t3 o3 c p3 e3 n0 f0 n1 f1 n2 m2 M2 I f2 n3 g4 u4 g5 u5 m3 M3 f3 P4 e4 P5 e5 J Z m4 m5 M4 f4 M5 f5",
+    last="a:Rw v:k U v:Tb Xb Qw v:Ta Xa S v:C Xq H A:r0 K q0 V:t0 A:r1 q1 o0 A:r2 q2 p0 y0 V:t1 o1 A:t2 p1 y1 A:r3 q3 o2 V:t3 p2 y2 A:r4 q4 o3 A:t4 p3 y3 o4 p4 y4 I p5 p6 y5 p7 y6 y7")
+CFG.update(rc=3, own=[0], once=2.5, across=0.6, fv=0.03,
+           ways=[(0.16, 1.0, 1.05, 1.0, 1.0), (0.12, 1.1, 1.45, 1.05, 0.85), (0.2, 1.3, 1.0, 1.0, 0.75), (0.3, 1.1, 1.4, 1.35, 1.0)])
+CFG.update(dr="v", front=CFG["front"].replace("d e", "E d e"), route0="xxxxv")
+CFG.update(seed=[2, 1, 1, 1, 4], tries=[[4000, 7000, 7000, 7000, 7000]], yk="ddaddvvv", lp=[(3584, W), (3072, 3584), (2048, 3072), (1536, 2048), (X, 1536), (512, X), (256, 512), (0, 256)])
+DONE = {}
 
 SCRATCH = {
     "s0": ("sbuf", [128, W + 2 * PB], "bfloat16"),
     "sa": ("sbuf", [128, W + 2 * PF], "float32"),
     "sb": ("sbuf", [128, W + 2 * PF], "float32"),
-    "bb": ("sbuf", [128, W // 2], "float32"),
     "cw": ("sbuf", [128, (FR + 1) * W], "bfloat16"),
-    "cr": ("sbuf", [128, W], "bfloat16"),
+    "srt": ("sbuf", [128, QX], "uint16"),
+    "sr": ("sbuf", [128, W], "float32"),
+    "hdt": ("sbuf", [128, 128], "float32"),
     "tb": ("sbuf", [128, W - X], "float32"),
     "xo": ("sbuf", [128, XW], "float32"),
+    "xb": ("sbuf", [128, XW], "bfloat16"),
+    "lb": ("sbuf", [128, XW], "bfloat16"),
     "vt": ("sbuf", [128, W], "float32"),
     "gv": ("sbuf", [128, W], "bfloat16"),
     "rg": ("sbuf", [128, W], "bfloat16"),
@@ -84,13 +109,12 @@ SCRATCH = {
     "ev": ("sbuf", [128, 144], "bfloat16"),
     "b2": ("sbuf", [128, 1024], "float32"),
     "b3": ("sbuf", [128, 1024], "float32"),
-    "er": ("sbuf", [128, 144], "bfloat16"),
+    "er": ("sbuf", [128, 272], "bfloat16"),
     "one": ("sbuf", [128, 16], "float32"),
     "nil": ("sbuf", [128, 128], "float32"),
     "idf": ("sbuf", [128, 256], "float32"),
-    "upf": ("sbuf", [128, 128], "float32"),
-    "dnf": ("sbuf", [128, 128], "float32"),
-    "hff": ("sbuf", [128, 128], "float32"),
+    "upf": ("sbuf", [128, 256], "float32"),
+    "dnf": ("sbuf", [128, 256], "float32"),
     "idb": ("sbuf", [128, 128], "bfloat16"),
     "upb": ("sbuf", [128, 128], "bfloat16"),
     "dnb": ("sbuf", [128, 128], "bfloat16"),
@@ -101,7 +125,7 @@ SCRATCH = {
     "c2": ("sbuf", [128, 48], "int32"),
     "c3": ("sbuf", [128, 48], "int32"),
     "c4": ("sbuf", [128, 48], "int32"),
-    "lst": ("sbuf", [128, 48], "uint16"),
+    "lst": ("sbuf", [128, 64], "uint16"),
     "pe0": ("psum", [128, 512], "float32"),
     "pe1": ("psum", [128, 512], "float32"),
     "pm": ("psum", [128, 1024], "float32"),
@@ -111,15 +135,11 @@ SCRATCH = {
 }
 for _t in range(FR):
     SCRATCH["lq%d" % _t] = ("sbuf", [128, XW], "float32")
-    if 0 < _t < FR - 1:
-        SCRATCH["lu%d" % _t] = ("sbuf", [128, XW - HX], "float32")
-    for _k, (_a, _b) in enumerate(PARTS):
-        SCRATCH["hx%d_%d" % (_t, _k)] = ("dram", [256, _b - _a], "float32")
 
 NP = 8
 SEMAPHORES = (["cv", "ca", "cp", "cg", "hs"] + ["sx%d" % k for k in range(len(PARTS))]
               + ["%s%d_%d" % (s, t, k) for s in ("xa", "arr") for t in range(FR) for k in range(len(PARTS))]
-              + ["ld%d" % k for k in range(6)] + ["ldc%d" % k for k in range(FR + 1)] + ["ldi0", "ldi1", "ldr", "ldh", "ldq", "rwd", "trn", "zd0", "zd1", "zd2", "zd3", "ya"]
+              + ["ld%d" % k for k in range(6)] + ["ldc%d" % k for k in range(FR + 1)] + ["ldi0", "ldi1", "ldr", "ldh", "ldt0", "ldt1", "ldt2", "ldt3", "rwd", "trn", "zf", "zd0", "zd1", "zd2", "zd3"]
               + ["out%d" % k for k in range(8)] + ["f%s%d" % (c, k) for c in "lab" for k in range(NP)])
 PSUM = ("pe0", "pe1", "pm", "pd", "pc", "pr")
 COUNTER = {"v": "cv", "a": "ca", "p": "cp", "g": "cg"}
@@ -136,7 +156,7 @@ def hazards(ops):
                 acc += [((name, b), max(lo, 512 * b), min(hi, 512 * b + 512), wr, True, lane) for b in range(lo // 512, (hi - 1) // 512 + 1)]
             else:
                 acc.append((name, lo, hi, wr, False, lane))
-        d, s = set(o["after"]), set()
+        d, s = set(o["after"]), set(o.get("follows", []))
         for name, lo, hi, wr, ps, lane in acc:
             for j, lo2, hi2, wr2, lane2 in seen.get(name, []):
                 if ps and ops[j]["q"] != o["q"]:
@@ -165,6 +185,12 @@ def hazards(ops):
 def arrange(ops, deps, soft):
     n, lat = len(ops), CFG["lat"]
     kids, parents = [[] for _ in range(n)], [sorted(deps[i] | soft[i]) for i in range(n)]
+    line = []
+    for q in CFG["strict"]:
+        mine = [i for i in range(n) if ops[i]["q"] == q and ops[i]["now"]]
+        line += [(i, j) for j, i in zip(mine, mine[1:]) if j not in parents[i]]
+    for i, j in line:
+        parents[i].append(j)
     for i in range(n):
         for j in parents[i]:
             kids[j].append(i)
@@ -182,7 +208,7 @@ def arrange(ops, deps, soft):
             mine = ready[q] + (ready.get("x", []) if q in ("a", "v") else [])
 
             def place(k):
-                return (q == "v" and queue[k] == "x" and not ops[k]["now"], rank[k], k)
+                return (q == "v" and queue[k] == "x", rank[k], k)
 
             i = min([k for k in mine if can[k] <= t + eps], key=place)
             if can[i] > t + 0.02:
@@ -225,13 +251,173 @@ def arrange(ops, deps, soft):
     best = None
     for eps in CFG["eps"]:
         now = lay([o["p"] for o in ops], queue, False, eps)
+        best = min(best or now, now) if not CFG["turns"] else best
         for _ in range(CFG["turns"]):
             now = lay([-e for e in lay([-e for e in now[3]], now[2], True, eps)[3]], queue, False, eps)
-            now = (sum(replay(now[1], now[2], *w) for w in CFG["ways"]),) + now[1:]
+            now = (sum(replay(now[1], now[2], *w[:3]) for w in CFG["ways"]),) + now[1:]
             best = min(best or now, now)
-    for o, q in zip(ops, best[2]):
+    order = list(best[1])
+    for i, j in line:
+        parents[i].remove(j)
+        kids[j].remove(i)
+    order, took = polish(ops, deps, parents, kids, order, list(best[2]))
+    for o, q in zip(ops, took):
         o["q"] = q or None
-    return best[1]
+    return order
+
+
+def polish(ops, deps, parents, kids, order, took):
+    n, ways = len(ops), CFG["ways"]
+    dep = [sorted(d) for d in deps]
+    free = [o.get("free", False) for o in ops]
+    cost = [[o["c"] * (pe if o["q"] == "p" else 1.0 if o["q"] in ("g", "s") else dma if o["q"] in ("L", "M") else cy) + o["g"] * cy * (ga - 1.0) for o in ops] for wake, dma, pe, cy, ga in ways]
+    tail = [[o["l"] * w[1] for o in ops] for w in ways]
+    move = [[o["d"] * w[1] for o in ops] for w in ways]
+
+    state = [([0.0] * n, {}, 0.0) for _ in ways]
+
+    def run(order, took, goal, keep=False):
+        total, why = 0.0, []
+        for x, (w, c, l, d) in enumerate(zip(ways, cost, tail, move)):
+            end, at, e = state[x]
+            wake, across, at, last, by, ej = w[0], CFG["across"] * w[0], dict(at), {}, {}, -1
+            for i in order:
+                q = took[i]
+                t, b = at.get(q, 0.0), last.get(q, -1)
+                for j in dep[i]:
+                    x1 = end[j] if took[j] == q else end[j] + across
+                    if x1 > t:
+                        t, b = x1, j
+                t += c[i] + (0.015 if free[i] and q == "a" else 0.0)
+                if q:
+                    at[q], last[q] = t, i
+                t += l[i]
+                if d[i]:
+                    if e > t:
+                        t, b = e, ej
+                    t += d[i]
+                    e, ej = t, i
+                end[i], by[i] = t + wake, b
+            top = goal if goal >= 0 else max(order, key=lambda i: end[i])
+            total += end[top] / w[3]
+            why.append((top, by))
+            if keep:
+                state[x] = (end, at, e)
+        return total, why
+
+    def before(order, place, i, j):
+        need, todo = {i}, [i]
+        while todo:
+            for k in parents[todo.pop()]:
+                if place.get(k, -1) >= place[j] and k not in need:
+                    if k == j:
+                        return None
+                    need.add(k)
+                    todo.append(k)
+        a, b = place[j], place[i] + 1
+        return order[:a] + [k for k in order[a:b] if k in need] + [k for k in order[a:b] if k not in need] + order[b:]
+
+    def behind(order, place, j, i):
+        need, todo = {j}, [j]
+        while todo:
+            for k in kids[todo.pop()]:
+                if place.get(k, n) <= place[i] and k not in need:
+                    if k == i:
+                        return None
+                    need.add(k)
+                    todo.append(k)
+        a, b = place[j], place[i] + 1
+        return order[:a] + [k for k in order[a:b] if k not in need] + [k for k in order[a:b] if k in need] + order[b:]
+
+    seed = [0]
+
+    def draw(k):
+        seed[0] = (seed[0] * 1103515245 + 12345) % 2 ** 31
+        return (seed[0] >> 8) % k
+
+    def stretch(order, took, goal, tries):
+        now, why = run(order, took, goal)
+        best, place = (now, order, took), None
+        for step in range(tries):
+            i, by = why[draw(len(ways))]
+            path = []
+            while by.get(i, -1) in by:
+                if by[i] not in deps[i] or free[i]:
+                    path.append((by[i], i))
+                i = by[i]
+            if not path:
+                break
+            j, i = path[draw(len(path))]
+            if place is None:
+                place = {k: x for x, k in enumerate(order)}
+            new, eng, kind = None, took, draw(10)
+            if kind >= 8:
+                j = order[draw(len(order))]
+                mates = [k for k in order[place[j] + 1:place[j] + 40] if took[k] == took[j]][:2]
+                if mates and took[j]:
+                    i = mates[draw(len(mates))]
+                    new = before(order, place, i, j) if kind % 2 else behind(order, place, j, i)
+            elif kind < 2 and (free[i] or free[j]):
+                k = i if free[i] and (kind or not free[j]) else j
+                new, eng = order, list(took)
+                eng[k] = "av"[took[k] == "a"]
+            elif j not in deps[i]:
+                if kind == 7:
+                    mates = [k for k in order[max(0, place[j] - 40):place[j]] if took[k] == took[i]]
+                    j = mates[-1] if mates else j
+                new = before(order, place, i, j) if kind % 2 else behind(order, place, j, i)
+            if new is None:
+                continue
+            got, how = run(new, eng, goal)
+            if got <= now + CFG["heat"] * (1.0 - step / tries) * draw(100) / 100.0:
+                now, why, order, took, place = got, how, new, eng, None
+                if now < best[0]:
+                    best = (now, order, took)
+        return best[1], best[2]
+
+    def like(part, took, model, t):
+        rank, r, took = {}, -1.0, list(took)
+        for i in part:
+            x = model.get((ops[i]["key"][0] - t,) + ops[i]["key"][1:])
+            r = x[0] if x else r + 0.001
+            rank[i] = r
+            if x and free[i]:
+                took[i] = x[1]
+        left = {i: sum(j in rank for j in parents[i]) for i in part}
+        ready, out = [i for i in part if not left[i]], []
+        while ready:
+            i = min(ready, key=lambda k: rank[k])
+            ready.remove(i)
+            out.append(i)
+            for k in kids[i]:
+                if k in left:
+                    left[k] -= 1
+                    if not left[k]:
+                        ready.append(k)
+        return out, took
+
+    gates = [i for i in range(n) if ops[i]["now"] == "gate"]
+    model, whole = None, order
+    for turn in CFG["tries"]:
+        done, order = [], whole
+        state[:] = [([0.0] * n, {}, 0.0) for _ in ways]
+        for t, (gate, goal, tries) in enumerate(zip(gates + [-1], [i for i in range(n) if ops[i]["now"] == "goal"] + [-1], turn)):
+            b = order.index(goal) + 1 if goal >= 0 else len(order)
+            part = order[:b]
+            if model and 0 < t < FR:
+                other = like(part, took, model, t)
+                if run(other[0], other[1], goal)[0] < run(part, took, goal)[0]:
+                    part, took = other
+            seed[0] = CFG["seed"][t]
+            part, took = stretch(part, took, goal, tries)
+            if t == 2:
+                model = {(ops[i]["key"][0] - t,) + ops[i]["key"][1:]: (float(x), took[i]) for x, i in enumerate(part)}
+            order = part + order[b:]
+            a = order.index(gate) if gate >= 0 else len(order)
+            run(order[:a], took, -1, True)
+            done, order = done + order[:a], order[a:]
+        whole = done
+    return whole, took
 
 
 def emit(g, T, ops, deps, order):
@@ -248,12 +434,12 @@ def emit(g, T, ops, deps, order):
         plan[i] = []
         mine = done.setdefault(o["q"], {})
         for key, j in sorted(last.items(), key=lambda x: -place[x[1]]):
-            if o["q"] and mine.get(key, -1) < place[j]:
+            if o["q"] in queue and mine.get(key, -1) < place[j]:
                 for k, v in list(knew[j].items()) + [(key, place[j])]:
                     mine[k] = max(mine.get(k, -1), v)
                 plan[i].append(j)
                 need.add(j)
-        knew[i] = dict(mine) if o["q"] else {}
+        knew[i] = dict(mine) if o["q"] in queue else {}
     total, mark = {}, {}
     for i in order:
         o = ops[i]
@@ -284,13 +470,10 @@ def helpers(core, nxt, T, topo):
     return out, [c for c in near if c not in out][:2]
 
 
-def turned(t):
-    return t if t < FR - 1 else 0
-
-
 def senders(t, core, nxt, T, topo):
     ports = helpers(core, nxt, T, topo)[0]
-    return [ports[0], core if topo.may_write(core, nxt) else ports[1]]
+    near = core if topo.may_write(core, nxt) else ports[1]
+    return [near if t in CFG["own"] else ports[0], near, near]
 
 
 def rank_program(g, core, T, topo):
@@ -298,44 +481,30 @@ def rank_program(g, core, T, topo):
     for rank, rc in enumerate(T.cores):
         nxt = T.cores[(rank + 1) % n_ranks]
         ports, turns = helpers(rc, nxt, T, topo)
-        if core in ports:
-            hand_on(g, core, rc, nxt, T, topo)
-        elif core == rc or core in turns:
+        if core == rc or core in turns or core in ports:
             ops = build(rc, T, topo)
             deps, soft = hazards(ops)
-            order = arrange(ops, deps, soft)
+            key = repr(CFG)
+            if key not in DONE:
+                DONE[key] = (arrange(ops, deps, soft), [o["q"] for o in ops])
+            order = DONE[key][0]
+            for o, q in zip(ops, DONE[key][1]):
+                o["q"] = q
             if core == rc:
                 emit(g, T, ops, deps, order)
             else:
-                hand_back(g, core, rc, [ops[i]["fold"] for i in order if ops[i]["fold"]], T, topo)
+                hand_on(g, core, rc, [ops[i]["fold"] for i in order if ops[i]["fold"]], T, topo)
 
 
-def hand_on(g, core, rc, nxt, T, topo):
-    rid, pid, _ = topo.addr(nxt)
-    n_in = len(topo.engines(rc, core))
-    calls = 0
-    for t in range(FR):
-        r0 = (128 - 16 * turned(t)) % 128
-        for k, (a, b) in enumerate(PARTS):
-            if senders(t, rc, nxt, T, topo)[k] == core:
-                g.wait_ge(T.sem["xa%d_%d" % (t, k)], n_in * (2 if turned(t) else 1))
-                g.remote_dma(T["lq%d" % t][:, a:b], T["hx%d_%d" % (t, k)][r0:r0 + 128, :], T.sem["arr%d_%d" % (t, k)], T.sem.hs,
-                             pid, rid, topo.mask(core, nxt))
-                calls += 1
-    if calls:
-        g.wait_ge(T.sem.hs, calls * len(topo.engines(core, nxt)))
-
-
-def hand_back(g, core, rc, folds, T, topo):
-    rid, pid, _ = topo.addr(rc)
-    n = len(topo.engines(rc, core))
+def hand_on(g, core, rc, jobs, T, topo):
     got, sent = {}, 0
-    for who, k, v0, v1 in folds:
+    for who, n, came, (buf, a, b), to, sem in jobs:
         if who == core:
-            got[k] = got.get(k, 0) + n
-            g.wait_ge(T.sem["fa%d" % k], got[k])
-            g.remote_dma(T.bb[:, v0 - BB:v1 - BB], T.bb[:, v0 - BB:v1 - BB], T.sem["fb%d" % k], T.sem.hs, pid, rid, topo.mask(core, rc))
-            sent += len(topo.engines(core, rc))
+            rid, pid, _ = topo.addr(to)
+            got[came] = got.get(came, 0) + n
+            g.wait_ge(T.sem[came], got[came])
+            g.remote_dma(T[buf][:, a:b], T[buf][:, a:b], T.sem[sem], T.sem.hs, pid, rid, topo.mask(core, to))
+            sent += len(topo.engines(core, to))
     if sent:
         g.wait_ge(T.sem.hs, sent)
 
@@ -347,12 +516,17 @@ def build(core, T, topo):
     prv = T.cores[(rank - 1) % n_ranks]
     turns = helpers(core, nxt, T, topo)[1]
     cy, GA = CFG["cy"], CFG["ga"]
-    ops, lag, firsts = [], [0], set()
+    ops, lag, firsts, tag = [], [0], set(), [-9, "", 0]
 
-    def op(q, f, r, w, c, sem=None, n=0, l=0.0, d=0.0, after=(), fold=None, now=False):
+    def op(q, f, r, w, c, sem=None, n=0, l=0.0, d=0.0, after=(), fold=None, now=False, g=0.0):
         ops.append({"q": q, "f": f, "r": r, "w": w, "c": c, "sem": sem, "n": n, "l": l, "d": d, "after": after, "fold": fold,
-                    "now": now, "p": len(ops) + lag[0]})
+                    "now": now, "p": len(ops) + lag[0], "g": g, "key": (tag[0], tag[1], len(ops) - tag[2])})
         return len(ops) - 1
+
+    def join(k):
+        parts = ops[-k:]
+        del ops[-k:]
+        op("p", lambda e: [x["f"](e) for x in parts][-1], [r for x in parts for r in x["r"]], parts[-1]["w"], sum(x["c"] for x in parts))
 
     def once(who):
         new = who not in firsts
@@ -372,10 +546,10 @@ def build(core, T, topo):
         return ap(win).indirect(ap(off))
 
     def cost(out, k=1.0):
-        return (0.05 if k == GA else 0.02) + max(64, size(out) * k) * cy
+        return (0.05 if k == GA else CFG["fv"]) + max(64, size(out) * k) * cy
 
     def dma(q, out, in_, r, w, sem, kb):
-        op(q, lambda e: e.dma_start(out, in_).then_inc(T.sem[sem], 16), r, w, 0.08, sem, 16, 1.5, kb / 600)
+        op(q, lambda e: e.dma_start(out, in_).then_inc(T.sem[sem], 16), r, w, 0.08, sem, 16, 1.5, 0.2 + kb / 600)
 
     def tt(out, a, b, alu):
         op("v", lambda e: e.tensor_tensor(ap(out), ap(a), ap(b), alu), [a, b], [out], cost(out, 1 if a[0] in PSUM or b[0] in PSUM else 2))
@@ -390,7 +564,7 @@ def build(core, T, topo):
         op("v", lambda e: e.tensor_copy(ap(out), ap(a)), [a], [out], cost(out))
 
     def act(out, a, func=F.Copy, col=None, **k):
-        op("a", lambda e: e.activation(ap(out), ap(a), func, **k), [a] + ([col] if col else []), [out], cost(out) + 0.03)
+        op("a", lambda e: e.activation(ap(out), ap(a), func, **k), [a] + ([col] if col else []), [out], cost(out) + 0.015)
 
     def fill(out, c):
         op("v", lambda e: e.memset(ap(out), c), [], [out], cost(out))
@@ -408,16 +582,14 @@ def build(core, T, topo):
                 return e.tensor_scalar(ap(out), ind(win, off), 0.0, 0.5, A.is_le, A.subtract)
             return e.tensor_copy(ap(out), ind(win, off))
 
-        op(q, call, [win, off], [out], cost(out, GA), now=now)
+        op(q.lower(), call, [win, off], [out], cost(out, GA), now=now, g=size(out) * GA * cy)
+        ops[i]["free"] = q in "xAV"
 
-    def gts(out, win, off, s1, o1, s2=None, o2=None):
-        if o2 is None:
-            op("v", lambda e: e.tensor_scalar(ap(out), ind(win, off), s1, None, o1), [win, off], [out], cost(out, GA))
-        else:
-            op("v", lambda e: e.tensor_scalar(ap(out), ind(win, off), s1, s2, o1, o2), [win, off], [out], cost(out, GA))
+    def gts(out, win, off, s1, o1, s2, o2):
+        op("v", lambda e: e.tensor_scalar(ap(out), ind(win, off), s1, s2, o1, o2), [win, off], [out], cost(out, GA), g=size(out) * GA * cy)
 
     def gtt(out, win, off, x, alu):
-        op("v", lambda e: e.tensor_tensor(ap(out), ind(win, off), ap(x), alu), [win, off, x], [out], cost(out, GA))
+        op("v", lambda e: e.tensor_tensor(ap(out), ind(win, off), ap(x), alu), [win, off, x], [out], cost(out, GA), g=size(out) * GA * cy)
 
     def scan(out, d0, d1, init, back=False):
         o = rev(out) if back else ap(out)
@@ -443,20 +615,24 @@ def build(core, T, topo):
 
     LA, LB, LP = ("lst", 0, 16), ("lst", 16, 32), ("lst", 32, 48)
 
-    def turn(kp, tw):
-        tr((tw, 0, 256), (kp, 16, 272))
-        tr((tw, 256, 544), (kp, 0, 288))
+    def turn(kp, tw, k):
+        if k:
+            tr((tw, 256, 544), (kp, 0, 288))
+        else:
+            tr((tw, 0, 256), (kp, 16, 272))
 
     cuts0 = CFG["cuts0"]
     n0 = len(cuts0) - 1
     for k in range(n0):
         a, b = cuts0[k], cuts0[k + 1]
-        dma("sa"[k % 2], T.s0[:, PB + a:PB + b], T.sp[:, a:b], [], [("s0", PB + a, PB + b)], "ld%d" % k, (b - a) / 4)
+        dma("s", T.s0[:, PB + a:PB + b], T.sp[:, a:b], [], [("s0", PB + a, PB + b)], "ld%d" % k, (b - a) / 4)
     dma("s", T.iti[:, 0:256], T.itg[:, 0:256], [], [("iti", 0, 256)], "ldi0", 128)
     dma("s", T.roti[:], T.rot[:], [], [("roti", 0, 256)], "ldr", 128)
+    for k in range(1, len(ops)):
+        ops[k]["follows"] = [k - 1]
     dma("s", T.iti[:, 256:1024], T.itg[:, 256:1024], [("s0", PB, PB + W)], [("iti", 256, 1024)], "ldi1", 384)
-    for c in range(16):
-        dma("s", T.hopi[c::16, :], T.hop[:], [("iti", 0, 256)], [("hopi%d" % c, 0, 4)], "ldh", 1)
+    op("s", lambda e: [e.dma_start(T.hopi[c::16, :], T.hop[:]).then_inc(T.sem.ldh, 16) for c in range(16)],
+       [("iti", 0, 256)], [("hopi", 0, 4)], 1.0, "ldh", 256, 1.5, 0.5)
 
     fill(("nil", 0, 128), 0.0)
     fill(("s0", 0, PB), 0.0)
@@ -477,7 +653,7 @@ def build(core, T, topo):
     fill(("one", 0, 8), 1.0)
     fill(("one", 8, 16), -BIG)
     fill(("ea", 0, 144), 0.0)
-    fill(("er", 0, 144), 0.0)
+    fill(("er", 0, 272), 0.0)
     fill(("cb", 0, 256), -3 * BIG)
     iota(("c1", 0, 48), [[0, 48]], 0, 1)
     iota(("c2", 0, 16), [[0, 16]], 0, 1)
@@ -503,9 +679,14 @@ def build(core, T, topo):
     lag[0] = 600
     iota(("mc", 0, 256), [[16, 256]], -6143, 0, True)
     const(("cm", 0, QX), W * RND)
-    for name, c in (("dnf", -4096.0), ("upf", 4096.0), ("idf", 1.0), ("hff", 2048.0)):
+    if CFG["rp"]:
+        lag[0] = 900
+        iota(("eh", 0, 2064), [[0, 2064]], 0, 0, True)
+        pick(("eh", 16, 2064, 16), ("nil", 0, 128), [[-1, 16], [-16, 8]], A.not_equal, 0, 1, 1.0)
+        lag[0] = 600
+    for name, c in (("dnf", -4096.0), ("upf", 4096.0), ("idf", 1.0)):
         diag((name, 0, 128), c)
-    diag(("idf", 128, 256), 1.0)
+        diag((name, 128, 256), c)
     for s in ("sa", "sb"):
         const((s, 0, PF), 0.0)
         const((s, PF + W, 2 * PF + W), 0.0)
@@ -519,31 +700,41 @@ def build(core, T, topo):
     tt(("c3", 0, 16), ("c3", 0, 16), ("c4", 32, 48), A.add)
     ts(("c2", 0, 32), ("c2", 0, 32), 272.0, A.mult)
     cp(LP, ("c3", 0, 16))
+    cp(("lst", 48, 64), ("c3", 16, 32))
     cp(("col", 0, 1), ("c1", 0, 1))
     tt(("c2", 0, 32), ("c2", 0, 32), ("c3", 0, 32), A.add)
     cp(("lst", 0, 32), ("c2", 0, 32))
     lag[0] = 600
     act(("mc", 0, 256), ("mc", 0, 256), F.Identity, ("col", 0, 1), bias=T.col[:, 0:1])
     tt(("er", 15, 143, 16), ("e8", 0, 8), ("e8", 8, 16), A.add)
+    act(("er", 143, 271, 16), ("er", 15, 143, 16))
     for k, a in (("kl", 0), ("kr", 8)):
         act(("e8", 24, 32), ("e8", a, a + 8), F.Identity, scale=BIG, bias=1024.0, accum_out=T[k][:, 0:1])
         ops[-1]["w"].append((k, 0, 1))
-    op("v", lambda e: e.tensor_scalar(T.hopf[:], T.hopi[:], -1.0 / W, None, A.mult), [("hopi%d" % c, 0, 4) for c in range(16)], [("hopf", 0, 4)], 0.12)
+    op("v", lambda e: e.tensor_scalar(T.hopf[:], T.hopi[:], -1.0 / W, None, A.mult), [("hopi", 0, 4)], [("hopf", 0, 4)], 0.12)
 
-    def targets(t, *after):
-        cp(("it16", 256 * t, 256 * t + 256), ("iti", 256 * t, 256 * t + 256))
-        ops[-1]["after"] = after
-        gat("v", ("kp2", 16, 272), ("iti", 256 * t, 256 * t + 256), LP)
-        ops[-1]["after"] = after
-        turn("kp2", "tw2")
-        gat("a", ("el", 256 * t, 256 * t + 256), ("tw2", 0, 544), LB, F.Identity, scale=-1.0, bias=float(4095 - 2 ** 24))
+    def targets(t, k):
+        if k == 1:
+            cp(("it16", 256 * t, 256 * t + 256), ("iti", 256 * t, 256 * t + 256))
+        elif t >= CFG["td"]:
+            if k == 2:
+                op("s", lambda e: [e.dma_start(T.eli[:, 256 * t + 16 * r:256 * t + 16 * r + 16], T.itg[r::16, 256 * t:256 * t + 256]).then_inc(T.sem["ldt%d" % t], 16) for r in range(16)],
+                   [("gv" if t == 1 else "dl", 0, W)], [("eli", 256 * t, 256 * t + 256)], 1.0, "ldt%d" % t, 256, 1.5, 5.0)
+            elif k == 5:
+                gat("a", ("el", 256 * t, 256 * t + 256), ("eli", 256 * t, 256 * t + 256), LP, F.Identity, scale=-1.0, bias=float(4095 - 2 ** 24))
+        elif k == 2:
+            gat("a" if CFG["ai"] else "v", ("kp2", 16, 272), ("iti", 256 * t, 256 * t + 256), LP)
+        elif k < 5:
+            turn("kp2", "tw2", k - 3)
+        else:
+            gat("a", ("el", 256 * t, 256 * t + 256), ("tw2", 0, 544), LB, F.Identity, scale=-1.0, bias=float(4095 - 2 ** 24))
 
     def rows(rw):
         buf, a, b = rw
         dma("s", T[buf][0::16, a:b], T.hl[:, 0:256], [("hl", 0, 256)], [(buf, a, b, 2)], "rwd", 100)
         dma("s", T[buf][15::16, a:b], T.hl[:, 256:512], [("hl", 256, 512)], [(buf, a + 1, b, 2)], "rwd", 100)
 
-    turnno = [0, 0, 0]
+    turnno, sent, added, landed = [0, 0, 0], [], [], []
 
     def bank(n):
         o = 512 * (turnno[1] % 2)
@@ -566,6 +757,8 @@ def build(core, T, topo):
                 for j, (name, buf, at) in enumerate([("dn", s, -pad)] + terms):
                     lhs, k = mat(name, s)
                     mm((p[0], p[1] + c - a, p[1] + min(b, c + step) - a), lhs, (buf, c - at, min(b, c + step) - at), j == 0, j == len(terms), k)
+                if s == "s0":
+                    join(len(terms) + 1)
             lag[0] -= CFG["jl"]
             if terms[0][1] == "bb":
                 ops[-1]["w"].append(("bbw", a, b))
@@ -579,67 +772,94 @@ def build(core, T, topo):
         u = "h%d" % k if s == "s0" and by not in "YZyz" else "b%d" % j
         lhs, c = mat("id", s)
         lo, hi = pad + v0, pad + v1
-        if by.islower():
-            act((p, 0, h + 2), (s, lo - 2, hi + 2, 2))
-        else:
-            mm((p, 0, h + 2), lhs, (s, lo - 2, hi + 2, 2), True, True, c)
-        by = by.upper()
+        kind = by.upper()
+        m, b = "pm" if kind == "V" else u, "a%d" % k
+        a = ("pm", 512 * k, 512 * k + h) if kind != "V" else ("pm", 1024 - h, 1024) if n + h <= 1024 else (p, 2, h + 2)
+
+        def even():
+            if by.islower():
+                act((p, 0, h + 2), (s, lo - 2, hi + 2, 2))
+            else:
+                mm((p, 0, h + 2), lhs, (s, lo - 2, hi + 2, 2), True, True, c)
+
+        def minus():
+            if kind in "YZ":
+                act(("vt", v0, v1), (s, lo, hi), scale=-2.0 if kind == "Y" else -1.0)
 
         def add(at):
             op("g", lambda e: e.dma_start(T.vt[:, v0:v1], T[u][:, at:at + n], accum_op=A.add).then_inc(T.sem["zd%d" % j], 16),
-               [(u, at, at + n)], [("vt", v0, v1)], 1.0 + once("g") / 3, "zd%d" % j, 16, CFG["add"], n / 600)
+               [(u, at, at + n)], [("vt", v0, v1)], 1.0 + once("g") / 3, "zd%d" % j, 16, CFG["add"] - 1.0, 0.3 + n / 600)
+            ops[-1]["follows"] = added[-1:]
+            added.append(len(ops) - 1)
 
-        if by in "YZ":
-            act(("vt", v0, v1), (s, lo, hi), scale=-2.0 if by == "Y" else -1.0)
-        if by in "XY":
-            tt((p, 0, h + 2), (p, 0, h + 2), (s, lo - 1, hi + 2, 2), A.max)
-            tt((u, 0, n + 2, 2), (p, 0, h + 1), (s, lo, hi + 1, 2), A.max)
-            tt((u, 1, n + 2, 2), (p, 1, h + 2), (s, lo - 1, hi, 2), A.max)
-            if by == "X":
-                judge(s, pad, v0, v1, [("hf", u, v0), ("hf", u, v0 - 2)])
+        def maxima():
+            if kind in "XY":
+                tt((p, 0, h + 2), (p, 0, h + 2), (s, lo - 1, hi + 2, 2), A.max)
+                return
+            tt((b, 0, h + 1), (p, 0, h + 1), (s, lo + 1, hi + 2, 2), A.max)
+            tt(a, (p, 2, h + 2), (s, lo - 1, hi - 1, 2), A.max)
+
+        def more():
+            if kind in "XY":
+                tt((u, 0, n + 2, 2), (p, 0, h + 1), (s, lo, hi + 1, 2), A.max)
+                tt((u, 1, n + 2, 2), (p, 1, h + 2), (s, lo - 1, hi, 2), A.max)
             else:
+                tt((m, 0, n, 2), a, (b, 0, h), A.max)
+                tt((m, 1, n, 2), a, (b, 1, h + 1), A.max)
+
+        def finish():
+            if kind == "X":
+                judge(s, pad, v0, v1, [("hf", u, v0), ("hf", u, v0 - 2)])
+            elif kind == "Y":
                 add(0)
                 add(2)
-            return
-        b, m = "a%d" % k, "pm" if by == "V" else u
-        a = ("pm", 512 * k, 512 * k + h) if by != "V" else ("pm", 1024 - h, 1024) if n + h <= 1024 else (p, 2, h + 2)
-        tt((b, 0, h + 1), (p, 0, h + 1), (s, lo + 1, hi + 2, 2), A.max)
-        tt(a, (p, 2, h + 2), (s, lo - 1, hi - 1, 2), A.max)
-        tt((m, 0, n, 2), a, (b, 0, h), A.max)
-        tt((m, 1, n, 2), a, (b, 1, h + 1), A.max)
-        if by == "V":
-            z = 1 if v0 == 0 else 0
-            tt(("vt", v0 + z, v1), (m, z, n), (s, lo + z, hi), A.subtract)
-        elif by == "Z":
-            add(0)
-        else:
-            judge(s, pad, v0, v1, [("up", u, v0)])
+            elif kind == "V":
+                z = 1 if v0 == 0 else 0
+                tt(("vt", v0 + z, v1), (m, z, n), (s, lo + z, hi), A.subtract)
+            elif kind == "Z":
+                add(0)
+            else:
+                judge(s, pad, v0, v1, [("up", u, v0)])
+
+        return {"e": even, "n": minus, "m": maxima, "M": more, "f": finish}
 
     def fold_out(s, pad, v0, v1, k):
-        who = turns[k % len(turns)]
+        who = helpers(core, nxt, T, topo)[0][0] if CFG["fw"] == "p" else turns[k % len(turns)]
         rid, pid, _ = topo.addr(who)
         kb = (v1 - v0) / 2
         x = RemoteDMATransfer(dst_ids=[DstId(rid=rid, pnc=pid)], dma_engine_mask=topo.mask(core, who), remote_sem=T.sem["fa%d" % k],
                               srcs=[T[s][:, pad + v0 + h:pad + v1 + h] for h in (-2, -1, 1, 2)], dsts=[T.bb[:, v0 - BB:v1 - BB]], alu_op=2)
         i = op("g", lambda e: e.remote_dma_fused([x], local_sem=T.sem["fl%d" % k]), [(s, pad + v0 - 2, pad + v1 + 2), ("bbw", v0, v1)], [],
-               1.0, "fl%d" % k, len(topo.engines(core, who)), 1.0, 4 * kb / 500, fold=(who, k, v0, v1))
+               1.0, "fl%d" % k, len(topo.engines(core, who)), 1.0, 4 * kb / 550,
+               fold=(who, len(topo.engines(core, who)), "fa%d" % k, ("bb", v0 - BB, v1 - BB), core, "fb%d" % k))
         op(None, None, [], [("bb", v0 - BB, v1 - BB)], 0.0, "fb%d" % k, len(topo.engines(who, core)), CFG["back"] + kb / 500 + once(who), after=(i,))
+
+    def folded(s, v0, v1, k):
+        turnno[0] += 1
+
+        def add():
+            op("g", lambda e: e.dma_start(T.vt[:, v0:v1], T.bb[:, v0 - BB:v1 - BB], accum_op=A.add).then_inc(T.sem.zf, 16),
+               [("bb", v0 - BB, v1 - BB)], [("vt", v0, v1), ("bbw", v0, v1)], 1.0, "zf", 16, CFG["add"] - 1.0, 0.3 + (v1 - v0) / 600)
+
+        return {"e": lambda: fold_out(s, PF, v0, v1, k), "n": lambda: act(("vt", v0, v1), (s, PF + v0, PF + v1), scale=-1.0),
+                "m": lambda: None, "M": lambda: None, "f": add}
 
     vc = [0] + [c - 4 for c in cuts0[1:n0]] + [W]
     lag[0] = 0
-    for k in range(n0):
-        piece("s0", PB, vc[k], vc[k + 1], CFG["route0"][k])
-    lag[0] = 400
-    targets(0)
+    kept_from = len(ops)
+    turnno[0] = n0 % 2
+    parts = [piece("s0", PB, vc[k], vc[k + 1], CFG["route0"][k]) for k in range(n0)]
+    for step in CFG["start"].split():
+        if step[0] == "t":
+            targets(0, int(step[1:]))
+        else:
+            parts[int(step[1:])][step[0]]()
     lag[0] = 1000
-    cp(("pr", 0, 256), ("roti", 0, 256))
-    act(("hl", 0, 256), ("pr", 0, 256))
-    tt(("hl", 256, 512), ("pr", 0, 256), ("hl", 0, 256), A.subtract)
 
     def records(k, after):
         dma("s", T.cw[:, k * W:k * W + W], T.rec[:], [after], [("cw", k * W, k * W + W)], "ldc%d" % k, 1024)
 
-    for k in range(3):
+    for k in range(CFG["rc"]):
         records(k, ("iti", 256, 1024))
 
     def frame(t):
@@ -647,248 +867,319 @@ def build(core, T, topo):
         old, opad = ("s0", PB) if t == 0 else (("sa", "sb")[(t - 1) % 2], PF)
         new = ("sa", "sb")[t % 2]
         lq = "lq%d" % t
+        xt, lt = ("xo", lq) if t else ("xb", "lb")
         win = (old, opad, opad + W)
         rw = ("s0", PB, PB + W) if t else ("gv", 0, W)
         up = float(W * (t // 2 + 1))
         kept = []
 
-        if t in (1, 2):
-            records(t + 2, ("vt", 0, W))
-        act(("hd", 0, 128), ("upf", 0, 128), F.Identity, ("hopf", 0, 4), scale=T.hopf[:, t:t + 1])
-        if last:
-            r0 = 16 * t
-            dma("s", T.cr[0:128 - r0, :], T.rec[r0:128, :], [("vt", 0, W)], [("cr", 0, W, 2)], "ldq", 600)
-            dma("s", T.cr[128 - r0:128, :], T.rec[0:r0, :], [("vt", 0, W)], [("cr", 1, W, 2)], "ldq", 400)
-        if t:
-            gat("a", ("kp3", 16, 272), ("qf", 0, 256), LP)
-            turn("kp3", "tw3")
-            if CFG["hold"]:
-                for o in ops[-2:]:
-                    o["r"].append(("vt", 0, X))
-            if CFG["lo"] == "v":
-                gat("a", ("hl", 0, 256), ("tw3", 0, 544), LB)
-                gtt(("hl", 256, 512), ("tw3", 0, 544), LB, ("hl", 0, 256), A.subtract)
-            else:
-                gat("a", ("qb", 0, 256), ("tw3", 0, 544), LB)
-                act(("hl", 0, 256), ("qb", 0, 256))
-                mm(("pr", 0, 256), ("upf", 0, 128), ("qb", 0, 256), True, False, 4)
-                mm(("pr", 0, 256), ("dnb", 0, 128), ("hl", 0, 256), False, True)
-                act(("hl", 256, 512), ("pr", 0, 256), scale=1.0 / W)
-            rows(rw)
-        if CFG["dr"] == "v":
-            act(("elr", 0, 256), ("el", 256 * t, 256 * t + 256), F.Identity, bias=4096.0)
-        mm(("pc", 0, 256), ("idb", 0, 128), ("cb", 0, 256), True, False)
-        for b0, b1 in zip(CFG["xs"], CFG["xs"][1:]):
-            i = len(ops)
-            gat("x", ("gv", 256 * b0, 256 * b1), ("vt", 0, W), ("it16", 256 * t + 16 * b0, 256 * t + 16 * b1), F.Sign, scale=-1.0, bias=2.0 ** -32)
-            for b in range(b0, b1):
-                op("p", lambda e, i=i, b=b: e.matmul(T.pc[:, 0:256], T["e" + ops[i]["q"]][:, 15 - b:143 - b], T.gv[:, 256 * b:256 * b + 256], False, b == 15),
-                   [("gv", 256 * b, 256 * b + 256), ("ea", 0, 144), ("ev", 0, 144)], [("pc", 0, 256)], 0.015 + 136 * cy)
-        if not t:
-            rows(rw)
+        r0 = 16 * t
+        at = (128 - r0) % 128
+        xs, counted = CFG["xs"], []
 
-        tt(("dl", 0, 256), ("pc", 0, 256), ("el", 256 * t, 256 * t + 256), A.max)
-        counted = len(ops) - 1
-        if CFG["dr"] == "a":
-            act(("dr", 0, 256), ("dl", 0, 256), F.Identity, bias=4096.0)
-        else:
-            tt(("dr", 0, 256), ("pc", 0, 256), ("elr", 0, 256), A.max)
-        if not last and CFG["tn"] == "c":
-            targets(t + 1, counted)
-        scan(("fg", 0, 256), ("kl", 0, 256), ("dl", 0, 256), NONE)
-        scan(("fg", 256, 512), ("kr", 0, 256), ("dr", 0, 256), NONE, True)
-        tr(("xe", 0, 32), ("fg", 240, 272))
-        scan(("yy", 1, 32), ("st", 0, 31), ("xe", 0, 31), NONE)
-        scan(("yy", 32, 63), ("st", 0, 31), ("xe", 1, 32), NONE, True)
-        tr(("zz", 0, 64), ("yy", 0, 64))
-        scan(("fg", 0, 256), ("kl", 0, 256), ("dl", 0, 256), ("zz", 15, 16))
-        scan(("pc", 256, 512), ("kr", 0, 256), ("dr", 0, 256), ("zz", 48, 49), True)
-        for a in range(0, 256, CFG["dc"]):
-            b = a + CFG["dc"]
-            z = ("pc", a, b)
-            tt(("ki", a, b), ("fg", a, b), ("pc", 256 + a, 256 + b), A.min)
-            ts(("pay", a, b), ("ki", a, b), 8191, A.bitwise_and)
-            ts(("dd", a, b), ("ki", a, b), 12, A.arith_shift_right, -2, A.bitwise_and)
-            ts(z, ("pay", a, b), 4096.0, A.is_lt, 0.5, A.subtract)
-            tt(z, z, ("dd", a, b), A.mult)
-            tt(("kp", 16 + a, 16 + b), z, ("pay", a, b), A.subtract)
-            tr(("tw", a, b), ("kp", 16 + a, 16 + b))
-            e = b if b < 256 else 288
-            tr(("tw", 256 + a, 256 + e), ("kp", a, e))
+        def copies():
+            if t >= CFG["tw"]:
+                dma("s", T.sr[r0:128, :], T[old][0:128 - r0, PF:PF + W], [win], [("sr", 0, W, 2)], "trn", 1800)
+                dma("s", T.sr[0:r0, :], T[old][128 - r0:128, PF:PF + W], [win], [("sr", 1, W, 2)], "trn", 300)
+
+        def hops():
+            act(("hd", 0, 128), ("upf", 0, 128), F.Identity, ("hopf", 0, 4), scale=T.hopf[:, t:t + 1])
+            if t:
+                act(("hdt", 0, 128), ("upf", at, at + 128), F.Identity, ("hopf", 0, 4), scale=T.hopf[:, t:t + 1])
+
+        def split(q):
+            act(("hl", 0, 256), (q, 0, 256))
+            mm(("pr", 0, 256), ("upf", 0, 128), (q, 0, 256), True, False, 4)
+            mm(("pr", 0, 256), ("dnb", 0, 128), ("hl", 0, 256), False, True)
+            act(("hl", 256, 512), ("pr", 0, 256), scale=1.0 / W)
+
+        def r_rows(k):
+            if t and CFG["rp"]:
+                if k == 5:
+                    for r in range(8):
+                        ps, o = (("pe0", 0), ("pe1", 0), ("pm", 0), ("pm", 512), ("pd", 0), ("pd", 512))[r % 6]
+                        for j in range(2):
+                            e0 = 16 + 128 * (r + 8 * j)
+                            mm((ps, o + j, o + 512, 2), ("eh", e0, e0 + 128), ("hl", 0, 256), True, False)
+                            mm((ps, o + j, o + 512, 2), ("eh", e0 - 15, e0 + 113), ("hl", 256, 512), False, True)
+                        join(4)
+                        ops[-1]["w"] = [(ps, o, o + 512)]
+                        if r >= CFG["rf"]:
+                            ops[-1]["follows"] = counted[-1:]
+                        act((rw[0], rw[1] + r, rw[2], 8), (ps, o, o + 512))
+                        ops[-1]["w"] = [("rw%d" % r, 0, 1)]
+                        ops[-1]["r"].append(("rwr", 0, 1))
+            elif k == 5:
+                rows(rw)
+            elif k < 4:
+                if t:
+                    turn("kp3", "tw3", k - 2)
+            else:
+                gat("a", ("qb", 0, 256), *((("tw3", 0, 544), LB) if t else (("roti", 0, 256), ("lst", 48, 64))))
+                split("qb")
+
+        def moved(q, k):
+            b0, b1, i = xs[k], xs[k + 1], len(ops)
+            gat(q, ("gv", 256 * b0, 256 * b1), ("vt", 0, W), ("it16", 256 * t + 16 * b0, 256 * t + 16 * b1), F.Sign, scale=-1.0, bias=2.0 ** -32)
+            for b in range(b0, b1):
+                op("p", lambda e, b=b: e.matmul(T.pc[:, 0:256], T["e" + ops[i]["q"]][:, 15 - b:143 - b], T.gv[:, 256 * b:256 * b + 256], False, b == 15),
+                   [("gv", 256 * b, 256 * b + 256), ("ea", 0, 144), ("ev", 0, 144)], [("pc", 0, 256)], 0.015 + 136 * cy)
+            join(b1 - b0)
+            counted.append(len(ops) - 1)
+
+        def right():
+            if CFG["dr"] == "a":
+                act(("dr", 0, 256), ("dl", 0, 256), F.Identity, bias=4096.0)
+            else:
+                tt(("dr", 0, 256), ("pc", 0, 256), ("elr", 0, 256), A.max)
+
+        def decode():
+            halves = [(a, a + CFG["dc"]) for a in range(0, 256, CFG["dc"])]
+            for a, b in halves:
+                tt(("ki", a, b), ("fg", a, b), ("pc", 256 + a, 256 + b), A.min)
+            for a, b in halves:
+                ts(("pay", a, b), ("ki", a, b), 8191, A.bitwise_and)
+            for a, b in halves:
+                ts(("pc", a, b), ("pay", a, b), 4096.0, A.is_lt, 0.5, A.subtract)
+            ts(("dd", 0, 256), ("ki", 0, 256), 12, A.arith_shift_right, -2, A.bitwise_and)
+            for a, b in halves:
+                tt(("pc", a, b), ("pc", a, b), ("dd", a, b), A.mult)
+            for a, b in halves:
+                tt(("kp", 16 + a, 16 + b), ("pc", a, b), ("pay", a, b), A.subtract)
+            tr(("tw", 0, 128), ("kp", 16, 144))
+            tr(("tw", 256, 544), ("kp", 0, 288))
+            tr(("tw", 128, 256), ("kp", 144, 272))
+
+        front = {
+            "c": lambda: t in (1, 2) and records(t + 2, ("vt", 0, W)), "C": copies, "h": hops,
+            "z": lambda: mm(("pc", 0, 256), ("idb", 0, 128), ("cb", 0, 256), True, False),
+            "E": lambda: CFG["dr"] == "v" and act(("elr", 0, 256), ("el", 256 * t, 256 * t + 256), F.Identity, bias=4096.0),
+            "d": lambda: tt(("dl", 0, 256), ("pc", 0, 256), ("el", 256 * t, 256 * t + 256), A.max), "e": right,
+            "L": lambda: scan(("fg", 0, 256), ("kl", 0, 256), ("dl", 0, 256), NONE),
+            "R": lambda: scan(("fg", 256, 512), ("kr", 0, 256), ("dr", 0, 256), NONE, True),
+            "x": lambda: tr(("xe", 0, 32), ("fg", 240, 272)),
+            "y": lambda: (scan(("yy", 1, 32), ("st", 0, 31), ("xe", 0, 31), NONE), scan(("yy", 32, 63), ("st", 0, 31), ("xe", 1, 32), NONE, True)),
+            "w": lambda: tr(("zz", 0, 64), ("yy", 0, 64)),
+            "F": lambda: scan(("fg", 0, 256), ("kl", 0, 256), ("dl", 0, 256), ("zz", 15, 16)),
+            "B": lambda: scan(("pc", 256, 512), ("kr", 0, 256), ("dr", 0, 256), ("zz", 48, 49), True), "D": decode}
+        for step in CFG["front"].split():
+            q, step = step.split(":") if ":" in step else (None, step)
+            tag[:] = [t, "front " + step, len(ops)]
+            if step[0] == "g":
+                moved(q, int(step[1:]))
+            elif step[0] == "r":
+                r_rows(int(step[1:]))
+            elif step[0] == "t":
+                if not last:
+                    targets(t + 1, int(step[1:]))
+            else:
+                if step == "d":
+                    mark.append(len(ops))
+                front[step]()
 
         def source(a, b):
             gts(("src", a, b), ("tw", 0, 544), ("lst", a // 16, b // 16), 6143.0, A.add, 4095.0, A.min)
 
         def phase(a, b):
             gtt(("hw", a, b), ("tw", 0, 544), ("lst", a // 16, b // 16), ("mc", a, b), A.subtract)
-            if CFG["kq"][a == 0] == "a":
-                act(("kk", a, b), ("hw", a, b), F.Identity, ("hopf", 0, 4), scale=T.hopf[:, t:t + 1], bias=RND)
-            else:
-                ts(("kk", a, b), ("hw", a, b), T.hopf[:, t:t + 1], A.mult, RND, A.add, ("hopf", 0, 4))
 
-        def r_gather(m0, m1, now=False, q="x"):
-            gat(q, ("rg", m0, m1), rw, ("src", m0 // 16, m1 // 16), now=now)
+        def whole(q, a, b):
+            if q == "v":
+                ts(("kk", a, b), ("hw", a, b), T.hopf[:, t:t + 1], A.mult, RND, A.add, ("hopf", 0, 4))
+            else:
+                act(("kk", a, b), ("hw", a, b), F.Identity, ("hopf", 0, 4), scale=T.hopf[:, t:t + 1], bias=RND)
+
+        def turned_source():
+            if t:
+                p = ("pd", 512, 512 + QX)
+                mm(p, ("idf", 0, 128), ("mc", 256 - QX, 256), True, False, 4)
+                mm(p, ("idf", at, at + 128), ("hw", 256 - QX, 256), False, True, 4)
+                ts(("srt", 0, QX), p, 6143.0, A.add, 4095.0, A.min)
+
+        def r_gather(q, m0, m1):
+            gat(q, ("rg", m0, m1), rw, ("src", m0 // 16, m1 // 16))
+            if CFG["rp"]:
+                ops[-1]["r"] += [("rw%d" % r, 0, 1) for r in range(8)]
 
         def rot_of(ps, m0, m1):
             a, b = m0 // 16, m1 // 16
             p = (ps, 256 + a, 256 + b)
-            mm(p, ("dnf", 0, 128), ("kk", a, b), True, False, 4)
-            mm(p, ("idb", 0, 128), ("cm", 0, b - a), False, False)
-            mm(p, ("hd", 0, 128), ("hw", a, b), False, False, 4)
+            z = at if m0 >= W - X else 0
+            e0 = 15 + z
+            mm(p, ("idb", 0, 128), ("cm", 0, b - a), True, False)
+            mm(p, ("dnf", z, z + 128), ("kk", a, b), False, False, 4)
+            mm(p, ("hdt" if z else "hd", 0, 128), ("hw", a, b), False, False, 4)
             for r in range(16):
-                mm(p, ("er", 15 - r, 143 - r), ("rg", m0 + r, m1, 16), False, r == 15)
+                mm(p, ("er", e0 - r, e0 + 128 - r), ("rg", m0 + r, m1, 16), False, r == 15)
                 ops[-1]["r"][0] = ("rg", m0, m1)
-            if m0 >= W - X and last:
-                ts(("qi", 0, QX), p, up, A.add)
-                ts(("qi", 0, QX), ("qi", 0, QX), W - 1, A.bitwise_and)
-                cp(("xo", HX, HX + QX), ("qi", 0, QX))
-            elif m0 >= W - X:
-                cp(("xo", HX, HX + QX), p)
-            else:
-                ts(("q16", QX + a, QX + b), p, up, A.add)
+            join(16)
+            if m0 < W - X:
                 kept.append((("qf", QX + a, QX + b), p))
 
-        def t_gather(m0, m1, now=False, q="x"):
-            at = 0 if m0 < W - X else W - X if m0 < W - HX else W - XW
-            gat(q, ("xo" if at else "tb", m0 - at, m1 - at), win, ("src", m0 // 16, m1 // 16), now=now)
+        def t_gather(q, m0, m1):
+            o = 0 if m0 < W - X else W - X if m0 < W - X + HX else W - XW
+            if o and t and t >= CFG["tw"]:
+                gat(q, ("xo", m0 - o, m1 - o), ("sr", 0, W), ("srt", (m0 - W + X) // 16, (m1 - W + X) // 16))
+            else:
+                gat(q, (xt if o else "tb", m0 - o, m1 - o), win, ("src", m0 // 16, m1 // 16))
+            if not t:
+                ops[-1]["r"] += [("rw%d" % r, 0, 1) for r in range(8)]
 
-        def product(n0, n1, by="v"):
-            x = ("tb", n0 - X, n1 - X) if n0 >= X else (lq, n0, n1) if n0 < HX else (lq, n0 + QX, n1 + QX)
-            c = ("cr", 0, W) if last and n0 < X else ("cw", 0, (t // 2 * 2 + 3) * W)
-            off, out, n = ("q16", n0 // 16, n1 // 16), (new, PF + n0, PF + n1), n1 - n0
-            if by == "v":
-                gtt(out, c, off, x, A.mult)
-                return
-            h = "h%d" % (turnno[2] % 2)
-            turnno[2] += 1
-            gat("a", (h, 0, n), c, off)
-            parts = (n + 511) // 512
-            for j in range(parts):
-                a, b = n * j // parts, n * (j + 1) // parts
-                p = bank(b - a)
-                mm(p, ("idb", 0, 128), (h, a, b), True, True)
-                tt((new, out[1] + a, out[1] + b), (x[0], x[1] + a, x[1] + b), p, A.mult)
+        def product(n0, n1):
+            x = ("tb", n0 - X, n1 - X) if n0 >= X else (lt, n0, n1) if n0 < HX else (lt, n0 + QX, n1 + QX)
+            gtt((new, PF + n0, PF + n1), ("cw", 0, (t // 2 * 2 + 3) * W), ("q16", n0 // 16, n1 // 16), x, A.mult)
+
+        def records_of(n0, n1, k):
+            gat("a", ("h%d" % (n0 == 0), 0, n1 - n0), ("cw", 0, (t // 2 * 2 + 3) * W), ("q16", n0 // 16, n1 // 16))
+
+        def turn_in(n0, n1, k):
+            held[k] = ("pe%d" % (k % 2), 0, n1 - n0) if last else (("pc", "pr")[n0 == 0], 0, n1 - n0)
+            if t >= CFG["tw"] or not t:
+                mm(held[k], ("idb", 0, 128), ("h%d" % (n0 == 0), 0, n1 - n0), True, True)
+            else:
+                mm(held[k], ("idf", at, at + 128), (lq, n0, n1) if n0 < HX else (lq, n0 + QX, n1 + QX), True, True, 4)
+
+        def times(n0, n1, k):
+            if t >= CFG["tw"] or not t:
+                tt((new, PF + n0, PF + n1), (lt, n0, n1) if n0 < HX else (lt, n0 + QX, n1 + QX), held[k], A.mult)
+            else:
+                tt((new, PF + n0, PF + n1), ("h%d" % (k % 2), 0, n1 - n0), held[k], A.mult)
+
+        held = {}
 
         def send(k):
             a, b = PARTS[k]
             who = senders(t, core, nxt, T, topo)[k]
             to = nxt if who == core else who
             rid, pid, _ = topo.addr(to)
-            r0 = 16 * turned(t) if who == core else 0
-            land = ("lu%d" % t, 0, b - a) if r0 else (lq, a, b)
-            if who == core:
-                dsts, sem = [ap(land)], "arr%d_%d" % (t, k)
-            else:
-                dsts, sem = [T["hx%d_%d" % (t, k)][128 * j:128 * j + 128, :] for j in range(2 if turned(t) else 1)], "xa%d_%d" % (t, k)
-            x = RemoteDMATransfer(dst_ids=[DstId(rid=rid, pnc=pid)] * len(dsts), dma_engine_mask=topo.mask(core, to),
-                                  remote_sem=T.sem[sem], srcs=[T.xo[:, a:b]], dsts=dsts)
-            i = op("g", lambda e: e.remote_dma_fused([x], local_sem=T.sem["sx%d" % k]), [("xo", a, b)], [],
-                   1.0 + once(core), "sx%d" % k, len(topo.engines(core, to)), 1.0, len(dsts) * (b - a) / (300 if who == core else 1000))
-            op(None, None, [], [land], 0.0, "arr%d_%d" % (t, k), len(topo.engines(senders(t, prv, core, T, topo)[k], core)),
+            sem = ("arr%d_%d" if who == core else "xa%d_%d") % (t, k)
+            mask, n = topo.mask(core, to), len(topo.engines(core, to))
+            out, land = (("xo", a, b), (lq, a, b)) if a == HX else ((xt, a, b), (lt, a, b))
+            i = op("g", lambda e: e.remote_dma(ap(land), ap(out), T.sem[sem], T.sem["sx%d" % k], pid, rid, mask),
+                   [out], [], 1.0 + once(core), "sx%d" % k, n, 1.0, (b - a) / 500,
+                   fold=None if who == core else (who, n, sem, land, nxt, "arr%d_%d" % (t, k)))
+            ops[i]["follows"] = sent[-1:]
+            sent.append(i)
+            way = (b - a) / CFG["link"] / (2 if land[0] == "lb" else 1)
+            op("L" if who == core else "M", None, [], [land], way, "arr%d_%d" % (t, k), len(topo.engines(senders(t, prv, core, T, topo)[k], core)),
                CFG["far"] if who == core else CFG["arr"] + once(who), after=(i,))
-            if r0:
-                dma("s", T[lq][r0:128, a:b], T[land[0]][0:128 - r0, :], [land], [(lq, a, b, 2)], "trn", 250)
-                dma("s", T[lq][0:r0, a:b], T[land[0]][128 - r0:128, :], [land], [(lq, a + 1, b, 2)], "trn", 50)
+            if who == core:
+                ops[-1]["follows"] = landed[-1:]
+                landed.append(len(ops) - 1)
 
-        def top_bins(now):
-            q = "xxxx" if now else CFG["top"]
-            t_gather(W - X, W - HX, now, q[0])
-            send(0)
-            r_gather(W - X, W - HX, now, q[1])
-            r_gather(W - HX, W, now, q[2])
-            t_gather(W - HX, W, now, q[3])
-            rot_of("pr", W - X, W)
-            send(1)
+        def output(n0, n1, k):
+            y0, y1 = n0 % 2048, n0 % 2048 + n1 - n0
+            ps, x, out = "pd" if y0 < X else "pm", (new, PF + n0, PF + n1), ("vt", y0, y1)
+            by = CFG["yk"][k]
+            if by == "d" and n0 >= 2048:
+                dma("s", T.y[:, y0:y1], ap(x), [x], [("y", y0, y1)], "out%d" % k, (n1 - n0) / 2)
+                return
+            if by == "d":
+                op("g", lambda e: e.dma_start(T.y[:, y0:y1], ap(x), accum_op=A.add).then_inc(T.sem["zd%d" % (k % 4)], 16),
+                   [x], [("y", y0, y1)], 1.0, "zd%d" % (k % 4), 16, CFG["add"] - 1.0, (n1 - n0) / 600)
+                return
+            for a in range(y0, y1, 512):
+                b = min(a + 512, y1)
+                p, xs = (ps, a % X, a % X + b - a), (new, x[1] + a - y0, x[1] + b - y0)
+                if by == "a":
+                    act(p, xs)
+                elif n0 >= 2048:
+                    mm(p, ("idf", 0, 128), xs, True, by == "p", 4)
+                elif by == "v":
+                    tt(("vt", a, b), xs, p, A.add)
+                else:
+                    mm(p, ("idf", 0, 128), xs, False, True, 4)
+                    act(("vt", a, b), p)
+            if n0 < 2048:
+                dma("s", T.y[:, y0:y1], T.vt[:, y0:y1], [out], [("y", y0, y1)], "out%d" % k, (n1 - n0) / 2)
 
         yc = CFG["yc"]
-        cut = (W - X if last else CFG["cut"]) // 16
+        cut = CFG["cut"] // 16
+        tag[:] = [t, "sources", len(ops)]
         source(cut, 256)
         phase(cut, 256)
-        begun = len(ops) - 1
-        if last:
-            source(0, cut)
-            phase(0, cut)
         got = (lq, HX, HX + QX)
+        pieces = CFG["lp"] if last else list(zip(yc[1:], yc))
         if not last:
-            vc = [W] + [c + 4 for c in CFG["vc"]] + [0]
+            vc = [W] + [c + 4 for c in CFG.get("vc", yc)[1:-1]] + [0]
             route = CFG["route"][t]
-            for step in CFG["steps"].split():
-                k = int(step[1:] or 0)
-                if step == "t":
-                    top_bins(CFG["now"])
-                elif step == "s":
-                    source(0, cut)
-                elif step == "h":
-                    phase(0, cut)
-                elif step == "n":
-                    if CFG["tn"] != "c":
-                        targets(t + 1, begun)
-                elif step == "q":
-                    ts(("q16", 0, QX), got, up, A.add)
-                    act(("qf", 0, QX), got)
-                elif step == "c":
-                    for out, p in kept:
-                        act(out, p)
-                elif step[0] == "g":
-                    r_gather(yc[k + 1] - X, yc[k] - X, q=CFG["rq"][k])
-                    t_gather(yc[k + 1] - X, yc[k] - X, q=CFG["tq"][k])
-                    rot_of(("pc", "pr")[k % 2], yc[k + 1] - X, yc[k] - X)
-                elif step[0] == "p":
-                    product(yc[k + 1], yc[k], CFG["by"][k])
-                elif step[0] == "v" and route[k] in "FG":
-                    fold_out(new, PF, vc[k + 1], vc[k], k)
-                elif step[0] == "v":
-                    piece(new, PF, vc[k + 1], vc[k], route[k])
-                elif route[k] in "FG":
-                    judge(new, PF, vc[k + 1], vc[k], [("up", "bb", BB)], route[k])
-        else:
-            r0 = 16 * t
-
-            def early(n0, ps, at):
-                mm((ps, n0 % X, n0 % X + HX), ("idf", at, at + 128), (new, PF + n0, PF + n0 + HX), True, True, 4)
-
-            def store(n0, n1, ps, k):
-                y0, y1 = n0 % 2048, n0 % 2048 + n1 - n0
-                product(n0, n1)
-                out = ("vt", y0, y1)
-                tt(out, (new, PF + n0, PF + n1), (ps, y0 % X, y0 % X + n1 - n0), A.add)
-                if n0 >= X:
-                    dma("s", T.y[:, y0:y1], T.vt[:, y0:y1], [out], [("y", y0, y1)], "out%d" % k, (n1 - n0) / 2)
+            turnno[0] = len(route) % 2
+            votes = [piece(new, PF, vc[k + 1], vc[k], by) if by not in "FGH" else folded(new, vc[k + 1], vc[k], k) if by == "H" else
+                     {"e": lambda k=k: fold_out(new, PF, vc[k + 1], vc[k], k), "n": lambda: None, "m": lambda: None, "M": lambda: None,
+                      "f": lambda k=k, by=by: judge(new, PF, vc[k + 1], vc[k], [("up", "bb", BB)], by)} for k, by in enumerate(route)]
+        top = {"w": (W - X, W), "a": (W - X + HX, W), "b": (W - X, W - X + HX)}
+        for step in CFG["last" if last else "steps"].split():
+            q, step = step.split(":") if ":" in step else (None, step)
+            c, k = step[0], step[1:]
+            tag[:] = [t, ("last " if last else "") + step, len(ops)]
+            if c == "S":
+                source(0, cut)
+            elif c == "H":
+                phase(0, cut)
+            elif c == "K":
+                whole(q, 0, cut)
+            elif c == "k":
+                whole(q, cut, 256)
+            elif c == "U":
+                turned_source()
+            elif c == "C":
+                (act if q == "a" else cp)(("xo", HX, HX + QX), ("pd", 512 - QX, 512))
+            elif c == "R":
+                r_gather(q, *top[k])
+            elif c == "T":
+                t_gather(q, *top[k])
+            elif c == "Q":
+                rot_of("pd", W - X, W)
+            elif c == "X":
+                if last and k == "q":
+                    mark.append(len(ops))
+                send("baq".index(k))
+            elif c == "I":
+                ts(("q16", 0, QX), got, up, A.add)
+            elif c == "c":
+                for out, p in kept:
+                    act(out, p)
+            elif c == "D":
+                if t < 2:
+                    records(t + 3, (new, PF + yc[2], PF + yc[1]))
+            elif c == "E":
+                targets(t + 1, 5)
+            elif c == "J":
+                act(("qf", 0, QX), got)
+            elif c == "Z" and CFG["rp"]:
+                split("qf")
+            elif c == "Z":
+                gat("a", ("kp3", 16, 272), ("qf", 0, 256), LP)
+            elif c in "enmMf":
+                votes[int(k)][c]()
+            else:
+                n0, n1 = pieces[int(k)]
+                if c == "r":
+                    r_gather(q, n0 - X, n1 - X)
+                elif c == "t":
+                    t_gather(q, n0 - X, n1 - X)
+                elif c == "q":
+                    rot_of(("pc", "pr")[int(k) % 2], n0 - X, n1 - X)
+                elif c == "o":
+                    ts(("q16", n0 // 16, n1 // 16), (("pc", "pr")[int(k) % 2], 192 + n0 // 16, 192 + n1 // 16), up, A.add)
+                elif c == "p":
+                    if len(mark) % 2:
+                        mark.append(len(ops))
+                    product(n0, n1)
+                elif c == "g":
+                    records_of(n0, n1, int(k))
+                elif c == "P":
+                    times(n0, n1, int(k))
+                elif c == "u":
+                    turn_in(n0, n1, int(k))
                 else:
-                    dma("s", T.y[r0:128, y0:y1], T.vt[0:128 - r0, y0:y1], [out], [("y", y0, y1, 2)], "out%d" % k, (n1 - n0) / 4)
-                    dma("a", T.y[0:r0, y0:y1], T.vt[128 - r0:128, y0:y1], [out], [("y", y0 + 1, y1, 2)], "out%d" % k, (n1 - n0) / 4)
+                    output(n0, n1, int(k))
 
-            top_bins(True)
-            for j, a in enumerate(CFG["ls"]):
-                if a < 0:
-                    cp(("q16", 0, QX), got)
-                    for k, (n1, n0) in enumerate(zip(CFG["lc"], CFG["lc"][1:])):
-                        store(n0, n1, "pd", k)
-                    continue
-                for h in (a, a + HX):
-                    r_gather(h, h + HX)
-                for h in (a, a + HX):
-                    t_gather(h, h + HX)
-                rot_of(("pc", "pr")[j % 2], a, a + X)
-                x = (new, PF + a + X, PF + a + 2 * X)
-                if a == 2 * X and CFG["ya"] != "d":
-                    for k, (n1, n0) in enumerate(zip(CFG["ld"], CFG["ld"][1:])):
-                        store(3 * X + n0, 3 * X + n1, "pm", 4 + k)
-                    continue
-                for h in (a + X, a + X + HX):
-                    product(h, h + HX)
-                    if a == X:
-                        early(h, "pd", r0)
-                    elif CFG["ya"] == "v":
-                        early(h, "pm", 0)
-                    elif CFG["ya"] == "a":
-                        act(("pm", h % X, h % X + HX), (new, PF + h, PF + h + HX))
-                if CFG["ya"] == "d" and a == 0:
-                    dma("s", T.y[:, X:2 * X], ap(x), [x], [("y", X, 2 * X)], "out4", 512)
-                elif CFG["ya"] == "d" and a == 2 * X:
-                    op("g", lambda e, x=x: e.dma_start(T.y[:, X:2 * X], ap(x), accum_op=A.add).then_inc(T.sem.ya, 16),
-                       [x], [("y", X, 2 * X)], 1.0, "ya", 16, CFG["add"], 1.7)
-
+    mark = []
     for t in range(FR):
         frame(t)
+    for o in ops[kept_from:]:
+        o["now"] = "kept"
+    for k, i in enumerate(mark):
+        ops[i]["now"] = ("gate", "goal")[k % 2]
     return ops

@@ -1,148 +1,56 @@
+import math
 from concourse.bass import DstId, RemoteDMATransfer
-from concourse.mybir import AluOpType as A, ActivationFunctionType as F, AxisListType as AX
+from concourse.mybir import AluOpType as A, ActivationFunctionType as F
 
 W = 4096
 X = 1024
 FR = 4
 PF, PB = 8, 16
-HX, QX = 512, X // 16
+QX = X // 16
 XW = X + QX
-PARTS = [(0, HX), (HX + QX, XW), (HX, HX + QX)]
 BIG = float(2 ** 27)
 NONE = float(2 ** 26)
 RND = 1.5 * 2 ** 23
-BB = W // 2
 
 CFG = {
-    "cuts0": [0, 896, 1536, 2304, 3200, W], "route0": "XwXWW",
-    "yc": [W, 3584, 3072, 2432, 1728, X, 512, 0], "route": ["ZZZZZwv"] * 3, "strict": 1,
-    "front": "r1 z a:g0 v:g1 C a:g2 v:g3 a:g4 v:g5 a:g6 r2 r3 d e r4 r5 c L t1 R t2 x y t3 w t4 F B t5 h D",
-    "cut": 2048, "ya": "p", "lo": "a", "add": 3.0, "jc": 512, "jl": 0,
-    "steps": "a:Rw S H v:Tb Xb a:r0 v:Ta K Qw Xa v:t0 q0 a:r1 a:t1 p0 e0 q1 a:r2 p1 a:t2 e1 m0 q2 a:r3 m1 a:t3 p2 e2 q3 p3 n0 f0 n1 f1 e3 m2 n2 f2 I m3 f3 p4 e4 c p5 e5 m4 f4 m5 f5",
-    "lp": [(2048, 2560), (2560, 3072), (3072, W), (X, 1536), (1536, 2048), (512, X), (256, 512), (0, 256)],
-    "last": "a:Rw S H v:Tb Xb a:r0 v:Ta K Qw Xa v:t0 q0 a:r1 a:t1 p0 q1 a:r2 p1 v:t2 y0 y1 q2 a:r3 a:t3 p2 y2 q3 a:r4 a:t4 p3 q4 y3 p4 y4 I p5 y5 p6 y6 p7 y7",
-    "eps": [0.05, 0.2, 0.35], "short": 0.05, "loose": 0, "tries": 2000, "heat": 0.3, "seed": 1,
-    "xs": [0, 2, 5, 8, 11, 13, 14, 15, 16], "xq": "xxxxxxxx", "kl": 0, "tl": 0, "ai": 0, "fw": "p",
-    "ways": [(0.15, 1.0, 1.0, 1.0, 1.0), (0.12, 1.4, 1.0, 0.95, 0.8), (0.25, 1.2, 1.3, 1.25, 1.2)], "safe": 1.5, "dr": "v", "dc": 128,
-    "cy": 0.00088, "lat": 0.25, "arr": 5.0, "far": 2.0, "back": 3.5, "once": 3.0, "turns": 3, "ga": 1.45, "fv": 0.045,
+    "cuts0": [0, 384, 1392, 2400, 3408, W], "route0": "bbbbv",
+    "start": "m0 m1 M0 f0 M1 f1 t2 m2 M2 f2 m3 e4 M3 f3 t3 t4 t5 t6 t7 m4 t1 M4 f4",
+    "xs": [0, 1, 3, 5, 7, 9, 11, 13, 14, 15, 16],
+    "front": "z a:g0 v:g1 C a:g2 v:g3 a:g4 v:g5 a:g6 v:g7 a:g8 v:g9 r2 r3 t2 t1 r4 L R r5 t6 d x e y t3 w t4 F B h t5 t7 D",
+    "yc": [W, 3328, 2336, 1472, X, 512, 0], "route": ["NNNwwv"] * 3, "fw": 0, "ahead": "234", "jc": 456, "banks": [("pd", 0), ("pd", 512), ("pr", 0), ("pe0", 0)], "banks0": [("pd", 0), ("pd", 512), ("pr", 0)],
+    "steps": "a:r0 H v:k S v:K U v:Tb Xb q0 a:r1 v:Rc q1 v:Rd a:t0 o0 Qw v:Ta a:t1 o1 v:C Xq Xa D p0 e0 a:r2 p1 q2 n0 a:t2 m0 o2 e1 M0 f0 p2 a:r3 q3 n1 "
+             "a:t3 e2 n2 N0 m1 o3 I g3 u3 M1 f1 N1 c G2 m2 J g4 g5 u4 u5 M2 f2 P3 P4 e3 P5 e4 m3 Z m4 e5 M3 f3 M4 f4 m5 G3 M5 G4 f5",
+    "lp": [(3072, W), (2048, 3072), (1536, 2048), (X, 1536), (512, X), (0, 512)], "yk": "smddvv",
+    "last": "a:Rc v:k v:Rd U a:Ta v:Tb Xb Qw S v:C Xq Xa H a:r0 a:K q0 V:t0 a:r1 q1 o0 A:t1 p0 y0 a:r2 q2 o1 I p1 A:t2 y1 a:r3 q3 o2 A:t3 g4 u4 "
+            "p2 y2 o3 g5 u5 p3 y3 P4 P5 y4 y5",
+    "hx": [512] * FR, "own": [0], "cut": 2048, "dc": 128, "rc": 3, "hb": {(False, 3): ("pd", 512)}, "bb": 1.0,
+    "cy": 0.00083, "ga": 1.56, "fv": 0.03, "add": 2.9, "link": 240.0, "far": 0.3, "arr": 2.6, "back": 3.5, "once": 2.5, "lat": 0.25, "across": 0.6,
+    "ways": [(0.16, 1.0, 1.05, 1.0, 1.0, 1.0), (0.12, 1.1, 1.45, 1.05, 0.85, 1.2), (0.2, 1.3, 1.0, 1.0, 0.75, 2.0), (0.3, 1.1, 1.4, 1.35, 1.0, 1.2),
+             (0.12, 1.0, 1.2, 1.1, 1.25, 1.0)], "soon": 0.05,
+    "tries": [25000, 30000, 35000, 12000, 30000], "seed": [1, 1, 1, 1, 1], "heat": [0.1, 0.04, 0.04, 0.03, 0.1],
 }
-CFG.update(
-    xs=[0, 2, 4, 7, 10, 12, 14, 15, 16], lp=[(3584, W), (3072, 3584), (2048, 3072), (1536, 2048), (X, 1536), (512, X), (0, 512)],
-    yc=[W, 3584, 2688, 1696, X, 512, 0], route=["ZZZWwv"] * 3, far=1.2,
-    front="z A:g0 V:g1 C A:g2 V:g3 A:g4 V:g5 A:g6 V:g7 t2 r2 r3 t1 d e r4 r5 c L R t3 x y t4 w F B h t5 D",
-    steps="a:r0 v:k V:Tb Xb q0 A:t0 S H K o0 A:r1 q1 p0 e0 V:Ta A:t1 m0 o1 M0 A:Ra V:Rb p1 e1 Qw A:r2 q2 A:t2 v:C Xa m1 o2 M1 A:r3 q3 p2 e2 A:t3 o3 c p3 e3 n0 f0 n1 f1 n2 m2 M2 I f2 n3 g4 u4 g5 u5 m3 M3 f3 P4 e4 P5 e5 J Z m4 m5 M4 f4 M5 f5",
-    last="a:Rw v:k v:Tb Xb Qw v:Ta S v:C Xa H A:r0 K q0 V:t0 A:r1 q1 o0 A:r2 q2 p0 y0 V:t1 o1 A:t2 p1 y1 A:r3 q3 o2 V:t3 p2 y2 A:r4 q4 o3 V:t4 p3 y3 I g5 u5 o4 g6 u6 p4 y4 P5 P6 y5 y6",
-    ub=0, rf=0, rp=0, td=9, tw=9, seed=2, yk="ddaddvv", own=[0], route0="xXXXv", cuts0=[0, 576, 1584, 2592, 3600, W],
-    start="e0 e1 m0 m1 M0 f0 e2 M1 f1 e3 t2 m2 m3 M2 f2 e4 M3 f3 m4 t1 M4 f4 t3 t4 t5",
-    tries=[[5000, 9000, 9000, 9000, 8000]], heat=0.3, dr="a", ai=1, strict="va", cy=0.00083, ga=1.56, fv=0.05, arr=5.0, add=2.9, once=1.8,
-    ways=[(0.11, 1.0, 1.0, 1.0, 1.0), (0.11, 1.0, 1.6, 1.05, 0.85), (0.1, 1.3, 1.1, 1.0, 0.75), (0.15, 1.1, 1.45, 1.4, 1.0)])
-CFG.update(
-    tw=1, route0="xxxwv", route=["ZZZwwv"] * 3, yc=[W, 3456, 2464, 1472, X, 512, 0], tries=[[6000, 3000, 16000, 3000, 9000], [0, 2000, 0, 0, 0]],
-    link=130.0, far=0.3, arr=2.6, own=[], fv=0.04,
-    steps="a:r0 v:k U v:Tb Xb q0 a:t0 S H K o0 A:r1 q1 p0 e0 v:Ta Xa A:t1 m0 o1 M0 A:Ra V:Rb p1 e1 Qw A:r2 q2 A:t2 v:C Xq m1 o2 M1 A:r3 q3 p2 e2 A:t3 o3 c p3 e3 n0 f0 n1 f1 n2 m2 M2 I f2 n3 g4 u4 g5 u5 m3 M3 f3 P4 e4 P5 e5 J Z m4 m5 M4 f4 M5 f5",
-    last="a:Rw v:k U v:Tb Xb Qw v:Ta Xa S v:C Xq H A:r0 K q0 V:t0 A:r1 q1 o0 A:r2 q2 p0 y0 V:t1 o1 A:t2 p1 y1 A:r3 q3 o2 V:t3 p2 y2 A:r4 q4 o3 A:t4 p3 y3 o4 p4 y4 I p5 p6 y5 p7 y6 y7")
-CFG.update(rc=3, own=[0], once=2.5, across=0.6, fv=0.03,
-           ways=[(0.16, 1.0, 1.05, 1.0, 1.0), (0.12, 1.1, 1.45, 1.05, 0.85), (0.2, 1.3, 1.0, 1.0, 0.75), (0.3, 1.1, 1.4, 1.35, 1.0)])
-CFG.update(dr="v", front=CFG["front"].replace("d e", "E d e"), route0="xxxxv")
-CFG.update(seed=[2, 1, 1, 1, 4], tries=[[4000, 7000, 7000, 7000, 7000]], yk="ddaddvvv", lp=[(3584, W), (3072, 3584), (2048, 3072), (1536, 2048), (X, 1536), (512, X), (256, 512), (0, 256)])
 DONE = {}
 
-SCRATCH = {
-    "s0": ("sbuf", [128, W + 2 * PB], "bfloat16"),
-    "sa": ("sbuf", [128, W + 2 * PF], "float32"),
-    "sb": ("sbuf", [128, W + 2 * PF], "float32"),
-    "cw": ("sbuf", [128, (FR + 1) * W], "bfloat16"),
-    "srt": ("sbuf", [128, QX], "uint16"),
-    "sr": ("sbuf", [128, W], "float32"),
-    "hdt": ("sbuf", [128, 128], "float32"),
-    "tb": ("sbuf", [128, W - X], "float32"),
-    "xo": ("sbuf", [128, XW], "float32"),
-    "xb": ("sbuf", [128, XW], "bfloat16"),
-    "lb": ("sbuf", [128, XW], "bfloat16"),
-    "vt": ("sbuf", [128, W], "float32"),
-    "gv": ("sbuf", [128, W], "bfloat16"),
-    "rg": ("sbuf", [128, W], "bfloat16"),
-    "a0": ("sbuf", [128, 512], "float32"),
-    "a1": ("sbuf", [128, 512], "float32"),
-    "b0": ("sbuf", [128, 1024], "float32"),
-    "b1": ("sbuf", [128, 1024], "float32"),
-    "h0": ("sbuf", [128, 1024], "bfloat16"),
-    "h1": ("sbuf", [128, 1024], "bfloat16"),
-    "iti": ("sbuf", [128, 1024], "int32"),
-    "it16": ("sbuf", [128, 1024], "uint16"),
-    "el": ("sbuf", [128, 1024], "float32"),
-    "roti": ("sbuf", [128, 256], "int32"),
-    "hl": ("sbuf", [128, 512], "bfloat16"),
-    "hopi": ("sbuf", [128, 4], "int32"),
-    "hopf": ("sbuf", [128, 4], "float32"),
-    "kp": ("sbuf", [128, 288], "float32"),
-    "tw": ("sbuf", [128, 544], "float32"),
-    "kp2": ("sbuf", [128, 288], "float32"),
-    "tw2": ("sbuf", [128, 544], "float32"),
-    "kp3": ("sbuf", [128, 288], "float32"),
-    "tw3": ("sbuf", [128, 544], "float32"),
-    "dl": ("sbuf", [128, 256], "float32"),
-    "dr": ("sbuf", [128, 256], "float32"),
-    "elr": ("sbuf", [128, 256], "float32"),
-    "fg": ("sbuf", [128, 512], "float32"),
-    "xe": ("sbuf", [128, 32], "float32"),
-    "yy": ("sbuf", [128, 64], "float32"),
-    "zz": ("sbuf", [128, 64], "float32"),
-    "st": ("sbuf", [128, 32], "float32"),
-    "kl": ("sbuf", [128, 256], "float32"),
-    "kr": ("sbuf", [128, 256], "float32"),
-    "ki": ("sbuf", [128, 256], "int32"),
-    "pay": ("sbuf", [128, 256], "int32"),
-    "dd": ("sbuf", [128, 256], "int32"),
-    "src": ("sbuf", [128, 256], "uint16"),
-    "mc": ("sbuf", [128, 256], "float32"),
-    "hw": ("sbuf", [128, 256], "float32"),
-    "qb": ("sbuf", [128, 256], "float32"),
-    "hd": ("sbuf", [128, 128], "float32"),
-    "kk": ("sbuf", [128, 256], "float32"),
-    "qf": ("sbuf", [128, 256], "float32"),
-    "qi": ("sbuf", [128, 64], "int32"),
-    "q16": ("sbuf", [128, 256], "uint16"),
-    "cb": ("sbuf", [128, 256], "bfloat16"),
-    "cm": ("sbuf", [128, QX], "bfloat16"),
-    "ea": ("sbuf", [128, 144], "bfloat16"),
-    "ev": ("sbuf", [128, 144], "bfloat16"),
-    "b2": ("sbuf", [128, 1024], "float32"),
-    "b3": ("sbuf", [128, 1024], "float32"),
-    "er": ("sbuf", [128, 272], "bfloat16"),
-    "one": ("sbuf", [128, 16], "float32"),
-    "nil": ("sbuf", [128, 128], "float32"),
-    "idf": ("sbuf", [128, 256], "float32"),
-    "upf": ("sbuf", [128, 256], "float32"),
-    "dnf": ("sbuf", [128, 256], "float32"),
-    "idb": ("sbuf", [128, 128], "bfloat16"),
-    "upb": ("sbuf", [128, 128], "bfloat16"),
-    "dnb": ("sbuf", [128, 128], "bfloat16"),
-    "hfb": ("sbuf", [128, 128], "bfloat16"),
-    "e8": ("sbuf", [128, 32], "float32"),
-    "col": ("sbuf", [128, 2], "float32"),
-    "c1": ("sbuf", [128, 48], "int32"),
-    "c2": ("sbuf", [128, 48], "int32"),
-    "c3": ("sbuf", [128, 48], "int32"),
-    "c4": ("sbuf", [128, 48], "int32"),
-    "lst": ("sbuf", [128, 64], "uint16"),
-    "pe0": ("psum", [128, 512], "float32"),
-    "pe1": ("psum", [128, 512], "float32"),
-    "pm": ("psum", [128, 1024], "float32"),
-    "pd": ("psum", [128, 1024], "float32"),
-    "pc": ("psum", [128, 512], "float32"),
-    "pr": ("psum", [128, 512], "float32"),
-}
-for _t in range(FR):
-    SCRATCH["lq%d" % _t] = ("sbuf", [128, XW], "float32")
+SCRATCH = {name: ("sbuf", [128, n], kind) for kind, names in {
+    "float32": {"sa": W + 2 * PF, "sb": W + 2 * PF, "sr": W, "vt": W, "tb": W - X, "xo": XW, "lq0": QX, "lq1": XW, "lq2": XW, "lq3": XW,
+                "a0": 512, "a1": 512, "b0": 1024, "b1": 1024, "b2": 1024, "b3": 1024,
+                "el": 512, "rmp": 512, "nk": 512, "dl": 256, "dr": 256, "fg": 512, "xe": 32, "yy": 64, "zz": 64, "st": 32,
+                "kl": 256, "kr": 256, "kp": 288, "tw": 544, "kp2": 288, "tw2": 544, "kp3": 288, "tw3": 544,
+                "mc": 256, "hw": 256, "kk": 256, "qb": 256, "qf": 256, "hd": 128, "hdt": 128, "hopf": 4,
+                "one": 16, "nil": 128, "idf": 256, "upf": 256, "dnf": 256, "ngf": 128, "e8": 32, "col": 4},
+    "bfloat16": {"s0": W + 2 * PB, "cw": (FR + 1) * W, "xb": X, "lb": X, "gv": W, "rg": W, "h0": 1024, "h1": 1024, "hl": 512,
+                 "cb": 256, "cm": QX, "ea": 144, "ev": 144, "er": 272, "idb": 128, "upb": 128, "dnb": 128, "hfb": 128},
+    "int32": {"iti": 1024, "roti": 256, "hopi": 4, "ki": 256, "pay": 256, "dd": 256, "c1": 48, "c2": 48, "c3": 48, "c4": 48},
+    "uint16": {"it16": 1024, "src": 256, "srt": QX, "q16": 256, "lst": 64},
+}.items() for name, n in names.items()}
+PSUM = {"pe0": 512, "pe1": 512, "pm": 1024, "pd": 1024, "pc": 512, "pr": 512}
+SCRATCH.update({name: ("psum", [128, n], "float32") for name, n in PSUM.items()})
 
-NP = 8
-SEMAPHORES = (["cv", "ca", "cp", "cg", "hs"] + ["sx%d" % k for k in range(len(PARTS))]
-              + ["%s%d_%d" % (s, t, k) for s in ("xa", "arr") for t in range(FR) for k in range(len(PARTS))]
-              + ["ld%d" % k for k in range(6)] + ["ldc%d" % k for k in range(FR + 1)] + ["ldi0", "ldi1", "ldr", "ldh", "ldt0", "ldt1", "ldt2", "ldt3", "rwd", "trn", "zf", "zd0", "zd1", "zd2", "zd3"]
-              + ["out%d" % k for k in range(8)] + ["f%s%d" % (c, k) for c in "lab" for k in range(NP)])
-PSUM = ("pe0", "pe1", "pm", "pd", "pc", "pr")
+SEMAPHORES = (["cv", "ca", "cp", "cg", "hs", "fl", "fa", "fb", "ldi0", "ldi1", "ldr", "ldh", "rwd", "trn", "nkc", "nka"] + ["sx%d" % k for k in range(3)]
+              + ["%s%d_%d" % (s, t, k) for s in ("xa", "arr") for t in range(FR) for k in range(3)]
+              + ["ld%d" % k for k in range(6)] + ["ldc%d" % k for k in range(FR + 1)] + ["zd%d" % k for k in range(4)] + ["out%d" % k for k in range(8)])
 COUNTER = {"v": "cv", "a": "ca", "p": "cp", "g": "cg"}
+QUEUES = "vapgsLM"
 
 
 def hazards(ops):
@@ -162,10 +70,7 @@ def hazards(ops):
                 if ps and ops[j]["q"] != o["q"]:
                     d.add(j)
                 elif (wr or wr2) and lo < hi2 and lo2 < hi and not (ps and o["q"] == "p") and (lane is None or lane2 is None or lane == lane2):
-                    if CFG["loose"] and wr and not wr2 and o["q"] in ("v", "a") and ops[j]["q"] == o["q"] and not o["sem"] and not ops[j]["sem"]:
-                        s.add(j)
-                    else:
-                        d.add(j)
+                    d.add(j)
             if ps and o["q"] == "p":
                 if name in chain:
                     s.add(chain[name])
@@ -185,40 +90,34 @@ def hazards(ops):
 def arrange(ops, deps, soft):
     n, lat = len(ops), CFG["lat"]
     kids, parents = [[] for _ in range(n)], [sorted(deps[i] | soft[i]) for i in range(n)]
-    line = []
-    for q in CFG["strict"]:
+    for q in "va":
         mine = [i for i in range(n) if ops[i]["q"] == q and ops[i]["now"]]
-        line += [(i, j) for j, i in zip(mine, mine[1:]) if j not in parents[i]]
-    for i, j in line:
-        parents[i].append(j)
+        for j, i in zip(mine, mine[1:]):
+            if j not in parents[i]:
+                parents[i].append(j)
     for i in range(n):
         for j in parents[i]:
             kids[j].append(i)
+    queue = [o["q"] or "" for o in ops]
 
-    def lay(rank, queue, back, eps):
+    def lay(rank, back):
         before, after = (kids, parents) if back else (parents, kids)
         left = [len(x) for x in before]
-        free, order, can, end, took = {}, [], [0.0] * n, [0.0] * n, list(queue)
-        ready = {q: [] for q in set(queue) | set("av")}
+        free, order, can, end = {}, [], [0.0] * n, [0.0] * n
+        ready = {q: [] for q in set(queue)}
         for i in range(n):
             if not left[i]:
                 ready[queue[i]].append(i)
         while len(order) < n:
-            t, q = min((max(min(can[i] for i in r), free.get(x, 0.0)), x) for y, r in ready.items() if r for x in ("av" if y == "x" else [y]))
-            mine = ready[q] + (ready.get("x", []) if q in ("a", "v") else [])
-
-            def place(k):
-                return (q == "v" and queue[k] == "x", rank[k], k)
-
-            i = min([k for k in mine if can[k] <= t + eps], key=place)
+            t, q = min((max(min(can[i] for i in r), free.get(x, 0.0)), x) for x, r in ready.items() if r)
+            i = min([k for k in ready[q] if can[k] <= t + 0.2], key=lambda k: (rank[k], k))
             if can[i] > t + 0.02:
-                short = [k for k in mine if max(t, can[k]) + ops[k]["c"] <= can[i] + CFG["short"]]
-                i = min(short, key=place) if short else i
-            ready[queue[i]].remove(i)
+                short = [k for k in ready[q] if max(t, can[k]) + ops[k]["c"] <= can[i] + 0.05]
+                i = min(short, key=lambda k: (rank[k], k)) if short else i
+            ready[q].remove(i)
             order.append(i)
             o = ops[i]
             t = max(can[i], free.get(q, 0.0)) + o["c"]
-            took[i] = q
             if q:
                 free[q] = t
             if not back:
@@ -229,195 +128,215 @@ def arrange(ops, deps, soft):
             end[i] = t
             for k in after[i]:
                 if (k in deps[i]) if back else (i in deps[k]):
-                    can[k] = max(can[k], t + lat + (ops[k]["l"] * CFG["safe"] + ops[k]["d"] if back else 0.0))
+                    can[k] = max(can[k], t + lat + (ops[k]["l"] * 1.5 + ops[k]["d"] if back else 0.0))
                 left[k] -= 1
                 if not left[k]:
                     ready[queue[k]].append(k)
-        return max(end), order, took, end
+        return order, end
 
-    def replay(order, took, wake, dma, pe):
-        free, end = {}, [0.0] * n
-        for i in order:
-            o, q = ops[i], took[i]
-            t = max([free.get(q, 0.0) if q else 0.0] + [end[j] + wake for j in deps[i]]) + o["c"] * (pe if q == "p" else 1.0)
-            free[q] = t
-            t += o["l"] * dma
-            if o["d"]:
-                t = free["e"] = max(t, free.get("e", 0.0)) + o["d"] * dma
-            end[i] = t
-        return max(end)
-
-    queue = [o["q"] or "" for o in ops]
-    best = None
-    for eps in CFG["eps"]:
-        now = lay([o["p"] for o in ops], queue, False, eps)
-        best = min(best or now, now) if not CFG["turns"] else best
-        for _ in range(CFG["turns"]):
-            now = lay([-e for e in lay([-e for e in now[3]], now[2], True, eps)[3]], queue, False, eps)
-            now = (sum(replay(now[1], now[2], *w[:3]) for w in CFG["ways"]),) + now[1:]
-            best = min(best or now, now)
-    order = list(best[1])
-    for i, j in line:
-        parents[i].remove(j)
-        kids[j].remove(i)
-    order, took = polish(ops, deps, parents, kids, order, list(best[2]))
-    for o, q in zip(ops, took):
-        o["q"] = q or None
-    return order
+    end = lay([o["p"] for o in ops], False)[1]
+    order = lay([-e for e in lay([-e for e in end], True)[1]], False)[0]
+    return polish(ops, deps, soft, order)
 
 
-def polish(ops, deps, parents, kids, order, took):
-    n, ways = len(ops), CFG["ways"]
-    dep = [sorted(d) for d in deps]
-    free = [o.get("free", False) for o in ops]
-    cost = [[o["c"] * (pe if o["q"] == "p" else 1.0 if o["q"] in ("g", "s") else dma if o["q"] in ("L", "M") else cy) + o["g"] * cy * (ga - 1.0) for o in ops] for wake, dma, pe, cy, ga in ways]
-    tail = [[o["l"] * w[1] for o in ops] for w in ways]
-    move = [[o["d"] * w[1] for o in ops] for w in ways]
-
-    state = [([0.0] * n, {}, 0.0) for _ in ways]
-
-    def run(order, took, goal, keep=False):
-        total, why = 0.0, []
-        for x, (w, c, l, d) in enumerate(zip(ways, cost, tail, move)):
-            end, at, e = state[x]
-            wake, across, at, last, by, ej = w[0], CFG["across"] * w[0], dict(at), {}, {}, -1
-            for i in order:
-                q = took[i]
-                t, b = at.get(q, 0.0), last.get(q, -1)
-                for j in dep[i]:
-                    x1 = end[j] if took[j] == q else end[j] + across
-                    if x1 > t:
-                        t, b = x1, j
-                t += c[i] + (0.015 if free[i] and q == "a" else 0.0)
-                if q:
-                    at[q], last[q] = t, i
-                t += l[i]
-                if d[i]:
-                    if e > t:
-                        t, b = e, ej
-                    t += d[i]
-                    e, ej = t, i
-                end[i], by[i] = t + wake, b
-            top = goal if goal >= 0 else max(order, key=lambda i: end[i])
-            total += end[top] / w[3]
-            why.append((top, by))
-            if keep:
-                state[x] = (end, at, e)
-        return total, why
-
-    def before(order, place, i, j):
-        need, todo = {i}, [i]
-        while todo:
-            for k in parents[todo.pop()]:
-                if place.get(k, -1) >= place[j] and k not in need:
-                    if k == j:
-                        return None
-                    need.add(k)
-                    todo.append(k)
-        a, b = place[j], place[i] + 1
-        return order[:a] + [k for k in order[a:b] if k in need] + [k for k in order[a:b] if k not in need] + order[b:]
-
-    def behind(order, place, j, i):
-        need, todo = {j}, [j]
-        while todo:
-            for k in kids[todo.pop()]:
-                if place.get(k, n) <= place[i] and k not in need:
-                    if k == i:
-                        return None
-                    need.add(k)
-                    todo.append(k)
-        a, b = place[j], place[i] + 1
-        return order[:a] + [k for k in order[a:b] if k not in need] + [k for k in order[a:b] if k in need] + order[b:]
-
+def polish(ops, deps, soft, order):
+    dep, above = [], []
+    for i in range(len(ops)):
+        far = 0
+        for j in deps[i]:
+            far |= above[j]
+        dep.append([j for j in sorted(deps[i]) if not far >> j & 1])
+        above.append(far | sum(1 << j for j in deps[i]))
+    ways = CFG["ways"]
+    ended = [{} for _ in ways]
+    state = [[0.0] * 9 for _ in ways]
+    began = [0.0] * len(ways)
     seed = [0]
 
-    def draw(k):
+    def draw():
         seed[0] = (seed[0] * 1103515245 + 12345) % 2 ** 31
-        return (seed[0] >> 8) % k
+        return (seed[0] >> 6) / 2.0 ** 25
 
-    def stretch(order, took, goal, tries):
-        now, why = run(order, took, goal)
-        best, place = (now, order, took), None
+    def stretch(win, k, model):
+        n, final = len(win), k == FR
+        loc = {g: x for x, g in enumerate(win)}
+        took = [QUEUES.index(ops[g]["q"]) if ops[g]["q"] else 7 for g in win]
+        free = [x for x, g in enumerate(win) if ops[g].get("free")]
+        par = [sorted(loc[j] for j in deps[g] | soft[g] if j in loc) for g in win]
+        kid = [[] for _ in win]
+        for x, p in enumerate(par):
+            for j in p:
+                kid[j].append(x)
+        dl = [[loc[j] for j in dep[g] if j in loc] for g in win]
+        sets = []
+        for (wake, dma, pe, cy, ga, link), end in zip(ways, ended):
+            rate = {"p": pe, "g": 1.0, "s": 1.0, "L": link, "M": link}
+            sets.append((wake, CFG["across"] * wake, [max([end[j] + CFG["across"] * wake for j in dep[g] if j not in loc] + [0.0]) for g in win],
+                         [ops[g]["c"] * rate.get(ops[g]["q"], cy) + ops[g]["g"] * cy * (ga - 1.0) for g in win],
+                         [ops[g]["l"] * dma for g in win], [ops[g]["d"] * dma for g in win], cy))
+        snaps = [[s[:]] + [None] * n for s in state]
+
+        def run(seq, a, ends, keep):
+            total, out = 0.0, []
+            for x, (wake, across, rel, c, l, d, cy) in enumerate(sets):
+                end, sn = ends[x][:], snaps[x]
+                at = sn[a][:]
+                for p in range(a, n):
+                    i = seq[p]
+                    if keep:
+                        sn[p] = at[:]
+                    q = took[i]
+                    t = at[q]
+                    if rel[i] > t:
+                        t = rel[i]
+                    for j in dl[i]:
+                        y = end[j] if took[j] == q else end[j] + across
+                        if y > t:
+                            t = y
+                    t += c[i]
+                    if q != 7:
+                        at[q] = t
+                    if l[i]:
+                        t += l[i]
+                        if d[i]:
+                            if at[8] > t:
+                                t = at[8]
+                            t += d[i]
+                            at[8] = t
+                    end[i] = t + wake
+                if keep:
+                    sn[n] = at
+                total += ((max(end) if final else end[n - 1]) - began[x] + CFG["soon"] * (sum(end) / n - began[x])) / cy
+                out.append(end)
+            return total / len(sets), out
+
+        def longest(x):
+            wake, across, rel, c, l, d, cy = sets[x]
+            end, path = ends[x], []
+            i = max(range(n), key=lambda z: end[z]) if final else n - 1
+            while i >= 0:
+                p, q, b, t = pos[i], took[i], -1, rel[i]
+                for j in dl[i]:
+                    y = end[j] if took[j] == q else end[j] + across
+                    if y > t:
+                        t, b = y, j
+                sn = snaps[x][p]
+                line = q != 7 and sn[q] > t
+                move = d[i] and sn[8] > max(t, sn[q]) + c[i] + l[i]
+                if line or move:
+                    z = p - 1
+                    while z >= 0 and not (d[seq[z]] if move else took[seq[z]] == q):
+                        z -= 1
+                    b = seq[z] if z >= 0 else -1
+                    if b >= 0:
+                        path.append((b, i))
+                i = b
+            return path
+
+        name = [(ops[g]["key"][0] - k,) + ops[g]["key"][1:] for g in win]
+        seq, ends = list(range(n)), [[0.0] * n for _ in ways]
+        now = run(seq, 0, ends, False)[0]
+        if model:
+            rank, r, mine = [], -1.0, took[:]
+            for x in range(n):
+                r = model[name[x]][0] if name[x] in model else r + 0.001
+                rank.append(r)
+            for x in free:
+                took[x] = model[name[x]][1] if name[x] in model else took[x]
+            left, like = [len(p) for p in par], []
+            ready = [x for x in range(n) if not left[x]]
+            while ready:
+                i = min(ready, key=lambda z: rank[z] if z < n - 1 or final else n)
+                ready.remove(i)
+                like.append(i)
+                for z in kid[i]:
+                    left[z] -= 1
+                    if not left[z]:
+                        ready.append(z)
+            if run(like, 0, ends, False)[0] < now:
+                seq = like
+            else:
+                took[:] = mine
+        now, ends = run(seq, 0, ends, True)
+        best, pos, paths = (now, seq, took[:]), [0] * n, {}
+        for p, i in enumerate(seq):
+            pos[i] = p
+        seed[0], tries = CFG["seed"][k], CFG["tries"][k]
         for step in range(tries):
-            i, by = why[draw(len(ways))]
-            path = []
-            while by.get(i, -1) in by:
-                if by[i] not in deps[i] or free[i]:
-                    path.append((by[i], i))
-                i = by[i]
-            if not path:
-                break
-            j, i = path[draw(len(path))]
-            if place is None:
-                place = {k: x for x, k in enumerate(order)}
-            new, eng, kind = None, took, draw(10)
-            if kind >= 8:
-                j = order[draw(len(order))]
-                mates = [k for k in order[place[j] + 1:place[j] + 40] if took[k] == took[j]][:2]
-                if mates and took[j]:
-                    i = mates[draw(len(mates))]
-                    new = before(order, place, i, j) if kind % 2 else behind(order, place, j, i)
-            elif kind < 2 and (free[i] or free[j]):
-                k = i if free[i] and (kind or not free[j]) else j
-                new, eng = order, list(took)
-                eng[k] = "av"[took[k] == "a"]
-            elif j not in deps[i]:
-                if kind == 7:
-                    mates = [k for k in order[max(0, place[j] - 40):place[j]] if took[k] == took[i]]
-                    j = mates[-1] if mates else j
-                new = before(order, place, i, j) if kind % 2 else behind(order, place, j, i)
-            if new is None:
-                continue
-            got, how = run(new, eng, goal)
-            if got <= now + CFG["heat"] * (1.0 - step / tries) * draw(100) / 100.0:
-                now, why, order, took, place = got, how, new, eng, None
+            u, flip = draw(), []
+            if u < 0.06 and free:
+                flip = [free[int(draw() * len(free))]]
+                z = free[int(draw() * len(free))]
+                if u < 0.03 and took[z] != took[flip[0]]:
+                    flip.append(z)
+                for z in flip:
+                    took[z] = 1 - took[z]
+                new, a = seq, min(pos[z] for z in flip)
+            elif u < 0.7:
+                x = int(draw() * len(ways))
+                if x not in paths:
+                    paths[x] = longest(x)
+                if not paths[x]:
+                    continue
+                j, i = paths[x][int(draw() * len(paths[x]))]
+                if draw() < 0.25:
+                    z = pos[j] - 1
+                    while z >= 0 and took[seq[z]] != took[j]:
+                        z -= 1
+                    j = seq[z] if z >= 0 else j
+                a, b, ahead = pos[j], pos[i] + 1, draw() < 0.5
+                need = {i if ahead else j}
+                todo = list(need)
+                while todo:
+                    for z in (par if ahead else kid)[todo.pop()]:
+                        if a <= pos[z] < b and z not in need:
+                            need.add(z)
+                            todo.append(z)
+                if (i in need and j in need) or (n - 1 in need and ahead and not final):
+                    continue
+                one, two = [z for z in seq[a:b] if z in need], [z for z in seq[a:b] if z not in need]
+                new = seq[:a] + (one + two if ahead else two + one) + seq[b:]
+                if new[-1] != n - 1 and not final:
+                    continue
+            else:
+                i = int(draw() * (n if final else n - 1))
+                p, q, d = pos[i], took[i], sets[0][5]
+                lo = max([pos[j] for j in par[i]] + [-1]) + 1
+                hi = min([pos[j] for j in kid[i]] + [n if final else n - 1]) - 1
+                mates = sorted((abs(z - p), z) for z in range(max(lo, p - 25), min(hi, p + 25) + 1) if z != p and (took[seq[z]] == q or (d[i] and d[seq[z]])))
+                z = mates[min(len(mates) - 1, int(-math.log(1.0 - draw()) / 0.6))][1] if mates else lo if u < 0.85 else hi
+                if z == p:
+                    continue
+                new = seq[:p] + seq[p + 1:]
+                new.insert(z, i)
+                a = min(p, z)
+            got = run(new, a, ends, False)[0]
+            if got <= now or draw() < math.exp((now - got) / (CFG["heat"][k] * (1.0 - step / tries) ** 2 + 0.003)):
+                now, seq, paths = got, new, {}
+                ends = run(seq, a, ends, True)[1]
+                for p in range(a, n):
+                    pos[seq[p]] = p
                 if now < best[0]:
-                    best = (now, order, took)
-        return best[1], best[2]
+                    best = (now, seq, took[:])
+            else:
+                for z in flip:
+                    took[z] = 1 - took[z]
+        now, seq, took[:] = best
+        ends, was = run(seq, 0, ends, True)[1], began[:]
+        for x in range(len(ways)):
+            ended[x].update(zip(win, ends[x]))
+            state[x], began[x] = snaps[x][n], ends[x][n - 1]
+        for x in free:
+            ops[win[x]]["q"] = QUEUES[took[x]]
+        DONE["stretch %d" % k] = sum(((max(e) if final else e[n - 1]) - b) / w[3] for e, b, w in zip(ends, was, ways)) / len(ways)
+        return [win[i] for i in seq], {name[i]: (float(p), took[i]) for p, i in enumerate(seq)}
 
-    def like(part, took, model, t):
-        rank, r, took = {}, -1.0, list(took)
-        for i in part:
-            x = model.get((ops[i]["key"][0] - t,) + ops[i]["key"][1:])
-            r = x[0] if x else r + 0.001
-            rank[i] = r
-            if x and free[i]:
-                took[i] = x[1]
-        left = {i: sum(j in rank for j in parents[i]) for i in part}
-        ready, out = [i for i in part if not left[i]], []
-        while ready:
-            i = min(ready, key=lambda k: rank[k])
-            ready.remove(i)
-            out.append(i)
-            for k in kids[i]:
-                if k in left:
-                    left[k] -= 1
-                    if not left[k]:
-                        ready.append(k)
-        return out, took
-
-    gates = [i for i in range(n) if ops[i]["now"] == "gate"]
-    model, whole = None, order
-    for turn in CFG["tries"]:
-        done, order = [], whole
-        state[:] = [([0.0] * n, {}, 0.0) for _ in ways]
-        for t, (gate, goal, tries) in enumerate(zip(gates + [-1], [i for i in range(n) if ops[i]["now"] == "goal"] + [-1], turn)):
-            b = order.index(goal) + 1 if goal >= 0 else len(order)
-            part = order[:b]
-            if model and 0 < t < FR:
-                other = like(part, took, model, t)
-                if run(other[0], other[1], goal)[0] < run(part, took, goal)[0]:
-                    part, took = other
-            seed[0] = CFG["seed"][t]
-            part, took = stretch(part, took, goal, tries)
-            if t == 2:
-                model = {(ops[i]["key"][0] - t,) + ops[i]["key"][1:]: (float(x), took[i]) for x, i in enumerate(part)}
-            order = part + order[b:]
-            a = order.index(gate) if gate >= 0 else len(order)
-            run(order[:a], took, -1, True)
-            done, order = done + order[:a], order[a:]
-        whole = done
-    return whole, took
+    cuts = [0] + [p + 1 for p, i in enumerate(order) if ops[i]["now"] == "gate"] + [len(order)]
+    done, model = [], None
+    for k in range(FR + 1):
+        part, found = stretch(order[cuts[k]:cuts[k + 1]], k, model)
+        done, model = done + part, found if k else None
+    return done
 
 
 def emit(g, T, ops, deps, order):
@@ -467,11 +386,11 @@ def helpers(core, nxt, T, topo):
     near = [c for c in others if topo.die(c) == topo.die(core)]
     far = [c for c in others if topo.die(c) != topo.die(core)]
     out = [[c for c in far if topo.may_write(c, nxt)][0], [c for c in near if topo.may_write(c, nxt)][0]]
-    return out, [c for c in near if c not in out][:2]
+    return out + [c for c in near if c not in out][:1]
 
 
 def senders(t, core, nxt, T, topo):
-    ports = helpers(core, nxt, T, topo)[0]
+    ports = helpers(core, nxt, T, topo)
     near = core if topo.may_write(core, nxt) else ports[1]
     return [near if t in CFG["own"] else ports[0], near, near]
 
@@ -479,34 +398,37 @@ def senders(t, core, nxt, T, topo):
 def rank_program(g, core, T, topo):
     n_ranks = len(T.cores)
     for rank, rc in enumerate(T.cores):
-        nxt = T.cores[(rank + 1) % n_ranks]
-        ports, turns = helpers(rc, nxt, T, topo)
-        if core == rc or core in turns or core in ports:
+        if core == rc or core in helpers(rc, T.cores[(rank + 1) % n_ranks], T, topo):
             ops = build(rc, T, topo)
             deps, soft = hazards(ops)
-            key = repr(CFG)
-            if key not in DONE:
-                DONE[key] = (arrange(ops, deps, soft), [o["q"] for o in ops])
-            order = DONE[key][0]
-            for o, q in zip(ops, DONE[key][1]):
+            if "order" not in DONE:
+                DONE["order"] = (arrange(ops, deps, soft), [o["q"] for o in ops])
+            order, took = DONE["order"]
+            for o, q in zip(ops, took):
                 o["q"] = q
             if core == rc:
                 emit(g, T, ops, deps, order)
             else:
-                hand_on(g, core, rc, [ops[i]["fold"] for i in order if ops[i]["fold"]], T, topo)
+                hand_on(g, core, rc, T.cores[(rank + 1) % n_ranks], [ops[i]["fold"] for i in order if ops[i]["fold"]], T, topo)
 
 
-def hand_on(g, core, rc, jobs, T, topo):
+def hand_on(g, core, rc, nxt, jobs, T, topo):
     got, sent = {}, 0
     for who, n, came, (buf, a, b), to, sem in jobs:
         if who == core:
             rid, pid, _ = topo.addr(to)
             got[came] = got.get(came, 0) + n
             g.wait_ge(T.sem[came], got[came])
-            g.remote_dma(T[buf][:, a:b], T[buf][:, a:b], T.sem[sem], T.sem.hs, pid, rid, topo.mask(core, to))
-            sent += len(topo.engines(core, to))
+            engines = spare(core, rc, nxt, topo) if to == rc else topo.engines(core, to)
+            g.remote_dma(T[buf][:, a:b], T[buf][:, a:b], T.sem[sem], T.sem.hs, pid, rid, sum(1 << e for e in engines))
+            sent += len(engines)
     if sent:
         g.wait_ge(T.sem.hs, sent)
+
+
+def spare(core, rc, nxt, topo):
+    off = topo.engines(core, nxt) if topo.may_write(core, nxt) else []
+    return [e for e in topo.engines(core, rc) if e not in off]
 
 
 def build(core, T, topo):
@@ -514,13 +436,12 @@ def build(core, T, topo):
     rank = T.rank_of(core)
     nxt = T.cores[(rank + 1) % n_ranks]
     prv = T.cores[(rank - 1) % n_ranks]
-    turns = helpers(core, nxt, T, topo)[1]
     cy, GA = CFG["cy"], CFG["ga"]
     ops, lag, firsts, tag = [], [0], set(), [-9, "", 0]
 
-    def op(q, f, r, w, c, sem=None, n=0, l=0.0, d=0.0, after=(), fold=None, now=False, g=0.0):
+    def op(q, f, r, w, c, sem=None, n=0, l=0.0, d=0.0, after=(), fold=None, g=0.0):
         ops.append({"q": q, "f": f, "r": r, "w": w, "c": c, "sem": sem, "n": n, "l": l, "d": d, "after": after, "fold": fold,
-                    "now": now, "p": len(ops) + lag[0], "g": g, "key": (tag[0], tag[1], len(ops) - tag[2])})
+                    "now": False, "p": len(ops) + lag[0], "g": g, "key": (tag[0], tag[1], len(ops) - tag[2])})
         return len(ops) - 1
 
     def join(k):
@@ -551,8 +472,11 @@ def build(core, T, topo):
     def dma(q, out, in_, r, w, sem, kb):
         op(q, lambda e: e.dma_start(out, in_).then_inc(T.sem[sem], 16), r, w, 0.08, sem, 16, 1.5, 0.2 + kb / 600)
 
-    def tt(out, a, b, alu):
-        op("v", lambda e: e.tensor_tensor(ap(out), ap(a), ap(b), alu), [a, b], [out], cost(out, 1 if a[0] in PSUM or b[0] in PSUM else 2))
+    def adding(out, in_, r, w, sem, d):
+        op("g", lambda e: e.dma_start(out, in_, accum_op=A.add).then_inc(T.sem[sem], 16), r, w, 1.0 + once("g") / 3, sem, 16, CFG["add"] - 1.0, d)
+
+    def tt(out, a, b, alu, k=2):
+        op("v", lambda e: e.tensor_tensor(ap(out), ap(a), ap(b), alu), [a, b], [out], cost(out, 1 if a[0] in PSUM or b[0] in PSUM else k))
 
     def ts(out, a, s1, o1, s2=None, o2=None, col=None):
         if o2 is None:
@@ -572,18 +496,18 @@ def build(core, T, topo):
     def tr(out, a):
         op("v", lambda e: e.transpose(ap(out), ap(a)), [a], [out], cost(out))
 
-    def gat(q, out, win, off, func=F.Copy, now=False, **k):
+    def gat(q, out, win, off, func=F.Copy, **k):
         i = len(ops)
 
         def call(e):
             if ops[i]["q"] == "a":
                 return e.activation(ap(out), ind(win, off), func, **k)
             if func == F.Sign:
-                return e.tensor_scalar(ap(out), ind(win, off), 0.0, 0.5, A.is_le, A.subtract)
+                return e.tensor_scalar(ap(out), ind(win, off), 0.0, 0.5, A.is_ge, A.subtract)
             return e.tensor_copy(ap(out), ind(win, off))
 
-        op(q.lower(), call, [win, off], [out], cost(out, GA), now=now, g=size(out) * GA * cy)
-        ops[i]["free"] = q in "xAV"
+        op(q.lower(), call, [win, off], [out], cost(out, GA), g=size(out) * GA * cy)
+        ops[i]["free"] = q in "AV"
 
     def gts(out, win, off, s1, o1, s2, o2):
         op("v", lambda e: e.tensor_scalar(ap(out), ind(win, off), s1, s2, o1, o2), [win, off], [out], cost(out, GA), g=size(out) * GA * cy)
@@ -645,10 +569,8 @@ def build(core, T, topo):
         pick(out, ("nil", 0, size(out)), [[0, size(out)]], A.not_equal, 0, 0, c)
 
     diag(("idb", 0, 128), 1.0)
-    act(("dnb", 0, 128), ("idb", 0, 128), scale=-4096.0)
-    act(("hfb", 0, 128), ("idb", 0, 128), scale=2048.0)
-    if "W" in CFG["route0"].upper():
-        act(("upb", 0, 128), ("idb", 0, 128), scale=4096.0)
+    act(("upb", 0, 128), ("idb", 0, 128), scale=4096.0)
+    act(("hfb", 0, 128), ("idb", 0, 128), scale=-2048.0)
     lag[0] = 400
     fill(("one", 0, 8), 1.0)
     fill(("one", 8, 16), -BIG)
@@ -660,31 +582,32 @@ def build(core, T, topo):
     iota(("c2", 16, 32), [[1, 16]], 0, 0)
     iota(("c3", 0, 16), [[1, 16]], 0, 0)
     iota(("c3", 16, 32), [[16, 16]], 0, 0)
-    for kp in ("kp2", "kp", "kp3"):
-        const((kp, 0, 16), 0.0)
-        const((kp, 272, 288), 0.0)
-        lag[0] = 600
+    const(("kp2", 0, 16), 0.0)
+    const(("kp2", 272, 288), 0.0)
+    diag(("idf", 0, 128), 1.0)
+    diag(("ngf", 0, 128), -1.0)
+    iota(("rmp", 256, 512), [[8192, 256]], 0, 0, True)
     lag[0] = 450
     pick(("e8", 16, 24), ("one", 8, 16), [[-16, 8]], A.is_ge, 0, 1)
     pick(("ea", 15, 143, 16), ("e8", 16, 24), [[16, 8]], A.is_ge, 15, -1)
-    const(("vt", 0, 1), -1.0)
+    const(("vt", 0, 1), 1.0)
     pick(("e8", 0, 8), ("one", 0, 8), [[-16, 8]], A.is_equal, 0, 1)
     pick(("e8", 8, 16), ("one", 0, 8), [[-16, 8]], A.is_equal, -15, 1)
     iota(("kl", 1, 256), [[0, 255]], 8192, 0, True)
     iota(("kr", 1, 256), [[0, 255]], 8192, 0, True)
-    const(("st", 0, 32), float(2 ** 21))
+    const(("st", 0, 32), 0.0)
     const(("yy", 0, 64), NONE)
     const(("st", 16, 17), BIG)
     act(("ev", 0, 144), ("ea", 0, 144), scale=2.0)
     lag[0] = 600
+    for kp in ("kp", "kp3"):
+        const((kp, 0, 16), 0.0)
+        const((kp, 272, 288), 0.0)
     iota(("mc", 0, 256), [[16, 256]], -6143, 0, True)
     const(("cm", 0, QX), W * RND)
-    if CFG["rp"]:
-        lag[0] = 900
-        iota(("eh", 0, 2064), [[0, 2064]], 0, 0, True)
-        pick(("eh", 16, 2064, 16), ("nil", 0, 128), [[-1, 16], [-16, 8]], A.not_equal, 0, 1, 1.0)
-        lag[0] = 600
-    for name, c in (("dnf", -4096.0), ("upf", 4096.0), ("idf", 1.0)):
+    diag(("dnb", 0, 128), -4096.0)
+    diag(("idf", 128, 256), 1.0)
+    for name, c in (("dnf", -4096.0), ("upf", 4096.0)):
         diag((name, 0, 128), c)
         diag((name, 128, 256), c)
     for s in ("sa", "sb"):
@@ -704,145 +627,137 @@ def build(core, T, topo):
     cp(("col", 0, 1), ("c1", 0, 1))
     tt(("c2", 0, 32), ("c2", 0, 32), ("c3", 0, 32), A.add)
     cp(("lst", 0, 32), ("c2", 0, 32))
+    for c, scale, bias in ((1, 2.0 ** 18, 512 - 2.0 ** 22), (2, -2.0 ** 18, -1024.0 * 255), (3, 2.0 ** 21, 0.0)):
+        ts(("col", c, c + 1), ("col", 0, 1), scale, A.mult, bias, A.add)
+    act(("rmp", 256, 512), ("rmp", 256, 512), F.Identity, ("col", 3, 4), bias=T.col[:, 3:4])
+    act(("rmp", 0, 256), ("rmp", 256, 512), F.Identity, scale=-1.0, bias=2.0 ** 25 - 4096)
     lag[0] = 600
     act(("mc", 0, 256), ("mc", 0, 256), F.Identity, ("col", 0, 1), bias=T.col[:, 0:1])
     tt(("er", 15, 143, 16), ("e8", 0, 8), ("e8", 8, 16), A.add)
     act(("er", 143, 271, 16), ("er", 15, 143, 16))
-    for k, a in (("kl", 0), ("kr", 8)):
-        act(("e8", 24, 32), ("e8", a, a + 8), F.Identity, scale=BIG, bias=1024.0, accum_out=T[k][:, 0:1])
+    for k, a, c in (("kl", 0, 1), ("kr", 8, 2)):
+        act(("e8", 24, 32), ("e8", a, a + 8), F.Identity, ("col", c, c + 1), scale=BIG, bias=T.col[:, c:c + 1], accum_out=T[k][:, 0:1])
         ops[-1]["w"].append((k, 0, 1))
     op("v", lambda e: e.tensor_scalar(T.hopf[:], T.hopi[:], -1.0 / W, None, A.mult), [("hopi", 0, 4)], [("hopf", 0, 4)], 0.12)
 
     def targets(t, k):
         if k == 1:
             cp(("it16", 256 * t, 256 * t + 256), ("iti", 256 * t, 256 * t + 256))
-        elif t >= CFG["td"]:
-            if k == 2:
-                op("s", lambda e: [e.dma_start(T.eli[:, 256 * t + 16 * r:256 * t + 16 * r + 16], T.itg[r::16, 256 * t:256 * t + 256]).then_inc(T.sem["ldt%d" % t], 16) for r in range(16)],
-                   [("gv" if t == 1 else "dl", 0, W)], [("eli", 256 * t, 256 * t + 256)], 1.0, "ldt%d" % t, 256, 1.5, 5.0)
-            elif k == 5:
-                gat("a", ("el", 256 * t, 256 * t + 256), ("eli", 256 * t, 256 * t + 256), LP, F.Identity, scale=-1.0, bias=float(4095 - 2 ** 24))
         elif k == 2:
-            gat("a" if CFG["ai"] else "v", ("kp2", 16, 272), ("iti", 256 * t, 256 * t + 256), LP)
+            gat("a", ("kp2", 16, 272), ("iti", 256 * t, 256 * t + 256), LP)
         elif k < 5:
             turn("kp2", "tw2", k - 3)
+        elif k == 5:
+            gat("a", ("el", 0, 256), ("tw2", 0, 544), LB, F.Identity, scale=-1.0, bias=4095 - 2.0 ** 24)
+            act(("el", 256, 512), ("el", 0, 256), F.Identity, bias=4096.0)
+        elif k == 6:
+            dma("s", T.nk[:], T.rmp[:], [("rmp", 0, 512)], [("nk", 0, 512)], "nkc", 256)
         else:
-            gat("a", ("el", 256 * t, 256 * t + 256), ("tw2", 0, 544), LB, F.Identity, scale=-1.0, bias=float(4095 - 2 ** 24))
+            adding(T.nk[:], T.el[:], [("el", 0, 512)], [("nk", 0, 512)], "nka", 0.3 + 512 / 600)
 
     def rows(rw):
         buf, a, b = rw
         dma("s", T[buf][0::16, a:b], T.hl[:, 0:256], [("hl", 0, 256)], [(buf, a, b, 2)], "rwd", 100)
         dma("s", T[buf][15::16, a:b], T.hl[:, 256:512], [("hl", 256, 512)], [(buf, a + 1, b, 2)], "rwd", 100)
 
-    turnno, sent, added, landed = [0, 0, 0], [], [], []
+    turnno, sent, added, landed = [0, 0], [], [], []
 
-    def bank(n):
-        o = 512 * (turnno[1] % 2)
-        turnno[1] += 1
-        return ("pd", o, o + n)
-
-    def judge(s, pad, v0, v1, terms, by="G"):
-        parts = (v1 - v0 + 511) // 512
+    def judge(s, pad, v0, v1, terms, whole):
+        most = 512 if whole else CFG["jc"]
+        parts = (v1 - v0 + most - 1) // most
         for h in range(parts):
             a, b = max(1, v0 + (v1 - v0) * h // parts), v0 + (v1 - v0) * (h + 1) // parts
-            p = bank(b - a)
-            if by == "F":
-                act(p, ("bb", a - BB, b - BB))
-                ops[-1]["w"].append(("bbw", a, b))
-                tt(("vt", a, b), p, (s, pad + a, pad + b), A.subtract)
-                continue
-            step = b - a if s == "s0" else CFG["jc"]
-            lag[0] += CFG["jl"]
-            for c in range(a, b, step):
-                for j, (name, buf, at) in enumerate([("dn", s, -pad)] + terms):
-                    lhs, k = mat(name, s)
-                    mm((p[0], p[1] + c - a, p[1] + min(b, c + step) - a), lhs, (buf, c - at, min(b, c + step) - at), j == 0, j == len(terms), k)
-                if s == "s0":
-                    join(len(terms) + 1)
-            lag[0] -= CFG["jl"]
-            if terms[0][1] == "bb":
-                ops[-1]["w"].append(("bbw", a, b))
+            banks = CFG["banks0" if s == "s0" else "banks"]
+            ps, o = banks[turnno[1] % len(banks)]
+            turnno[1] += 1
+            p = (ps, o, o + b - a)
+            for j, (name, buf, at) in enumerate([("up", s, -pad)] + terms):
+                lhs, k = mat(name, s)
+                mm(p, lhs, (buf, a - at, b - at), j == 0, j == len(terms), k)
+            if whole:
+                join(len(terms) + 1)
             act(("vt", a, b), p)
 
     def piece(s, pad, v0, v1, by):
-        k = turnno[0] % 2
+        k, j = turnno[0] % 2, turnno[0] % 4
         turnno[0] += 1
         p, h, n = "pe%d" % k, (v1 - v0) // 2, v1 - v0
-        j = (turnno[0] - 1) % 4
-        u = "h%d" % k if s == "s0" and by not in "YZyz" else "b%d" % j
-        lhs, c = mat("id", s)
-        lo, hi = pad + v0, pad + v1
+        u = "h%d" % k if s == "s0" else "b%d" % j
         kind = by.upper()
+        lhs, c = mat("ng" if kind == "N" else "id", s)
+        lo, hi = pad + v0, pad + v1
         m, b = "pm" if kind == "V" else u, "a%d" % k
         a = ("pm", 512 * k, 512 * k + h) if kind != "V" else ("pm", 1024 - h, 1024) if n + h <= 1024 else (p, 2, h + 2)
 
         def even():
-            if by.islower():
-                act((p, 0, h + 2), (s, lo - 2, hi + 2, 2))
+            if kind in "GH":
+                who = helpers(core, nxt, T, topo)[CFG["fw"]]
+                rid, pid, _ = topo.addr(who)
+                out, back = len(topo.engines(core, who)), len(spare(who, core, nxt, topo))
+                x = RemoteDMATransfer(dst_ids=[DstId(rid=rid, pnc=pid)], dma_engine_mask=topo.mask(core, who), remote_sem=T.sem.fa,
+                                      srcs=[T[s][:, lo + z:hi + z] for z in (-2, -1, 1, 2)], dsts=[T[u][:, 0:n]], alu_op=2)
+                i = op("g", lambda e: e.remote_dma_fused([x], local_sem=T.sem.fl), [(s, lo - 2, hi + 2)], [(u, 0, n)],
+                       1.0, "fl", out, 1.0, 2 * n / 550, fold=(who, out, "fa", (u, 0, n), core, "fb"))
+                op(None, None, [], [(u, 0, n)], 0.0, "fb", back, CFG["back"] + n / 1000 + once(who), after=(i,))
+            elif kind == "B":
+                return
+            elif by.islower():
+                act((p, 0, h + 2), (s, lo - 2, hi + 2, 2), scale=-1.0 if kind == "N" else 1.0)
             else:
                 mm((p, 0, h + 2), lhs, (s, lo - 2, hi + 2, 2), True, True, c)
 
         def minus():
-            if kind in "YZ":
-                act(("vt", v0, v1), (s, lo, hi), scale=-2.0 if kind == "Y" else -1.0)
+            if kind == "N":
+                act((u, 0, h + 2), (s, lo - 1, hi + 2, 2), scale=-1.0)
 
-        def add(at):
-            op("g", lambda e: e.dma_start(T.vt[:, v0:v1], T[u][:, at:at + n], accum_op=A.add).then_inc(T.sem["zd%d" % j], 16),
-               [(u, at, at + n)], [("vt", v0, v1)], 1.0 + once("g") / 3, "zd%d" % j, 16, CFG["add"] - 1.0, 0.3 + n / 600)
-            ops[-1]["follows"] = added[-1:]
-            added.append(len(ops) - 1)
+        def folded():
+            if kind in "HZ":
+                act(("vt", v0, v1), (u, 0, n), scale=-1.0)
+                add()
+            elif kind == "G":
+                judge(s, pad, v0, v1, [("dn", u, v0)], True)
+
+        def add():
+            adding(T.vt[:, v0:v1], T[s][:, lo:hi], [(s, lo, hi)], [("vt", v0, v1)], "zd%d" % j, 0.3 + n / 600)
 
         def maxima():
-            if kind in "XY":
+            if kind == "X":
                 tt((p, 0, h + 2), (p, 0, h + 2), (s, lo - 1, hi + 2, 2), A.max)
-                return
-            tt((b, 0, h + 1), (p, 0, h + 1), (s, lo + 1, hi + 2, 2), A.max)
-            tt(a, (p, 2, h + 2), (s, lo - 1, hi - 1, 2), A.max)
+            elif kind == "B":
+                tt(("rg", X * k, X * k + h + 2), (s, lo - 2, hi + 2, 2), (s, lo - 1, hi + 2, 2), A.max, CFG["bb"])
+            elif kind == "N":
+                tt((b, 0, h + 1), (p, 0, h + 1), (u, 1, h + 2), A.min)
+                tt(a, (p, 2, h + 2), (u, 0, h), A.min)
+            elif kind not in "GH":
+                tt((b, 0, h + 1), (p, 0, h + 1), (s, lo + 1, hi + 2, 2), A.max)
+                tt(a, (p, 2, h + 2), (s, lo - 1, hi - 1, 2), A.max)
 
         def more():
-            if kind in "XY":
+            if kind == "X":
                 tt((u, 0, n + 2, 2), (p, 0, h + 1), (s, lo, hi + 1, 2), A.max)
                 tt((u, 1, n + 2, 2), (p, 1, h + 2), (s, lo - 1, hi, 2), A.max)
-            else:
+            elif kind == "B":
+                tt((u, 0, n + 2, 2), ("rg", X * k, X * k + h + 1), (s, lo, hi + 1, 2), A.max, CFG["bb"])
+                tt((u, 1, n + 2, 2), ("rg", X * k + 1, X * k + h + 2), (s, lo - 1, hi, 2), A.max, CFG["bb"])
+            elif kind == "N":
+                tt(("vt", v0, v1, 2), a, (b, 0, h), A.min)
+                tt(("vt", v0 + 1, v1, 2), a, (b, 1, h + 1), A.min)
+            elif kind not in "GH":
                 tt((m, 0, n, 2), a, (b, 0, h), A.max)
                 tt((m, 1, n, 2), a, (b, 1, h + 1), A.max)
 
         def finish():
-            if kind == "X":
-                judge(s, pad, v0, v1, [("hf", u, v0), ("hf", u, v0 - 2)])
-            elif kind == "Y":
-                add(0)
-                add(2)
+            if kind in "XB":
+                judge(s, pad, v0, v1, [("hf", u, v0), ("hf", u, v0 - 2)], True)
             elif kind == "V":
                 z = 1 if v0 == 0 else 0
-                tt(("vt", v0 + z, v1), (m, z, n), (s, lo + z, hi), A.subtract)
-            elif kind == "Z":
-                add(0)
-            else:
-                judge(s, pad, v0, v1, [("up", u, v0)])
+                tt(("vt", v0 + z, v1), (s, lo + z, hi), (m, z, n), A.subtract)
+            elif kind == "N":
+                add()
+            elif kind == "W":
+                judge(s, pad, v0, v1, [("dn", u, v0)], False)
 
-        return {"e": even, "n": minus, "m": maxima, "M": more, "f": finish}
-
-    def fold_out(s, pad, v0, v1, k):
-        who = helpers(core, nxt, T, topo)[0][0] if CFG["fw"] == "p" else turns[k % len(turns)]
-        rid, pid, _ = topo.addr(who)
-        kb = (v1 - v0) / 2
-        x = RemoteDMATransfer(dst_ids=[DstId(rid=rid, pnc=pid)], dma_engine_mask=topo.mask(core, who), remote_sem=T.sem["fa%d" % k],
-                              srcs=[T[s][:, pad + v0 + h:pad + v1 + h] for h in (-2, -1, 1, 2)], dsts=[T.bb[:, v0 - BB:v1 - BB]], alu_op=2)
-        i = op("g", lambda e: e.remote_dma_fused([x], local_sem=T.sem["fl%d" % k]), [(s, pad + v0 - 2, pad + v1 + 2), ("bbw", v0, v1)], [],
-               1.0, "fl%d" % k, len(topo.engines(core, who)), 1.0, 4 * kb / 550,
-               fold=(who, len(topo.engines(core, who)), "fa%d" % k, ("bb", v0 - BB, v1 - BB), core, "fb%d" % k))
-        op(None, None, [], [("bb", v0 - BB, v1 - BB)], 0.0, "fb%d" % k, len(topo.engines(who, core)), CFG["back"] + kb / 500 + once(who), after=(i,))
-
-    def folded(s, v0, v1, k):
-        turnno[0] += 1
-
-        def add():
-            op("g", lambda e: e.dma_start(T.vt[:, v0:v1], T.bb[:, v0 - BB:v1 - BB], accum_op=A.add).then_inc(T.sem.zf, 16),
-               [("bb", v0 - BB, v1 - BB)], [("vt", v0, v1), ("bbw", v0, v1)], 1.0, "zf", 16, CFG["add"] - 1.0, 0.3 + (v1 - v0) / 600)
-
-        return {"e": lambda: fold_out(s, PF, v0, v1, k), "n": lambda: act(("vt", v0, v1), (s, PF + v0, PF + v1), scale=-1.0),
-                "m": lambda: None, "M": lambda: None, "f": add}
+        return {"e": even, "n": minus, "m": maxima, "M": more, "f": finish, "N": folded}
 
     vc = [0] + [c - 4 for c in cuts0[1:n0]] + [W]
     lag[0] = 0
@@ -850,6 +765,7 @@ def build(core, T, topo):
     turnno[0] = n0 % 2
     parts = [piece("s0", PB, vc[k], vc[k + 1], CFG["route0"][k]) for k in range(n0)]
     for step in CFG["start"].split():
+        tag[:] = [-1, step, len(ops)]
         if step[0] == "t":
             targets(0, int(step[1:]))
         else:
@@ -859,6 +775,7 @@ def build(core, T, topo):
     def records(k, after):
         dma("s", T.cw[:, k * W:k * W + W], T.rec[:], [after], [("cw", k * W, k * W + W)], "ldc%d" % k, 1024)
 
+    tag[:] = [-1, "c", len(ops)]
     for k in range(CFG["rc"]):
         records(k, ("iti", 256, 1024))
 
@@ -868,70 +785,50 @@ def build(core, T, topo):
         new = ("sa", "sb")[t % 2]
         lq = "lq%d" % t
         xt, lt = ("xo", lq) if t else ("xb", "lb")
+        got = (lq, X, XW) if t else (lq, 0, QX)
         win = (old, opad, opad + W)
         rw = ("s0", PB, PB + W) if t else ("gv", 0, W)
         up = float(W * (t // 2 + 1))
-        kept = []
+        recs = ("cw", 0, (t // 2 * 2 + 3) * W)
+        kept, held = [], {}
 
         r0 = 16 * t
         at = (128 - r0) % 128
-        xs, counted = CFG["xs"], []
+        xs = CFG["xs"]
 
         def copies():
-            if t >= CFG["tw"]:
-                dma("s", T.sr[r0:128, :], T[old][0:128 - r0, PF:PF + W], [win], [("sr", 0, W, 2)], "trn", 1800)
-                dma("s", T.sr[0:r0, :], T[old][128 - r0:128, PF:PF + W], [win], [("sr", 1, W, 2)], "trn", 300)
+            if t:
+                dma("s", T.sr[r0:128, :], T[old][0:128 - r0, PF:PF + W], [win, ("vt", X, W)], [("sr", 0, W, 2)], "trn", 1800)
+                dma("s", T.sr[0:r0, :], T[old][128 - r0:128, PF:PF + W], [win, ("vt", X, W)], [("sr", 1, W, 2)], "trn", 300)
 
         def hops():
             act(("hd", 0, 128), ("upf", 0, 128), F.Identity, ("hopf", 0, 4), scale=T.hopf[:, t:t + 1])
             if t:
                 act(("hdt", 0, 128), ("upf", at, at + 128), F.Identity, ("hopf", 0, 4), scale=T.hopf[:, t:t + 1])
 
-        def split(q):
-            act(("hl", 0, 256), (q, 0, 256))
-            mm(("pr", 0, 256), ("upf", 0, 128), (q, 0, 256), True, False, 4)
-            mm(("pr", 0, 256), ("dnb", 0, 128), ("hl", 0, 256), False, True)
-            act(("hl", 256, 512), ("pr", 0, 256), scale=1.0 / W)
-
         def r_rows(k):
-            if t and CFG["rp"]:
-                if k == 5:
-                    for r in range(8):
-                        ps, o = (("pe0", 0), ("pe1", 0), ("pm", 0), ("pm", 512), ("pd", 0), ("pd", 512))[r % 6]
-                        for j in range(2):
-                            e0 = 16 + 128 * (r + 8 * j)
-                            mm((ps, o + j, o + 512, 2), ("eh", e0, e0 + 128), ("hl", 0, 256), True, False)
-                            mm((ps, o + j, o + 512, 2), ("eh", e0 - 15, e0 + 113), ("hl", 256, 512), False, True)
-                        join(4)
-                        ops[-1]["w"] = [(ps, o, o + 512)]
-                        if r >= CFG["rf"]:
-                            ops[-1]["follows"] = counted[-1:]
-                        act((rw[0], rw[1] + r, rw[2], 8), (ps, o, o + 512))
-                        ops[-1]["w"] = [("rw%d" % r, 0, 1)]
-                        ops[-1]["r"].append(("rwr", 0, 1))
-            elif k == 5:
+            if k == 5:
                 rows(rw)
             elif k < 4:
                 if t:
                     turn("kp3", "tw3", k - 2)
             else:
                 gat("a", ("qb", 0, 256), *((("tw3", 0, 544), LB) if t else (("roti", 0, 256), ("lst", 48, 64))))
-                split("qb")
+                act(("hl", 0, 256), ("qb", 0, 256))
+                mm(("pr", 0, 256), ("upf", 0, 128), ("qb", 0, 256), True, False, 4)
+                mm(("pr", 0, 256), ("dnb", 0, 128), ("hl", 0, 256), False, True)
+                act(("hl", 256, 512), ("pr", 0, 256), scale=1.0 / W)
 
         def moved(q, k):
             b0, b1, i = xs[k], xs[k + 1], len(ops)
-            gat(q, ("gv", 256 * b0, 256 * b1), ("vt", 0, W), ("it16", 256 * t + 16 * b0, 256 * t + 16 * b1), F.Sign, scale=-1.0, bias=2.0 ** -32)
+            gat(q, ("gv", 256 * b0, 256 * b1), ("vt", 0, W), ("it16", 256 * t + 16 * b0, 256 * t + 16 * b1), F.Sign, bias=2.0 ** -32)
             for b in range(b0, b1):
                 op("p", lambda e, b=b: e.matmul(T.pc[:, 0:256], T["e" + ops[i]["q"]][:, 15 - b:143 - b], T.gv[:, 256 * b:256 * b + 256], False, b == 15),
                    [("gv", 256 * b, 256 * b + 256), ("ea", 0, 144), ("ev", 0, 144)], [("pc", 0, 256)], 0.015 + 136 * cy)
             join(b1 - b0)
-            counted.append(len(ops) - 1)
 
-        def right():
-            if CFG["dr"] == "a":
-                act(("dr", 0, 256), ("dl", 0, 256), F.Identity, bias=4096.0)
-            else:
-                tt(("dr", 0, 256), ("pc", 0, 256), ("elr", 0, 256), A.max)
+        def latest(out, key, way):
+            op("v", lambda e: e.tensor_tensor_scan(way(out), way(("pc", 0, 256)), way(key), NONE, A.min, A.max), [("pc", 0, 256), key], [out], cost(out))
 
         def decode():
             halves = [(a, a + CFG["dc"]) for a in range(0, 256, CFG["dc"])]
@@ -951,12 +848,11 @@ def build(core, T, topo):
             tr(("tw", 128, 256), ("kp", 144, 272))
 
         front = {
-            "c": lambda: t in (1, 2) and records(t + 2, ("vt", 0, W)), "C": copies, "h": hops,
+            "C": copies, "h": hops,
             "z": lambda: mm(("pc", 0, 256), ("idb", 0, 128), ("cb", 0, 256), True, False),
-            "E": lambda: CFG["dr"] == "v" and act(("elr", 0, 256), ("el", 256 * t, 256 * t + 256), F.Identity, bias=4096.0),
-            "d": lambda: tt(("dl", 0, 256), ("pc", 0, 256), ("el", 256 * t, 256 * t + 256), A.max), "e": right,
-            "L": lambda: scan(("fg", 0, 256), ("kl", 0, 256), ("dl", 0, 256), NONE),
-            "R": lambda: scan(("fg", 256, 512), ("kr", 0, 256), ("dr", 0, 256), NONE, True),
+            "d": lambda: tt(("dl", 0, 256), ("pc", 0, 256), ("el", 0, 256), A.max),
+            "e": lambda: tt(("dr", 0, 256), ("pc", 0, 256), ("el", 256, 512), A.max),
+            "L": lambda: latest(("fg", 0, 256), ("nk", 0, 256), ap), "R": lambda: latest(("fg", 256, 512), ("nk", 256, 512), rev),
             "x": lambda: tr(("xe", 0, 32), ("fg", 240, 272)),
             "y": lambda: (scan(("yy", 1, 32), ("st", 0, 31), ("xe", 0, 31), NONE), scan(("yy", 32, 63), ("st", 0, 31), ("xe", 1, 32), NONE, True)),
             "w": lambda: tr(("zz", 0, 64), ("yy", 0, 64)),
@@ -970,11 +866,11 @@ def build(core, T, topo):
             elif step[0] == "r":
                 r_rows(int(step[1:]))
             elif step[0] == "t":
-                if not last:
+                if not last and (t == 0 or step[1] not in CFG["ahead"]):
                     targets(t + 1, int(step[1:]))
             else:
-                if step == "d":
-                    mark.append(len(ops))
+                if step == "L":
+                    gates.append(len(ops))
                 front[step]()
 
         def source(a, b):
@@ -996,11 +892,6 @@ def build(core, T, topo):
                 mm(p, ("idf", at, at + 128), ("hw", 256 - QX, 256), False, True, 4)
                 ts(("srt", 0, QX), p, 6143.0, A.add, 4095.0, A.min)
 
-        def r_gather(q, m0, m1):
-            gat(q, ("rg", m0, m1), rw, ("src", m0 // 16, m1 // 16))
-            if CFG["rp"]:
-                ops[-1]["r"] += [("rw%d" % r, 0, 1) for r in range(8)]
-
         def rot_of(ps, m0, m1):
             a, b = m0 // 16, m1 // 16
             p = (ps, 256 + a, 256 + b)
@@ -1017,101 +908,81 @@ def build(core, T, topo):
                 kept.append((("qf", QX + a, QX + b), p))
 
         def t_gather(q, m0, m1):
-            o = 0 if m0 < W - X else W - X if m0 < W - X + HX else W - XW
-            if o and t and t >= CFG["tw"]:
-                gat(q, ("xo", m0 - o, m1 - o), ("sr", 0, W), ("srt", (m0 - W + X) // 16, (m1 - W + X) // 16))
+            o = W - X
+            if m0 < o:
+                gat(q, ("tb", m0, m1), win, ("src", m0 // 16, m1 // 16))
+            elif t:
+                gat(q, (xt, m0 - o, m1 - o), ("sr", 0, W), ("srt", (m0 - o) // 16, (m1 - o) // 16))
             else:
-                gat(q, (xt if o else "tb", m0 - o, m1 - o), win, ("src", m0 // 16, m1 // 16))
-            if not t:
-                ops[-1]["r"] += [("rw%d" % r, 0, 1) for r in range(8)]
+                gat(q, (xt, m0 - o, m1 - o), win, ("src", m0 // 16, m1 // 16))
 
-        def product(n0, n1):
-            x = ("tb", n0 - X, n1 - X) if n0 >= X else (lt, n0, n1) if n0 < HX else (lt, n0 + QX, n1 + QX)
-            gtt((new, PF + n0, PF + n1), ("cw", 0, (t // 2 * 2 + 3) * W), ("q16", n0 // 16, n1 // 16), x, A.mult)
-
-        def records_of(n0, n1, k):
-            gat("a", ("h%d" % (n0 == 0), 0, n1 - n0), ("cw", 0, (t // 2 * 2 + 3) * W), ("q16", n0 // 16, n1 // 16))
+        def factor(n0, n1):
+            return ("tb", n0 - X, n1 - X) if n0 >= X else (lt, n0, n1)
 
         def turn_in(n0, n1, k):
-            held[k] = ("pe%d" % (k % 2), 0, n1 - n0) if last else (("pc", "pr")[n0 == 0], 0, n1 - n0)
-            if t >= CFG["tw"] or not t:
-                mm(held[k], ("idb", 0, 128), ("h%d" % (n0 == 0), 0, n1 - n0), True, True)
-            else:
-                mm(held[k], ("idf", at, at + 128), (lq, n0, n1) if n0 < HX else (lq, n0 + QX, n1 + QX), True, True, 4)
-
-        def times(n0, n1, k):
-            if t >= CFG["tw"] or not t:
-                tt((new, PF + n0, PF + n1), (lt, n0, n1) if n0 < HX else (lt, n0 + QX, n1 + QX), held[k], A.mult)
-            else:
-                tt((new, PF + n0, PF + n1), ("h%d" % (k % 2), 0, n1 - n0), held[k], A.mult)
-
-        held = {}
+            ps, o = CFG["hb"].get((last, k)) or (("pe%d" % (k % 2), 0) if last else (("pc", "pr")[n0 == 0], 0))
+            held[k] = (ps, o, o + n1 - n0)
+            for a in range(0, n1 - n0, 512):
+                b = min(a + 512, n1 - n0)
+                mm((ps, o + a, o + b), ("idb", 0, 128), ("h%d" % (k % 2), a, b), True, True)
 
         def send(k):
-            a, b = PARTS[k]
+            hx = CFG["hx"][t]
+            out, land = [((xt, 0, hx), (lt, 0, hx)), ((xt, hx, X), (lt, hx, X)), (("xo", X, XW), got)][k]
             who = senders(t, core, nxt, T, topo)[k]
             to = nxt if who == core else who
             rid, pid, _ = topo.addr(to)
             sem = ("arr%d_%d" if who == core else "xa%d_%d") % (t, k)
             mask, n = topo.mask(core, to), len(topo.engines(core, to))
-            out, land = (("xo", a, b), (lq, a, b)) if a == HX else ((xt, a, b), (lt, a, b))
             i = op("g", lambda e: e.remote_dma(ap(land), ap(out), T.sem[sem], T.sem["sx%d" % k], pid, rid, mask),
-                   [out], [], 1.0 + once(core), "sx%d" % k, n, 1.0, (b - a) / 500,
+                   [out], [], 1.0 + once(core), "sx%d" % k, n, 1.0, size(out) / 500,
                    fold=None if who == core else (who, n, sem, land, nxt, "arr%d_%d" % (t, k)))
-            ops[i]["follows"] = sent[-1:]
-            sent.append(i)
-            way = (b - a) / CFG["link"] / (2 if land[0] == "lb" else 1)
+            way = size(out) / CFG["link"] / (2 if land[0] == "lb" else 1)
             op("L" if who == core else "M", None, [], [land], way, "arr%d_%d" % (t, k), len(topo.engines(senders(t, prv, core, T, topo)[k], core)),
                CFG["far"] if who == core else CFG["arr"] + once(who), after=(i,))
+            ops[i]["follows"] = sent[-1:]
+            sent.append(i)
             if who == core:
                 ops[-1]["follows"] = landed[-1:]
                 landed.append(len(ops) - 1)
 
         def output(n0, n1, k):
             y0, y1 = n0 % 2048, n0 % 2048 + n1 - n0
-            ps, x, out = "pd" if y0 < X else "pm", (new, PF + n0, PF + n1), ("vt", y0, y1)
+            ps, x = "pd" if y0 < X else "pm", (new, PF + n0, PF + n1)
             by = CFG["yk"][k]
-            if by == "d" and n0 >= 2048:
+            if by == "s":
                 dma("s", T.y[:, y0:y1], ap(x), [x], [("y", y0, y1)], "out%d" % k, (n1 - n0) / 2)
-                return
-            if by == "d":
-                op("g", lambda e: e.dma_start(T.y[:, y0:y1], ap(x), accum_op=A.add).then_inc(T.sem["zd%d" % (k % 4)], 16),
-                   [x], [("y", y0, y1)], 1.0, "zd%d" % (k % 4), 16, CFG["add"] - 1.0, (n1 - n0) / 600)
-                return
-            for a in range(y0, y1, 512):
-                b = min(a + 512, y1)
-                p, xs = (ps, a % X, a % X + b - a), (new, x[1] + a - y0, x[1] + b - y0)
-                if by == "a":
-                    act(p, xs)
-                elif n0 >= 2048:
-                    mm(p, ("idf", 0, 128), xs, True, by == "p", 4)
-                elif by == "v":
-                    tt(("vt", a, b), xs, p, A.add)
-                else:
-                    mm(p, ("idf", 0, 128), xs, False, True, 4)
-                    act(("vt", a, b), p)
-            if n0 < 2048:
-                dma("s", T.y[:, y0:y1], T.vt[:, y0:y1], [out], [("y", y0, y1)], "out%d" % k, (n1 - n0) / 2)
+            elif by == "d":
+                adding(T.y[:, y0:y1], ap(x), [x], [("y", y0, y1)], "zd%d" % (k % 4), (n1 - n0) / 600)
+            else:
+                for a in range(y0, y1, 512):
+                    b = min(a + 512, y1)
+                    p, z = (ps, a % X, a % X + b - a), (new, x[1] + a - y0, x[1] + b - y0)
+                    if by == "a":
+                        act(p, z)
+                    elif by == "m":
+                        mm(p, ("idf", 0, 128), z, True, True, 4)
+                    else:
+                        tt(("vt", a, b), z, p, A.add)
+                if by == "v":
+                    dma("s", T.y[:, y0:y1], T.vt[:, y0:y1], [("vt", y0, y1)], [("y", y0, y1)], "out%d" % k, (n1 - n0) / 2)
 
         yc = CFG["yc"]
         cut = CFG["cut"] // 16
         tag[:] = [t, "sources", len(ops)]
         source(cut, 256)
         phase(cut, 256)
-        got = (lq, HX, HX + QX)
         pieces = CFG["lp"] if last else list(zip(yc[1:], yc))
         if not last:
             vc = [W] + [c + 4 for c in CFG.get("vc", yc)[1:-1]] + [0]
             route = CFG["route"][t]
-            turnno[0] = len(route) % 2
-            votes = [piece(new, PF, vc[k + 1], vc[k], by) if by not in "FGH" else folded(new, vc[k + 1], vc[k], k) if by == "H" else
-                     {"e": lambda k=k: fold_out(new, PF, vc[k + 1], vc[k], k), "n": lambda: None, "m": lambda: None, "M": lambda: None,
-                      "f": lambda k=k, by=by: judge(new, PF, vc[k + 1], vc[k], [("up", "bb", BB)], by)} for k, by in enumerate(route)]
-        top = {"w": (W - X, W), "a": (W - X + HX, W), "b": (W - X, W - X + HX)}
+            turnno[:] = [len(route) % 2, 0]
+            votes = [piece(new, PF, vc[k + 1], vc[k], by) for k, by in enumerate(route)]
+        top = {"w": (W - X, W), "a": (W - X + CFG["hx"][t], W), "b": (W - X, W - X + CFG["hx"][t]), "c": (W - X // 2, W), "d": (W - X, W - X // 2)}
         for step in CFG["last" if last else "steps"].split():
             q, step = step.split(":") if ":" in step else (None, step)
             c, k = step[0], step[1:]
-            tag[:] = [t, ("last " if last else "") + step, len(ops)]
+            tag[:] = [t, step, len(ops)]
             if c == "S":
                 source(0, cut)
             elif c == "H":
@@ -1123,16 +994,15 @@ def build(core, T, topo):
             elif c == "U":
                 turned_source()
             elif c == "C":
-                (act if q == "a" else cp)(("xo", HX, HX + QX), ("pd", 512 - QX, 512))
+                (act if q == "a" else cp)(("xo", X, XW), ("pd", 512 - QX, 512))
             elif c == "R":
-                r_gather(q, *top[k])
+                m0, m1 = top[k]
+                gat(q, ("rg", m0, m1), rw, ("src", m0 // 16, m1 // 16))
             elif c == "T":
                 t_gather(q, *top[k])
             elif c == "Q":
                 rot_of("pd", W - X, W)
             elif c == "X":
-                if last and k == "q":
-                    mark.append(len(ops))
                 send("baq".index(k))
             elif c == "I":
                 ts(("q16", 0, QX), got, up, A.add)
@@ -1141,45 +1011,43 @@ def build(core, T, topo):
                     act(out, p)
             elif c == "D":
                 if t < 2:
-                    records(t + 3, (new, PF + yc[2], PF + yc[1]))
-            elif c == "E":
-                targets(t + 1, 5)
+                    records(t + 3, ("xo", X, XW))
+            elif c == "G":
+                if t + 2 < FR and k in CFG["ahead"]:
+                    targets(t + 2, int(k))
             elif c == "J":
                 act(("qf", 0, QX), got)
-            elif c == "Z" and CFG["rp"]:
-                split("qf")
             elif c == "Z":
                 gat("a", ("kp3", 16, 272), ("qf", 0, 256), LP)
-            elif c in "enmMf":
+            elif c in "enmMfN":
                 votes[int(k)][c]()
             else:
-                n0, n1 = pieces[int(k)]
+                k = int(k)
+                n0, n1 = pieces[k]
                 if c == "r":
-                    r_gather(q, n0 - X, n1 - X)
+                    gat(q, ("rg", n0 - X, n1 - X), rw, ("src", (n0 - X) // 16, (n1 - X) // 16))
                 elif c == "t":
                     t_gather(q, n0 - X, n1 - X)
                 elif c == "q":
-                    rot_of(("pc", "pr")[int(k) % 2], n0 - X, n1 - X)
+                    rot_of(("pc", "pr")[k % 2], n0 - X, n1 - X)
                 elif c == "o":
-                    ts(("q16", n0 // 16, n1 // 16), (("pc", "pr")[int(k) % 2], 192 + n0 // 16, 192 + n1 // 16), up, A.add)
+                    ts(("q16", n0 // 16, n1 // 16), (("pc", "pr")[k % 2], 192 + n0 // 16, 192 + n1 // 16), up, A.add)
                 elif c == "p":
-                    if len(mark) % 2:
-                        mark.append(len(ops))
-                    product(n0, n1)
+                    gtt((new, PF + n0, PF + n1), recs, ("q16", n0 // 16, n1 // 16), factor(n0, n1), A.mult)
                 elif c == "g":
-                    records_of(n0, n1, int(k))
-                elif c == "P":
-                    times(n0, n1, int(k))
+                    gat("a", ("h%d" % (k % 2), 0, n1 - n0), recs, ("q16", n0 // 16, n1 // 16))
                 elif c == "u":
-                    turn_in(n0, n1, int(k))
+                    turn_in(n0, n1, k)
+                elif c == "P":
+                    tt((new, PF + n0, PF + n1), factor(n0, n1), held[k], A.mult)
                 else:
-                    output(n0, n1, int(k))
+                    output(n0, n1, k)
 
-    mark = []
+    gates = []
     for t in range(FR):
         frame(t)
     for o in ops[kept_from:]:
         o["now"] = "kept"
-    for k, i in enumerate(mark):
-        ops[i]["now"] = ("gate", "goal")[k % 2]
+    for i in gates:
+        ops[i]["now"] = "gate"
     return ops

import math
from concourse.bass import DstId, RemoteDMATransfer
from concourse.mybir import AluOpType as A, ActivationFunctionType as F

W = 4096
X = 1024
FR = 4
PF, PB = 8, 16
QX = X // 16
XW = X + QX
BIG = float(2 ** 27)
NONE = float(2 ** 26)
RND = 1.5 * 2 ** 23

CFG = {
    "cuts0": [0, 384, 1392, 2400, 3408, W], "route0": "bbbbv",
    "start": "m0 m1 M0 f0 M1 f1 t2 m2 M2 f2 m3 e4 M3 f3 t3 t4 t5 t6 t7 m4 t1 M4 f4",
    "xs": [0, 1, 3, 5, 7, 9, 11, 13, 14, 15, 16],
    "front": "z a:g0 v:g1 C a:g2 v:g3 a:g4 v:g5 a:g6 v:g7 a:g8 v:g9 r2 r3 t2 t1 r4 L R r5 t6 d x e y t3 w t4 F B h t5 t7 D",
    "yc": [W, 3328, 2336, 1472, X, 512, 0], "route": ["NNNwwv"] * 3, "fw": 0, "ahead": "234", "jc": 456, "banks": [("pd", 0), ("pd", 512), ("pr", 0), ("pe0", 0)], "banks0": [("pd", 0), ("pd", 512), ("pr", 0)],
    "steps": "a:r0 H v:k S v:K U v:Tb Xb q0 a:r1 v:Rc q1 v:Rd a:t0 o0 Qw v:Ta a:t1 o1 v:C Xq Xa D p0 e0 a:r2 p1 q2 n0 a:t2 m0 o2 e1 M0 f0 p2 a:r3 q3 n1 "
             "a:t3 e2 n2 N0 m1 o3 I g3 u3 M1 f1 N1 c G2 m2 J g4 g5 u4 u5 M2 f2 P3 P4 e3 P5 e4 m3 Z m4 e5 M3 f3 M4 f4 m5 G3 M5 G4 f5",
    "lp": [(3072, W), (2048, 3072), (1536, 2048), (X, 1536), (512, X), (0, 512)], "yk": "smddvv",
    "last": "a:Rc v:k v:Rd U a:Ta v:Tb Xb Qw S v:C Xq Xa H a:r0 a:K q0 V:t0 a:r1 q1 o0 A:t1 p0 y0 a:r2 q2 o1 I p1 A:t2 y1 a:r3 q3 o2 A:t3 g4 u4 "
            "p2 y2 o3 g5 u5 p3 y3 P4 P5 y4 y5",
    "hx": [512] * FR, "own": [0], "cut": 2048, "dc": 128, "rc": 3, "hb": {(False, 3): ("pd", 512)}, "bb": 1.0,
    "cy": 0.00083, "ga": 1.56, "fv": 0.03, "add": 2.9, "link": 240.0, "far": 0.3, "arr": 2.6, "back": 3.5, "once": 2.5, "lat": 0.25, "across": 0.6,
    "ways": [(0.16, 1.0, 1.05, 1.0, 1.0, 1.0), (0.12, 1.1, 1.45, 1.05, 0.85, 1.2), (0.2, 1.3, 1.0, 1.0, 0.75, 2.0), (0.3, 1.1, 1.4, 1.35, 1.0, 1.2),
             (0.12, 1.0, 1.2, 1.1, 1.25, 1.0)], "soon": 0.05,
    "tries": [25000, 30000, 35000, 12000, 30000], "seed": [1, 1, 1, 1, 1], "heat": [0.1, 0.04, 0.04, 0.03, 0.1],
}
DONE = {}

SCRATCH = {name: ("sbuf", [128, n], kind) for kind, names in {
    "float32": {"sa": W + 2 * PF, "sb": W + 2 * PF, "sr": W, "vt": W, "tb": W - X, "xo": XW, "lq0": QX, "lq1": XW, "lq2": XW, "lq3": XW,
                "a0": 512, "a1": 512, "b0": 1024, "b1": 1024, "b2": 1024, "b3": 1024,
                "el": 512, "rmp": 512, "nk": 512, "dl": 256, "dr": 256, "fg": 512, "xe": 32, "yy": 64, "zz": 64, "st": 32,
                "kl": 256, "kr": 256, "kp": 288, "tw": 544, "kp2": 288, "tw2": 544, "kp3": 288, "tw3": 544,
                "mc": 256, "hw": 256, "kk": 256, "qb": 256, "qf": 256, "hd": 128, "hdt": 128, "hopf": 4,
                "one": 16, "nil": 128, "idf": 256, "upf": 256, "dnf": 256, "ngf": 128, "e8": 32, "col": 4},
    "bfloat16": {"s0": W + 2 * PB, "cw": (FR + 1) * W, "xb": X, "lb": X, "gv": W, "rg": W, "h0": 1024, "h1": 1024, "hl": 512,
                 "cb": 256, "cm": QX, "ea": 144, "ev": 144, "er": 272, "idb": 128, "upb": 128, "dnb": 128, "hfb": 128},
    "int32": {"iti": 1024, "roti": 256, "hopi": 4, "ki": 256, "pay": 256, "dd": 256, "c1": 48, "c2": 48, "c3": 48, "c4": 48},
    "uint16": {"it16": 1024, "src": 256, "srt": QX, "q16": 256, "lst": 64},
}.items() for name, n in names.items()}
PSUM = {"pe0": 512, "pe1": 512, "pm": 1024, "pd": 1024, "pc": 512, "pr": 512}
SCRATCH.update({name: ("psum", [128, n], "float32") for name, n in PSUM.items()})

SEMAPHORES = (["cv", "ca", "cp", "cg", "hs", "fl", "fa", "fb", "ldi0", "ldi1", "ldr", "ldh", "rwd", "trn", "nkc", "nka"] + ["sx%d" % k for k in range(3)]
              + ["%s%d_%d" % (s, t, k) for s in ("xa", "arr") for t in range(FR) for k in range(3)]
              + ["ld%d" % k for k in range(6)] + ["ldc%d" % k for k in range(FR + 1)] + ["zd%d" % k for k in range(4)] + ["out%d" % k for k in range(8)])
COUNTER = {"v": "cv", "a": "ca", "p": "cp", "g": "cg"}
QUEUES = "vapgsLM"


def hazards(ops):
    seen, chain, deps, soft = {}, {}, [], []
    for i, o in enumerate(ops):
        acc = []
        for x, wr in [(r, False) for r in o["r"]] + [(w, True) for w in o["w"]]:
            name, lo, hi = x[:3]
            lane = lo % 2 if len(x) > 3 else None
            if name in PSUM:
                acc += [((name, b), max(lo, 512 * b), min(hi, 512 * b + 512), wr, True, lane) for b in range(lo // 512, (hi - 1) // 512 + 1)]
            else:
                acc.append((name, lo, hi, wr, False, lane))
        d, s = set(o["after"]), set(o.get("follows", []))
        for name, lo, hi, wr, ps, lane in acc:
            for j, lo2, hi2, wr2, lane2 in seen.get(name, []):
                if ps and ops[j]["q"] != o["q"]:
                    d.add(j)
                elif (wr or wr2) and lo < hi2 and lo2 < hi and not (ps and o["q"] == "p") and (lane is None or lane2 is None or lane == lane2):
                    d.add(j)
            if ps and o["q"] == "p":
                if name in chain:
                    s.add(chain[name])
                chain[name] = i
        for name, lo, hi, wr, ps, lane in acc:
            old = seen.get(name, [])
            if wr:
                old = [e for e in old if not (lo <= e[1] and e[2] <= hi and lane in (None, e[4]) and (not ps or e[0] in d or ops[e[0]]["q"] == o["q"]))]
            seen[name] = old + [(i, lo, hi, wr, lane)]
        d.discard(i)
        s.discard(i)
        deps.append(d)
        soft.append(s - d)
    return deps, soft


def arrange(ops, deps, soft):
    n, lat = len(ops), CFG["lat"]
    kids, parents = [[] for _ in range(n)], [sorted(deps[i] | soft[i]) for i in range(n)]
    for q in "va":
        mine = [i for i in range(n) if ops[i]["q"] == q and ops[i]["now"]]
        for j, i in zip(mine, mine[1:]):
            if j not in parents[i]:
                parents[i].append(j)
    for i in range(n):
        for j in parents[i]:
            kids[j].append(i)
    queue = [o["q"] or "" for o in ops]

    def lay(rank, back):
        before, after = (kids, parents) if back else (parents, kids)
        left = [len(x) for x in before]
        free, order, can, end = {}, [], [0.0] * n, [0.0] * n
        ready = {q: [] for q in set(queue)}
        for i in range(n):
            if not left[i]:
                ready[queue[i]].append(i)
        while len(order) < n:
            t, q = min((max(min(can[i] for i in r), free.get(x, 0.0)), x) for x, r in ready.items() if r)
            i = min([k for k in ready[q] if can[k] <= t + 0.2], key=lambda k: (rank[k], k))
            if can[i] > t + 0.02:
                short = [k for k in ready[q] if max(t, can[k]) + ops[k]["c"] <= can[i] + 0.05]
                i = min(short, key=lambda k: (rank[k], k)) if short else i
            ready[q].remove(i)
            order.append(i)
            o = ops[i]
            t = max(can[i], free.get(q, 0.0)) + o["c"]
            if q:
                free[q] = t
            if not back:
                t += o["l"]
                if o["d"]:
                    t = max(t, free.get("e", 0.0)) + o["d"]
                    free["e"] = t
            end[i] = t
            for k in after[i]:
                if (k in deps[i]) if back else (i in deps[k]):
                    can[k] = max(can[k], t + lat + (ops[k]["l"] * 1.5 + ops[k]["d"] if back else 0.0))
                left[k] -= 1
                if not left[k]:
                    ready[queue[k]].append(k)
        return order, end

    end = lay([o["p"] for o in ops], False)[1]
    order = lay([-e for e in lay([-e for e in end], True)[1]], False)[0]
    return polish(ops, deps, soft, order)


def polish(ops, deps, soft, order):
    dep, above = [], []
    for i in range(len(ops)):
        far = 0
        for j in deps[i]:
            far |= above[j]
        dep.append([j for j in sorted(deps[i]) if not far >> j & 1])
        above.append(far | sum(1 << j for j in deps[i]))
    ways = CFG["ways"]
    ended = [{} for _ in ways]
    state = [[0.0] * 9 for _ in ways]
    began = [0.0] * len(ways)
    seed = [0]

    def draw():
        seed[0] = (seed[0] * 1103515245 + 12345) % 2 ** 31
        return (seed[0] >> 6) / 2.0 ** 25

    def stretch(win, k, model):
        n, final = len(win), k == FR
        loc = {g: x for x, g in enumerate(win)}
        took = [QUEUES.index(ops[g]["q"]) if ops[g]["q"] else 7 for g in win]
        free = [x for x, g in enumerate(win) if ops[g].get("free")]
        par = [sorted(loc[j] for j in deps[g] | soft[g] if j in loc) for g in win]
        kid = [[] for _ in win]
        for x, p in enumerate(par):
            for j in p:
                kid[j].append(x)
        dl = [[loc[j] for j in dep[g] if j in loc] for g in win]
        sets = []
        for (wake, dma, pe, cy, ga, link), end in zip(ways, ended):
            rate = {"p": pe, "g": 1.0, "s": 1.0, "L": link, "M": link}
            sets.append((wake, CFG["across"] * wake, [max([end[j] + CFG["across"] * wake for j in dep[g] if j not in loc] + [0.0]) for g in win],
                         [ops[g]["c"] * rate.get(ops[g]["q"], cy) + ops[g]["g"] * cy * (ga - 1.0) for g in win],
                         [ops[g]["l"] * dma for g in win], [ops[g]["d"] * dma for g in win], cy))
        snaps = [[s[:]] + [None] * n for s in state]

        def run(seq, a, ends, keep):
            total, out = 0.0, []
            for x, (wake, across, rel, c, l, d, cy) in enumerate(sets):
                end, sn = ends[x][:], snaps[x]
                at = sn[a][:]
                for p in range(a, n):
                    i = seq[p]
                    if keep:
                        sn[p] = at[:]
                    q = took[i]
                    t = at[q]
                    if rel[i] > t:
                        t = rel[i]
                    for j in dl[i]:
                        y = end[j] if took[j] == q else end[j] + across
                        if y > t:
                            t = y
                    t += c[i]
                    if q != 7:
                        at[q] = t
                    if l[i]:
                        t += l[i]
                        if d[i]:
                            if at[8] > t:
                                t = at[8]
                            t += d[i]
                            at[8] = t
                    end[i] = t + wake
                if keep:
                    sn[n] = at
                total += ((max(end) if final else end[n - 1]) - began[x] + CFG["soon"] * (sum(end) / n - began[x])) / cy
                out.append(end)
            return total / len(sets), out

        def longest(x):
            wake, across, rel, c, l, d, cy = sets[x]
            end, path = ends[x], []
            i = max(range(n), key=lambda z: end[z]) if final else n - 1
            while i >= 0:
                p, q, b, t = pos[i], took[i], -1, rel[i]
                for j in dl[i]:
                    y = end[j] if took[j] == q else end[j] + across
                    if y > t:
                        t, b = y, j
                sn = snaps[x][p]
                line = q != 7 and sn[q] > t
                move = d[i] and sn[8] > max(t, sn[q]) + c[i] + l[i]
                if line or move:
                    z = p - 1
                    while z >= 0 and not (d[seq[z]] if move else took[seq[z]] == q):
                        z -= 1
                    b = seq[z] if z >= 0 else -1
                    if b >= 0:
                        path.append((b, i))
                i = b
            return path

        name = [(ops[g]["key"][0] - k,) + ops[g]["key"][1:] for g in win]
        seq, ends = list(range(n)), [[0.0] * n for _ in ways]
        now = run(seq, 0, ends, False)[0]
        if model:
            rank, r, mine = [], -1.0, took[:]
            for x in range(n):
                r = model[name[x]][0] if name[x] in model else r + 0.001
                rank.append(r)
            for x in free:
                took[x] = model[name[x]][1] if name[x] in model else took[x]
            left, like = [len(p) for p in par], []
            ready = [x for x in range(n) if not left[x]]
            while ready:
                i = min(ready, key=lambda z: rank[z] if z < n - 1 or final else n)
                ready.remove(i)
                like.append(i)
                for z in kid[i]:
                    left[z] -= 1
                    if not left[z]:
                        ready.append(z)
            if run(like, 0, ends, False)[0] < now:
                seq = like
            else:
                took[:] = mine
        now, ends = run(seq, 0, ends, True)
        best, pos, paths = (now, seq, took[:]), [0] * n, {}
        for p, i in enumerate(seq):
            pos[i] = p
        seed[0], tries = CFG["seed"][k], CFG["tries"][k]
        for step in range(tries):
            u, flip = draw(), []
            if u < 0.06 and free:
                flip = [free[int(draw() * len(free))]]
                z = free[int(draw() * len(free))]
                if u < 0.03 and took[z] != took[flip[0]]:
                    flip.append(z)
                for z in flip:
                    took[z] = 1 - took[z]
                new, a = seq, min(pos[z] for z in flip)
            elif u < 0.7:
                x = int(draw() * len(ways))
                if x not in paths:
                    paths[x] = longest(x)
                if not paths[x]:
                    continue
                j, i = paths[x][int(draw() * len(paths[x]))]
                if draw() < 0.25:
                    z = pos[j] - 1
                    while z >= 0 and took[seq[z]] != took[j]:
                        z -= 1
                    j = seq[z] if z >= 0 else j
                a, b, ahead = pos[j], pos[i] + 1, draw() < 0.5
                need = {i if ahead else j}
                todo = list(need)
                while todo:
                    for z in (par if ahead else kid)[todo.pop()]:
                        if a <= pos[z] < b and z not in need:
                            need.add(z)
                            todo.append(z)
                if (i in need and j in need) or (n - 1 in need and ahead and not final):
                    continue
                one, two = [z for z in seq[a:b] if z in need], [z for z in seq[a:b] if z not in need]
                new = seq[:a] + (one + two if ahead else two + one) + seq[b:]
                if new[-1] != n - 1 and not final:
                    continue
            else:
                i = int(draw() * (n if final else n - 1))
                p, q, d = pos[i], took[i], sets[0][5]
                lo = max([pos[j] for j in par[i]] + [-1]) + 1
                hi = min([pos[j] for j in kid[i]] + [n if final else n - 1]) - 1
                mates = sorted((abs(z - p), z) for z in range(max(lo, p - 25), min(hi, p + 25) + 1) if z != p and (took[seq[z]] == q or (d[i] and d[seq[z]])))
                z = mates[min(len(mates) - 1, int(-math.log(1.0 - draw()) / 0.6))][1] if mates else lo if u < 0.85 else hi
                if z == p:
                    continue
                new = seq[:p] + seq[p + 1:]
                new.insert(z, i)
                a = min(p, z)
            got = run(new, a, ends, False)[0]
            if got <= now or draw() < math.exp((now - got) / (CFG["heat"][k] * (1.0 - step / tries) ** 2 + 0.003)):
                now, seq, paths = got, new, {}
                ends = run(seq, a, ends, True)[1]
                for p in range(a, n):
                    pos[seq[p]] = p
                if now < best[0]:
                    best = (now, seq, took[:])
            else:
                for z in flip:
                    took[z] = 1 - took[z]
        now, seq, took[:] = best
        ends, was = run(seq, 0, ends, True)[1], began[:]
        for x in range(len(ways)):
            ended[x].update(zip(win, ends[x]))
            state[x], began[x] = snaps[x][n], ends[x][n - 1]
        for x in free:
            ops[win[x]]["q"] = QUEUES[took[x]]
        DONE["stretch %d" % k] = sum(((max(e) if final else e[n - 1]) - b) / w[3] for e, b, w in zip(ends, was, ways)) / len(ways)
        return [win[i] for i in seq], {name[i]: (float(p), took[i]) for p, i in enumerate(seq)}

    cuts = [0] + [p + 1 for p, i in enumerate(order) if ops[i]["now"] == "gate"] + [len(order)]
    done, model = [], None
    for k in range(FR + 1):
        part, found = stretch(order[cuts[k]:cuts[k + 1]], k, model)
        done, model = done + part, found if k else None
    return done


def emit(g, T, ops, deps, order):
    queue = {"v": g.vector, "a": g.scalar, "p": g.tensor, "g": g, "s": g.sync}
    place = {j: k for k, j in enumerate(order)}
    need, done, knew, plan = set(), {}, {}, {}
    for i in order:
        o = ops[i]
        last = {}
        for j in deps[i]:
            key = ops[j]["sem"] or ops[j]["q"]
            if key not in last or place[last[key]] < place[j]:
                last[key] = j
        plan[i] = []
        mine = done.setdefault(o["q"], {})
        for key, j in sorted(last.items(), key=lambda x: -place[x[1]]):
            if o["q"] in queue and mine.get(key, -1) < place[j]:
                for k, v in list(knew[j].items()) + [(key, place[j])]:
                    mine[k] = max(mine.get(k, -1), v)
                plan[i].append(j)
                need.add(j)
        knew[i] = dict(mine) if o["q"] in queue else {}
    total, mark = {}, {}
    for i in order:
        o = ops[i]
        q = queue.get(o["q"])
        for j in plan[i]:
            s = ops[j]["sem"]
            q.wait_ge(T.sem[s or COUNTER[ops[j]["q"]]], total[s] if s else mark[j])
        if o["sem"]:
            if q is not None:
                o["f"](q)
            total[o["sem"]] = total.get(o["sem"], 0) + o["n"]
        elif i in need:
            s = COUNTER[o["q"]]
            o["f"](q).then_inc(T.sem[s], 1)
            total[s] = total.get(s, 0) + 1
            mark[i] = total[s]
        else:
            o["f"](q)
    for s in sorted(total):
        g.wait_ge(T.sem[s], total[s])


def helpers(core, nxt, T, topo):
    others = [c for c in topo.cores_of(core) if T.rank_of(c) is None]
    near = [c for c in others if topo.die(c) == topo.die(core)]
    far = [c for c in others if topo.die(c) != topo.die(core)]
    out = [[c for c in far if topo.may_write(c, nxt)][0], [c for c in near if topo.may_write(c, nxt)][0]]
    return out + [c for c in near if c not in out][:1]


def senders(t, core, nxt, T, topo):
    ports = helpers(core, nxt, T, topo)
    near = core if topo.may_write(core, nxt) else ports[1]
    return [near if t in CFG["own"] else ports[0], near, near]


def rank_program(g, core, T, topo):
    n_ranks = len(T.cores)
    for rank, rc in enumerate(T.cores):
        if core == rc or core in helpers(rc, T.cores[(rank + 1) % n_ranks], T, topo):
            ops = build(rc, T, topo)
            deps, soft = hazards(ops)
            if "order" not in DONE:
                DONE["order"] = (arrange(ops, deps, soft), [o["q"] for o in ops])
            order, took = DONE["order"]
            for o, q in zip(ops, took):
                o["q"] = q
            if core == rc:
                emit(g, T, ops, deps, order)
            else:
                hand_on(g, core, rc, T.cores[(rank + 1) % n_ranks], [ops[i]["fold"] for i in order if ops[i]["fold"]], T, topo)


def hand_on(g, core, rc, nxt, jobs, T, topo):
    got, sent = {}, 0
    for who, n, came, (buf, a, b), to, sem in jobs:
        if who == core:
            rid, pid, _ = topo.addr(to)
            got[came] = got.get(came, 0) + n
            g.wait_ge(T.sem[came], got[came])
            engines = spare(core, rc, nxt, topo) if to == rc else topo.engines(core, to)
            g.remote_dma(T[buf][:, a:b], T[buf][:, a:b], T.sem[sem], T.sem.hs, pid, rid, sum(1 << e for e in engines))
            sent += len(engines)
    if sent:
        g.wait_ge(T.sem.hs, sent)


def spare(core, rc, nxt, topo):
    off = topo.engines(core, nxt) if topo.may_write(core, nxt) else []
    return [e for e in topo.engines(core, rc) if e not in off]


def build(core, T, topo):
    n_ranks = len(T.cores)
    rank = T.rank_of(core)
    nxt = T.cores[(rank + 1) % n_ranks]
    prv = T.cores[(rank - 1) % n_ranks]
    cy, GA = CFG["cy"], CFG["ga"]
    ops, lag, firsts, tag = [], [0], set(), [-9, "", 0]

    def op(q, f, r, w, c, sem=None, n=0, l=0.0, d=0.0, after=(), fold=None, g=0.0):
        ops.append({"q": q, "f": f, "r": r, "w": w, "c": c, "sem": sem, "n": n, "l": l, "d": d, "after": after, "fold": fold,
                    "now": False, "p": len(ops) + lag[0], "g": g, "key": (tag[0], tag[1], len(ops) - tag[2])})
        return len(ops) - 1

    def join(k):
        parts = ops[-k:]
        del ops[-k:]
        op("p", lambda e: [x["f"](e) for x in parts][-1], [r for x in parts for r in x["r"]], parts[-1]["w"], sum(x["c"] for x in parts))

    def once(who):
        new = who not in firsts
        firsts.add(who)
        return CFG["once"] if new else 0.0

    def ap(x):
        return T[x[0]][:, x[1]:x[2]:x[3]] if len(x) > 3 else T[x[0]][:, x[1]:x[2]]

    def size(x):
        return len(range(*x[1:]))

    def rev(x):
        return T[x[0]][:, slice(x[2] - 1, x[1] - 1 if x[1] else None, -1)]

    def ind(win, off):
        return ap(win).indirect(ap(off))

    def cost(out, k=1.0):
        return (0.05 if k == GA else CFG["fv"]) + max(64, size(out) * k) * cy

    def dma(q, out, in_, r, w, sem, kb):
        op(q, lambda e: e.dma_start(out, in_).then_inc(T.sem[sem], 16), r, w, 0.08, sem, 16, 1.5, 0.2 + kb / 600)

    def adding(out, in_, r, w, sem, d):
        op("g", lambda e: e.dma_start(out, in_, accum_op=A.add).then_inc(T.sem[sem], 16), r, w, 1.0 + once("g") / 3, sem, 16, CFG["add"] - 1.0, d)

    def tt(out, a, b, alu, k=2):
        op("v", lambda e: e.tensor_tensor(ap(out), ap(a), ap(b), alu), [a, b], [out], cost(out, 1 if a[0] in PSUM or b[0] in PSUM else k))

    def ts(out, a, s1, o1, s2=None, o2=None, col=None):
        if o2 is None:
            op("v", lambda e: e.tensor_scalar(ap(out), ap(a), s1, None, o1), [a] + ([col] if col else []), [out], cost(out))
        else:
            op("v", lambda e: e.tensor_scalar(ap(out), ap(a), s1, s2, o1, o2), [a] + ([col] if col else []), [out], cost(out))

    def cp(out, a):
        op("v", lambda e: e.tensor_copy(ap(out), ap(a)), [a], [out], cost(out))

    def act(out, a, func=F.Copy, col=None, **k):
        op("a", lambda e: e.activation(ap(out), ap(a), func, **k), [a] + ([col] if col else []), [out], cost(out) + 0.015)

    def fill(out, c):
        op("v", lambda e: e.memset(ap(out), c), [], [out], cost(out))

    def tr(out, a):
        op("v", lambda e: e.transpose(ap(out), ap(a)), [a], [out], cost(out))

    def gat(q, out, win, off, func=F.Copy, **k):
        i = len(ops)

        def call(e):
            if ops[i]["q"] == "a":
                return e.activation(ap(out), ind(win, off), func, **k)
            if func == F.Sign:
                return e.tensor_scalar(ap(out), ind(win, off), 0.0, 0.5, A.is_ge, A.subtract)
            return e.tensor_copy(ap(out), ind(win, off))

        op(q.lower(), call, [win, off], [out], cost(out, GA), g=size(out) * GA * cy)
        ops[i]["free"] = q in "AV"

    def gts(out, win, off, s1, o1, s2, o2):
        op("v", lambda e: e.tensor_scalar(ap(out), ind(win, off), s1, s2, o1, o2), [win, off], [out], cost(out, GA), g=size(out) * GA * cy)

    def gtt(out, win, off, x, alu):
        op("v", lambda e: e.tensor_tensor(ap(out), ind(win, off), ap(x), alu), [win, off, x], [out], cost(out, GA), g=size(out) * GA * cy)

    def scan(out, d0, d1, init, back=False):
        o = rev(out) if back else ap(out)
        x = rev(d1) if back else ap(d1)
        col = [] if init == NONE else [init]
        s0 = ap(init) if col else init
        op("v", lambda e: e.tensor_tensor_scan(o, ap(d0), x, s0, A.add, A.min), [d0, d1] + col, [out], cost(out))

    def iota(out, pattern, base, cm, small=False):
        if small:
            op("g", lambda e: e.iota(ap(out), pattern, base, cm, allow_small_or_imprecise_dtypes=True), [], [out], 0.15 + cost(out, 2))
        else:
            op("g", lambda e: e.iota(ap(out), pattern, base, cm), [], [out], 0.15 + cost(out, 2))

    def pick(out, a, pattern, alu, base, cm, c=0.0):
        op("g", lambda e: e.affine_select(ap(out), ap(a), pattern, alu, c, base, cm), [a], [out], 0.17 + size(a) * 2 * cy)

    def mm(out, lhs, x, start, stop, k=1):
        op("p", lambda e: e.matmul(ap(out), ap(lhs), ap(x), start, stop), [x[:3], lhs], [out], 0.015 + max(64, size(out)) * k * cy * 0.53)

    def mat(name, s):
        return ((name + "b", 0, 128), 1) if s == "s0" else ((name + "f", 0, 128), 4)

    LA, LB, LP = ("lst", 0, 16), ("lst", 16, 32), ("lst", 32, 48)

    def turn(kp, tw, k):
        if k:
            tr((tw, 256, 544), (kp, 0, 288))
        else:
            tr((tw, 0, 256), (kp, 16, 272))

    cuts0 = CFG["cuts0"]
    n0 = len(cuts0) - 1
    for k in range(n0):
        a, b = cuts0[k], cuts0[k + 1]
        dma("s", T.s0[:, PB + a:PB + b], T.sp[:, a:b], [], [("s0", PB + a, PB + b)], "ld%d" % k, (b - a) / 4)
    dma("s", T.iti[:, 0:256], T.itg[:, 0:256], [], [("iti", 0, 256)], "ldi0", 128)
    dma("s", T.roti[:], T.rot[:], [], [("roti", 0, 256)], "ldr", 128)
    for k in range(1, len(ops)):
        ops[k]["follows"] = [k - 1]
    dma("s", T.iti[:, 256:1024], T.itg[:, 256:1024], [("s0", PB, PB + W)], [("iti", 256, 1024)], "ldi1", 384)
    op("s", lambda e: [e.dma_start(T.hopi[c::16, :], T.hop[:]).then_inc(T.sem.ldh, 16) for c in range(16)],
       [("iti", 0, 256)], [("hopi", 0, 4)], 1.0, "ldh", 256, 1.5, 0.5)

    fill(("nil", 0, 128), 0.0)
    fill(("s0", 0, PB), 0.0)
    fill(("s0", PB + W, 2 * PB + W), 0.0)

    def diag(out, c):
        pick(out, ("nil", 0, 128), [[-1, 128]], A.not_equal, 0, 1, c)

    def const(out, c):
        pick(out, ("nil", 0, size(out)), [[0, size(out)]], A.not_equal, 0, 0, c)

    diag(("idb", 0, 128), 1.0)
    act(("upb", 0, 128), ("idb", 0, 128), scale=4096.0)
    act(("hfb", 0, 128), ("idb", 0, 128), scale=-2048.0)
    lag[0] = 400
    fill(("one", 0, 8), 1.0)
    fill(("one", 8, 16), -BIG)
    fill(("ea", 0, 144), 0.0)
    fill(("er", 0, 272), 0.0)
    fill(("cb", 0, 256), -3 * BIG)
    iota(("c1", 0, 48), [[0, 48]], 0, 1)
    iota(("c2", 0, 16), [[0, 16]], 0, 1)
    iota(("c2", 16, 32), [[1, 16]], 0, 0)
    iota(("c3", 0, 16), [[1, 16]], 0, 0)
    iota(("c3", 16, 32), [[16, 16]], 0, 0)
    const(("kp2", 0, 16), 0.0)
    const(("kp2", 272, 288), 0.0)
    diag(("idf", 0, 128), 1.0)
    diag(("ngf", 0, 128), -1.0)
    iota(("rmp", 256, 512), [[8192, 256]], 0, 0, True)
    lag[0] = 450
    pick(("e8", 16, 24), ("one", 8, 16), [[-16, 8]], A.is_ge, 0, 1)
    pick(("ea", 15, 143, 16), ("e8", 16, 24), [[16, 8]], A.is_ge, 15, -1)
    const(("vt", 0, 1), 1.0)
    pick(("e8", 0, 8), ("one", 0, 8), [[-16, 8]], A.is_equal, 0, 1)
    pick(("e8", 8, 16), ("one", 0, 8), [[-16, 8]], A.is_equal, -15, 1)
    iota(("kl", 1, 256), [[0, 255]], 8192, 0, True)
    iota(("kr", 1, 256), [[0, 255]], 8192, 0, True)
    const(("st", 0, 32), 0.0)
    const(("yy", 0, 64), NONE)
    const(("st", 16, 17), BIG)
    act(("ev", 0, 144), ("ea", 0, 144), scale=2.0)
    lag[0] = 600
    for kp in ("kp", "kp3"):
        const((kp, 0, 16), 0.0)
        const((kp, 272, 288), 0.0)
    iota(("mc", 0, 256), [[16, 256]], -6143, 0, True)
    const(("cm", 0, QX), W * RND)
    diag(("dnb", 0, 128), -4096.0)
    diag(("idf", 128, 256), 1.0)
    for name, c in (("dnf", -4096.0), ("upf", 4096.0)):
        diag((name, 0, 128), c)
        diag((name, 128, 256), c)
    for s in ("sa", "sb"):
        const((s, 0, PF), 0.0)
        const((s, PF + W, 2 * PF + W), 0.0)
    lag[0] = 400
    ts(("c4", 0, 32), ("c1", 0, 32), 4, A.arith_shift_right)
    ts(("c1", 0, 32), ("c1", 0, 32), 15, A.bitwise_and)
    tt(("c2", 0, 32), ("c2", 0, 32), ("c4", 0, 32), A.add)
    tt(("c3", 16, 32), ("c3", 16, 32), ("c1", 16, 32), A.add)
    ts(("c4", 32, 48), ("c1", 0, 16), 16.0, A.mult)
    ts(("c2", 0, 32), ("c2", 0, 32), 1, A.bitwise_and)
    tt(("c3", 0, 16), ("c3", 0, 16), ("c4", 32, 48), A.add)
    ts(("c2", 0, 32), ("c2", 0, 32), 272.0, A.mult)
    cp(LP, ("c3", 0, 16))
    cp(("lst", 48, 64), ("c3", 16, 32))
    cp(("col", 0, 1), ("c1", 0, 1))
    tt(("c2", 0, 32), ("c2", 0, 32), ("c3", 0, 32), A.add)
    cp(("lst", 0, 32), ("c2", 0, 32))
    for c, scale, bias in ((1, 2.0 ** 18, 512 - 2.0 ** 22), (2, -2.0 ** 18, -1024.0 * 255), (3, 2.0 ** 21, 0.0)):
        ts(("col", c, c + 1), ("col", 0, 1), scale, A.mult, bias, A.add)
    act(("rmp", 256, 512), ("rmp", 256, 512), F.Identity, ("col", 3, 4), bias=T.col[:, 3:4])
    act(("rmp", 0, 256), ("rmp", 256, 512), F.Identity, scale=-1.0, bias=2.0 ** 25 - 4096)
    lag[0] = 600
    act(("mc", 0, 256), ("mc", 0, 256), F.Identity, ("col", 0, 1), bias=T.col[:, 0:1])
    tt(("er", 15, 143, 16), ("e8", 0, 8), ("e8", 8, 16), A.add)
    act(("er", 143, 271, 16), ("er", 15, 143, 16))
    for k, a, c in (("kl", 0, 1), ("kr", 8, 2)):
        act(("e8", 24, 32), ("e8", a, a + 8), F.Identity, ("col", c, c + 1), scale=BIG, bias=T.col[:, c:c + 1], accum_out=T[k][:, 0:1])
        ops[-1]["w"].append((k, 0, 1))
    op("v", lambda e: e.tensor_scalar(T.hopf[:], T.hopi[:], -1.0 / W, None, A.mult), [("hopi", 0, 4)], [("hopf", 0, 4)], 0.12)

    def targets(t, k):
        if k == 1:
            cp(("it16", 256 * t, 256 * t + 256), ("iti", 256 * t, 256 * t + 256))
        elif k == 2:
            gat("a", ("kp2", 16, 272), ("iti", 256 * t, 256 * t + 256), LP)
        elif k < 5:
            turn("kp2", "tw2", k - 3)
        elif k == 5:
            gat("a", ("el", 0, 256), ("tw2", 0, 544), LB, F.Identity, scale=-1.0, bias=4095 - 2.0 ** 24)
            act(("el", 256, 512), ("el", 0, 256), F.Identity, bias=4096.0)
        elif k == 6:
            dma("s", T.nk[:], T.rmp[:], [("rmp", 0, 512)], [("nk", 0, 512)], "nkc", 256)
        else:
            adding(T.nk[:], T.el[:], [("el", 0, 512)], [("nk", 0, 512)], "nka", 0.3 + 512 / 600)

    def rows(rw):
        buf, a, b = rw
        dma("s", T[buf][0::16, a:b], T.hl[:, 0:256], [("hl", 0, 256)], [(buf, a, b, 2)], "rwd", 100)
        dma("s", T[buf][15::16, a:b], T.hl[:, 256:512], [("hl", 256, 512)], [(buf, a + 1, b, 2)], "rwd", 100)

    turnno, sent, added, landed = [0, 0], [], [], []

    def judge(s, pad, v0, v1, terms, whole):
        most = 512 if whole else CFG["jc"]
        parts = (v1 - v0 + most - 1) // most
        for h in range(parts):
            a, b = max(1, v0 + (v1 - v0) * h // parts), v0 + (v1 - v0) * (h + 1) // parts
            banks = CFG["banks0" if s == "s0" else "banks"]
            ps, o = banks[turnno[1] % len(banks)]
            turnno[1] += 1
            p = (ps, o, o + b - a)
            for j, (name, buf, at) in enumerate([("up", s, -pad)] + terms):
                lhs, k = mat(name, s)
                mm(p, lhs, (buf, a - at, b - at), j == 0, j == len(terms), k)
            if whole:
                join(len(terms) + 1)
            act(("vt", a, b), p)

    def piece(s, pad, v0, v1, by):
        k, j = turnno[0] % 2, turnno[0] % 4
        turnno[0] += 1
        p, h, n = "pe%d" % k, (v1 - v0) // 2, v1 - v0
        u = "h%d" % k if s == "s0" else "b%d" % j
        kind = by.upper()
        lhs, c = mat("ng" if kind == "N" else "id", s)
        lo, hi = pad + v0, pad + v1
        m, b = "pm" if kind == "V" else u, "a%d" % k
        a = ("pm", 512 * k, 512 * k + h) if kind != "V" else ("pm", 1024 - h, 1024) if n + h <= 1024 else (p, 2, h + 2)

        def even():
            if kind in "GH":
                who = helpers(core, nxt, T, topo)[CFG["fw"]]
                rid, pid, _ = topo.addr(who)
                out, back = len(topo.engines(core, who)), len(spare(who, core, nxt, topo))
                x = RemoteDMATransfer(dst_ids=[DstId(rid=rid, pnc=pid)], dma_engine_mask=topo.mask(core, who), remote_sem=T.sem.fa,
                                      srcs=[T[s][:, lo + z:hi + z] for z in (-2, -1, 1, 2)], dsts=[T[u][:, 0:n]], alu_op=2)
                i = op("g", lambda e: e.remote_dma_fused([x], local_sem=T.sem.fl), [(s, lo - 2, hi + 2)], [(u, 0, n)],
                       1.0, "fl", out, 1.0, 2 * n / 550, fold=(who, out, "fa", (u, 0, n), core, "fb"))
                op(None, None, [], [(u, 0, n)], 0.0, "fb", back, CFG["back"] + n / 1000 + once(who), after=(i,))
            elif kind == "B":
                return
            elif by.islower():
                act((p, 0, h + 2), (s, lo - 2, hi + 2, 2), scale=-1.0 if kind == "N" else 1.0)
            else:
                mm((p, 0, h + 2), lhs, (s, lo - 2, hi + 2, 2), True, True, c)

        def minus():
            if kind == "N":
                act((u, 0, h + 2), (s, lo - 1, hi + 2, 2), scale=-1.0)

        def folded():
            if kind in "HZ":
                act(("vt", v0, v1), (u, 0, n), scale=-1.0)
                add()
            elif kind == "G":
                judge(s, pad, v0, v1, [("dn", u, v0)], True)

        def add():
            adding(T.vt[:, v0:v1], T[s][:, lo:hi], [(s, lo, hi)], [("vt", v0, v1)], "zd%d" % j, 0.3 + n / 600)

        def maxima():
            if kind == "X":
                tt((p, 0, h + 2), (p, 0, h + 2), (s, lo - 1, hi + 2, 2), A.max)
            elif kind == "B":
                tt(("rg", X * k, X * k + h + 2), (s, lo - 2, hi + 2, 2), (s, lo - 1, hi + 2, 2), A.max, CFG["bb"])
            elif kind == "N":
                tt((b, 0, h + 1), (p, 0, h + 1), (u, 1, h + 2), A.min)
                tt(a, (p, 2, h + 2), (u, 0, h), A.min)
            elif kind not in "GH":
                tt((b, 0, h + 1), (p, 0, h + 1), (s, lo + 1, hi + 2, 2), A.max)
                tt(a, (p, 2, h + 2), (s, lo - 1, hi - 1, 2), A.max)

        def more():
            if kind == "X":
                tt((u, 0, n + 2, 2), (p, 0, h + 1), (s, lo, hi + 1, 2), A.max)
                tt((u, 1, n + 2, 2), (p, 1, h + 2), (s, lo - 1, hi, 2), A.max)
            elif kind == "B":
                tt((u, 0, n + 2, 2), ("rg", X * k, X * k + h + 1), (s, lo, hi + 1, 2), A.max, CFG["bb"])
                tt((u, 1, n + 2, 2), ("rg", X * k + 1, X * k + h + 2), (s, lo - 1, hi, 2), A.max, CFG["bb"])
            elif kind == "N":
                tt(("vt", v0, v1, 2), a, (b, 0, h), A.min)
                tt(("vt", v0 + 1, v1, 2), a, (b, 1, h + 1), A.min)
            elif kind not in "GH":
                tt((m, 0, n, 2), a, (b, 0, h), A.max)
                tt((m, 1, n, 2), a, (b, 1, h + 1), A.max)

        def finish():
            if kind in "XB":
                judge(s, pad, v0, v1, [("hf", u, v0), ("hf", u, v0 - 2)], True)
            elif kind == "V":
                z = 1 if v0 == 0 else 0
                tt(("vt", v0 + z, v1), (s, lo + z, hi), (m, z, n), A.subtract)
            elif kind == "N":
                add()
            elif kind == "W":
                judge(s, pad, v0, v1, [("dn", u, v0)], False)

        return {"e": even, "n": minus, "m": maxima, "M": more, "f": finish, "N": folded}

    vc = [0] + [c - 4 for c in cuts0[1:n0]] + [W]
    lag[0] = 0
    kept_from = len(ops)
    turnno[0] = n0 % 2
    parts = [piece("s0", PB, vc[k], vc[k + 1], CFG["route0"][k]) for k in range(n0)]
    for step in CFG["start"].split():
        tag[:] = [-1, step, len(ops)]
        if step[0] == "t":
            targets(0, int(step[1:]))
        else:
            parts[int(step[1:])][step[0]]()
    lag[0] = 1000

    def records(k, after):
        dma("s", T.cw[:, k * W:k * W + W], T.rec[:], [after], [("cw", k * W, k * W + W)], "ldc%d" % k, 1024)

    tag[:] = [-1, "c", len(ops)]
    for k in range(CFG["rc"]):
        records(k, ("iti", 256, 1024))

    def frame(t):
        last = t == FR - 1
        old, opad = ("s0", PB) if t == 0 else (("sa", "sb")[(t - 1) % 2], PF)
        new = ("sa", "sb")[t % 2]
        lq = "lq%d" % t
        xt, lt = ("xo", lq) if t else ("xb", "lb")
        got = (lq, X, XW) if t else (lq, 0, QX)
        win = (old, opad, opad + W)
        rw = ("s0", PB, PB + W) if t else ("gv", 0, W)
        up = float(W * (t // 2 + 1))
        recs = ("cw", 0, (t // 2 * 2 + 3) * W)
        kept, held = [], {}

        r0 = 16 * t
        at = (128 - r0) % 128
        xs = CFG["xs"]

        def copies():
            if t:
                dma("s", T.sr[r0:128, :], T[old][0:128 - r0, PF:PF + W], [win, ("vt", X, W)], [("sr", 0, W, 2)], "trn", 1800)
                dma("s", T.sr[0:r0, :], T[old][128 - r0:128, PF:PF + W], [win, ("vt", X, W)], [("sr", 1, W, 2)], "trn", 300)

        def hops():
            act(("hd", 0, 128), ("upf", 0, 128), F.Identity, ("hopf", 0, 4), scale=T.hopf[:, t:t + 1])
            if t:
                act(("hdt", 0, 128), ("upf", at, at + 128), F.Identity, ("hopf", 0, 4), scale=T.hopf[:, t:t + 1])

        def r_rows(k):
            if k == 5:
                rows(rw)
            elif k < 4:
                if t:
                    turn("kp3", "tw3", k - 2)
            else:
                gat("a", ("qb", 0, 256), *((("tw3", 0, 544), LB) if t else (("roti", 0, 256), ("lst", 48, 64))))
                act(("hl", 0, 256), ("qb", 0, 256))
                mm(("pr", 0, 256), ("upf", 0, 128), ("qb", 0, 256), True, False, 4)
                mm(("pr", 0, 256), ("dnb", 0, 128), ("hl", 0, 256), False, True)
                act(("hl", 256, 512), ("pr", 0, 256), scale=1.0 / W)

        def moved(q, k):
            b0, b1, i = xs[k], xs[k + 1], len(ops)
            gat(q, ("gv", 256 * b0, 256 * b1), ("vt", 0, W), ("it16", 256 * t + 16 * b0, 256 * t + 16 * b1), F.Sign, bias=2.0 ** -32)
            for b in range(b0, b1):
                op("p", lambda e, b=b: e.matmul(T.pc[:, 0:256], T["e" + ops[i]["q"]][:, 15 - b:143 - b], T.gv[:, 256 * b:256 * b + 256], False, b == 15),
                   [("gv", 256 * b, 256 * b + 256), ("ea", 0, 144), ("ev", 0, 144)], [("pc", 0, 256)], 0.015 + 136 * cy)
            join(b1 - b0)

        def latest(out, key, way):
            op("v", lambda e: e.tensor_tensor_scan(way(out), way(("pc", 0, 256)), way(key), NONE, A.min, A.max), [("pc", 0, 256), key], [out], cost(out))

        def decode():
            halves = [(a, a + CFG["dc"]) for a in range(0, 256, CFG["dc"])]
            for a, b in halves:
                tt(("ki", a, b), ("fg", a, b), ("pc", 256 + a, 256 + b), A.min)
            for a, b in halves:
                ts(("pay", a, b), ("ki", a, b), 8191, A.bitwise_and)
            for a, b in halves:
                ts(("pc", a, b), ("pay", a, b), 4096.0, A.is_lt, 0.5, A.subtract)
            ts(("dd", 0, 256), ("ki", 0, 256), 12, A.arith_shift_right, -2, A.bitwise_and)
            for a, b in halves:
                tt(("pc", a, b), ("pc", a, b), ("dd", a, b), A.mult)
            for a, b in halves:
                tt(("kp", 16 + a, 16 + b), ("pc", a, b), ("pay", a, b), A.subtract)
            tr(("tw", 0, 128), ("kp", 16, 144))
            tr(("tw", 256, 544), ("kp", 0, 288))
            tr(("tw", 128, 256), ("kp", 144, 272))

        front = {
            "C": copies, "h": hops,
            "z": lambda: mm(("pc", 0, 256), ("idb", 0, 128), ("cb", 0, 256), True, False),
            "d": lambda: tt(("dl", 0, 256), ("pc", 0, 256), ("el", 0, 256), A.max),
            "e": lambda: tt(("dr", 0, 256), ("pc", 0, 256), ("el", 256, 512), A.max),
            "L": lambda: latest(("fg", 0, 256), ("nk", 0, 256), ap), "R": lambda: latest(("fg", 256, 512), ("nk", 256, 512), rev),
            "x": lambda: tr(("xe", 0, 32), ("fg", 240, 272)),
            "y": lambda: (scan(("yy", 1, 32), ("st", 0, 31), ("xe", 0, 31), NONE), scan(("yy", 32, 63), ("st", 0, 31), ("xe", 1, 32), NONE, True)),
            "w": lambda: tr(("zz", 0, 64), ("yy", 0, 64)),
            "F": lambda: scan(("fg", 0, 256), ("kl", 0, 256), ("dl", 0, 256), ("zz", 15, 16)),
            "B": lambda: scan(("pc", 256, 512), ("kr", 0, 256), ("dr", 0, 256), ("zz", 48, 49), True), "D": decode}
        for step in CFG["front"].split():
            q, step = step.split(":") if ":" in step else (None, step)
            tag[:] = [t, "front " + step, len(ops)]
            if step[0] == "g":
                moved(q, int(step[1:]))
            elif step[0] == "r":
                r_rows(int(step[1:]))
            elif step[0] == "t":
                if not last and (t == 0 or step[1] not in CFG["ahead"]):
                    targets(t + 1, int(step[1:]))
            else:
                if step == "L":
                    gates.append(len(ops))
                front[step]()

        def source(a, b):
            gts(("src", a, b), ("tw", 0, 544), ("lst", a // 16, b // 16), 6143.0, A.add, 4095.0, A.min)

        def phase(a, b):
            gtt(("hw", a, b), ("tw", 0, 544), ("lst", a // 16, b // 16), ("mc", a, b), A.subtract)

        def whole(q, a, b):
            if q == "v":
                ts(("kk", a, b), ("hw", a, b), T.hopf[:, t:t + 1], A.mult, RND, A.add, ("hopf", 0, 4))
            else:
                act(("kk", a, b), ("hw", a, b), F.Identity, ("hopf", 0, 4), scale=T.hopf[:, t:t + 1], bias=RND)

        def turned_source():
            if t:
                p = ("pd", 512, 512 + QX)
                mm(p, ("idf", 0, 128), ("mc", 256 - QX, 256), True, False, 4)
                mm(p, ("idf", at, at + 128), ("hw", 256 - QX, 256), False, True, 4)
                ts(("srt", 0, QX), p, 6143.0, A.add, 4095.0, A.min)

        def rot_of(ps, m0, m1):
            a, b = m0 // 16, m1 // 16
            p = (ps, 256 + a, 256 + b)
            z = at if m0 >= W - X else 0
            e0 = 15 + z
            mm(p, ("idb", 0, 128), ("cm", 0, b - a), True, False)
            mm(p, ("dnf", z, z + 128), ("kk", a, b), False, False, 4)
            mm(p, ("hdt" if z else "hd", 0, 128), ("hw", a, b), False, False, 4)
            for r in range(16):
                mm(p, ("er", e0 - r, e0 + 128 - r), ("rg", m0 + r, m1, 16), False, r == 15)
                ops[-1]["r"][0] = ("rg", m0, m1)
            join(16)
            if m0 < W - X:
                kept.append((("qf", QX + a, QX + b), p))

        def t_gather(q, m0, m1):
            o = W - X
            if m0 < o:
                gat(q, ("tb", m0, m1), win, ("src", m0 // 16, m1 // 16))
            elif t:
                gat(q, (xt, m0 - o, m1 - o), ("sr", 0, W), ("srt", (m0 - o) // 16, (m1 - o) // 16))
            else:
                gat(q, (xt, m0 - o, m1 - o), win, ("src", m0 // 16, m1 // 16))

        def factor(n0, n1):
            return ("tb", n0 - X, n1 - X) if n0 >= X else (lt, n0, n1)

        def turn_in(n0, n1, k):
            ps, o = CFG["hb"].get((last, k)) or (("pe%d" % (k % 2), 0) if last else (("pc", "pr")[n0 == 0], 0))
            held[k] = (ps, o, o + n1 - n0)
            for a in range(0, n1 - n0, 512):
                b = min(a + 512, n1 - n0)
                mm((ps, o + a, o + b), ("idb", 0, 128), ("h%d" % (k % 2), a, b), True, True)

        def send(k):
            hx = CFG["hx"][t]
            out, land = [((xt, 0, hx), (lt, 0, hx)), ((xt, hx, X), (lt, hx, X)), (("xo", X, XW), got)][k]
            who = senders(t, core, nxt, T, topo)[k]
            to = nxt if who == core else who
            rid, pid, _ = topo.addr(to)
            sem = ("arr%d_%d" if who == core else "xa%d_%d") % (t, k)
            mask, n = topo.mask(core, to), len(topo.engines(core, to))
            i = op("g", lambda e: e.remote_dma(ap(land), ap(out), T.sem[sem], T.sem["sx%d" % k], pid, rid, mask),
                   [out], [], 1.0 + once(core), "sx%d" % k, n, 1.0, size(out) / 500,
                   fold=None if who == core else (who, n, sem, land, nxt, "arr%d_%d" % (t, k)))
            way = size(out) / CFG["link"] / (2 if land[0] == "lb" else 1)
            op("L" if who == core else "M", None, [], [land], way, "arr%d_%d" % (t, k), len(topo.engines(senders(t, prv, core, T, topo)[k], core)),
               CFG["far"] if who == core else CFG["arr"] + once(who), after=(i,))
            ops[i]["follows"] = sent[-1:]
            sent.append(i)
            if who == core:
                ops[-1]["follows"] = landed[-1:]
                landed.append(len(ops) - 1)

        def output(n0, n1, k):
            y0, y1 = n0 % 2048, n0 % 2048 + n1 - n0
            ps, x = "pd" if y0 < X else "pm", (new, PF + n0, PF + n1)
            by = CFG["yk"][k]
            if by == "s":
                dma("s", T.y[:, y0:y1], ap(x), [x], [("y", y0, y1)], "out%d" % k, (n1 - n0) / 2)
            elif by == "d":
                adding(T.y[:, y0:y1], ap(x), [x], [("y", y0, y1)], "zd%d" % (k % 4), (n1 - n0) / 600)
            else:
                for a in range(y0, y1, 512):
                    b = min(a + 512, y1)
                    p, z = (ps, a % X, a % X + b - a), (new, x[1] + a - y0, x[1] + b - y0)
                    if by == "a":
                        act(p, z)
                    elif by == "m":
                        mm(p, ("idf", 0, 128), z, True, True, 4)
                    else:
                        tt(("vt", a, b), z, p, A.add)
                if by == "v":
                    dma("s", T.y[:, y0:y1], T.vt[:, y0:y1], [("vt", y0, y1)], [("y", y0, y1)], "out%d" % k, (n1 - n0) / 2)

        yc = CFG["yc"]
        cut = CFG["cut"] // 16
        tag[:] = [t, "sources", len(ops)]
        source(cut, 256)
        phase(cut, 256)
        pieces = CFG["lp"] if last else list(zip(yc[1:], yc))
        if not last:
            vc = [W] + [c + 4 for c in CFG.get("vc", yc)[1:-1]] + [0]
            route = CFG["route"][t]
            turnno[:] = [len(route) % 2, 0]
            votes = [piece(new, PF, vc[k + 1], vc[k], by) for k, by in enumerate(route)]
        top = {"w": (W - X, W), "a": (W - X + CFG["hx"][t], W), "b": (W - X, W - X + CFG["hx"][t]), "c": (W - X // 2, W), "d": (W - X, W - X // 2)}
        for step in CFG["last" if last else "steps"].split():
            q, step = step.split(":") if ":" in step else (None, step)
            c, k = step[0], step[1:]
            tag[:] = [t, step, len(ops)]
            if c == "S":
                source(0, cut)
            elif c == "H":
                phase(0, cut)
            elif c == "K":
                whole(q, 0, cut)
            elif c == "k":
                whole(q, cut, 256)
            elif c == "U":
                turned_source()
            elif c == "C":
                (act if q == "a" else cp)(("xo", X, XW), ("pd", 512 - QX, 512))
            elif c == "R":
                m0, m1 = top[k]
                gat(q, ("rg", m0, m1), rw, ("src", m0 // 16, m1 // 16))
            elif c == "T":
                t_gather(q, *top[k])
            elif c == "Q":
                rot_of("pd", W - X, W)
            elif c == "X":
                send("baq".index(k))
            elif c == "I":
                ts(("q16", 0, QX), got, up, A.add)
            elif c == "c":
                for out, p in kept:
                    act(out, p)
            elif c == "D":
                if t < 2:
                    records(t + 3, ("xo", X, XW))
            elif c == "G":
                if t + 2 < FR and k in CFG["ahead"]:
                    targets(t + 2, int(k))
            elif c == "J":
                act(("qf", 0, QX), got)
            elif c == "Z":
                gat("a", ("kp3", 16, 272), ("qf", 0, 256), LP)
            elif c in "enmMfN":
                votes[int(k)][c]()
            else:
                k = int(k)
                n0, n1 = pieces[k]
                if c == "r":
                    gat(q, ("rg", n0 - X, n1 - X), rw, ("src", (n0 - X) // 16, (n1 - X) // 16))
                elif c == "t":
                    t_gather(q, n0 - X, n1 - X)
                elif c == "q":
                    rot_of(("pc", "pr")[k % 2], n0 - X, n1 - X)
                elif c == "o":
                    ts(("q16", n0 // 16, n1 // 16), (("pc", "pr")[k % 2], 192 + n0 // 16, 192 + n1 // 16), up, A.add)
                elif c == "p":
                    gtt((new, PF + n0, PF + n1), recs, ("q16", n0 // 16, n1 // 16), factor(n0, n1), A.mult)
                elif c == "g":
                    gat("a", ("h%d" % (k % 2), 0, n1 - n0), recs, ("q16", n0 // 16, n1 // 16))
                elif c == "u":
                    turn_in(n0, n1, k)
                elif c == "P":
                    tt((new, PF + n0, PF + n1), factor(n0, n1), held[k], A.mult)
                else:
                    output(n0, n1, k)

    gates = []
    for t in range(FR):
        frame(t)
    for o in ops[kept_from:]:
        o["now"] = "kept"
    for i in gates:
        ops[i]["now"] = "gate"
    return ops
